import numpy as np, ml_dtypes
CORES = [16,17,18,19,32,33,34,35]
N = 8
BF = ml_dtypes.bfloat16
V, L, RO, HP, S, ST = 3328, 256, 4, 1, 3, 61
def parts(rng):
    cen = rng.integers(0, 255, (1, 8, 16, 24)); k = rng.integers(0, 24, (N, 8, 1, V)); size = rng.choice(np.array([3, 12, 40, 90]), (N, 8, 1, V))
    x = np.take_along_axis(cen, k, 3) + np.floor((2 * size + 1) * rng.random((N, 8, 16, V))).astype(np.int64) - size
    x = np.minimum(np.maximum(x, 0), 254)
    hub = np.argsort(rng.random((N, 8, 1, V)), axis=3); u = rng.random((N, 8, 16, V))
    c = np.take_along_axis(hub, np.minimum((V * u * u).astype(np.int64), V - 1), 3)
    c = np.where(rng.random((N, 8, 1, V)) < 0.06, c[:, :, :1], c)
    w = rng.integers(0, V, (N, 8, 16, L)); u = rng.random((N, 8, L)); n = 2 * np.minimum((8 * u * u).astype(np.int64), 7) + 1
    t = rng.integers(0, 1600, (N, 8, L))
    return x, c, w, n, t
def trap(rng, d, T, f):
    x, c, w, n, t = d
    o = np.argsort(rng.random((N, 8, V)), axis=2); z = np.argsort(rng.random((N, 8, L)), axis=2)
    if len(f):
        for r in range(N):
            for g in range(8):
                u = o[r, g].copy(); o[r, g] = np.concatenate([np.array(f), u[~np.isin(u, np.array(f))]])
    for r in range(N):
        q = (r + S) % N; b = (r - S) % N
        for g in range(8):
            tv = o[r, g, :T]; tw = o[q, g, T:2 * T]; h = o[b, g, 2 * T:3 * T]; la = z[r, g, :T]; lb = z[b, g, T:2 * T]
            c[r, g][:, tv] = tw; c[q, g][:, tw] = tv
            w[r, g][0, la] = tv; n[r, g][la] = 1
            x[b, g][:, h] = x[r, g][:, tv]
            w[b, g][0, lb] = h; w[b, g][1, lb] = tv; n[b, g][lb] = 3; t[b, g][lb] = np.maximum(t[b, g][lb], 1)
def pack(d):
    x, c, w, n, t = d
    return {"pts": np.ascontiguousarray(x.reshape(N, 128, V)).astype(np.float32).astype(BF), "cand": np.ascontiguousarray(c.reshape(N, 128, V)).astype(np.int32),
            "way": np.ascontiguousarray(w.reshape(N, 128, L)).astype(np.int32), "cnt": np.ascontiguousarray(n).astype(np.int32), "th": np.ascontiguousarray(t).astype(np.int32)}
def setup_inputs(rng):
    d = parts(rng); trap(rng, d, 12, [])
    return pack(d)
def setup_inputs_spread(rng):
    x, c, w, n, t = parts(rng)
    x = np.minimum((np.exp2(8 * rng.random((N, 8, 1, V))) * rng.random((N, 8, 16, V))).astype(np.int64), 254)
    hub = np.argsort(rng.random((N, 8, 1, V)), axis=3)
    c = np.take_along_axis(hub, np.minimum((V * rng.random((N, 8, 16, V)) ** 6).astype(np.int64), V - 1), 3)
    hub = np.argsort(rng.random((N, 8, 1, V)), axis=3)
    w = np.take_along_axis(hub, np.minimum((V * rng.random((N, 8, 16, L)) ** 3).astype(np.int64), V - 1), 3)
    n = 2 * rng.integers(0, 8, (N, 8, L)) + 1; t = np.minimum(np.exp2(12 * rng.random((N, 8, L))).astype(np.int64) - 1, 4095)
    d = (x, c, w, n, t); trap(rng, d, 12, [])
    return pack(d)
def setup_inputs_ends(rng):
    cls = rng.integers(0, 5, (N, 8, 1, V)); cls[..., 0] = 0; cls[..., V - 1] = 1
    x = 254 * np.where(cls == 0, 0, np.where(cls == 1, 1, rng.integers(0, 2, (N, 8, 16, V))))
    c = np.where(rng.random((N, 8, 16, V)) < 0.7, (V - 1) * rng.integers(0, 2, (N, 8, 16, V)), rng.integers(0, V, (N, 8, 16, V)))
    w = np.where(rng.random((N, 8, 1, L)) < 0.25, rng.integers(0, V, (N, 8, 16, L)), (V - 1) * rng.integers(0, 2, (N, 8, 16, L)))
    n = 1 + 14 * rng.integers(0, 2, (N, 8, L)); t = 4095 * rng.integers(0, 2, (N, 8, L))
    for r in range(N):
        q = (r + S) % N
        for g in range(8):
            lo = rng.permutation(np.flatnonzero(cls[r, g, 0, 1:] == 0) + 1); up = rng.permutation(np.flatnonzero(cls[q, g, 0, :V - 1] == 1)); lq = rng.permutation(np.flatnonzero(cls[q, g, 0, 1:] == 0) + 1)
            uh = rng.permutation(np.flatnonzero(cls[r, g, 0, :V - 1] == 1))
            for m, l in enumerate((3, 8, L - 2, L - 1)):
                w[r, g][0::2, l] = lo[8 * m:8 * m + 8]; w[r, g][1::2, l] = up[8 * m:8 * m + 8]; n[r, g, l] = 15; t[r, g, l] = 4095
            for m, l in enumerate((5, L - 4, L - 3)):
                e = lo[32 + m]; col = np.concatenate([up[32:40], up[32:40]])
                if m > 0: col[15] = lq[0]
                if m > 1: col[6] = lq[1]
                c[r, g][:, e] = col; w[r, g][0, l] = e; n[r, g, l] = 1; t[r, g, l] = 4095
            for m, l in enumerate((6, L - 6, 11, L - 5)):
                e = lo[36 + m]; h = lo[40 + m]; f = up[44 + m]; z = lq[24 + m]
                w[r, g][0, l] = uh[m]; w[r, g][1, l] = z; w[r, g][2, l] = e; n[r, g, l] = 3; t[r, g, l] = 0
                if m < 2:
                    c[r, g][:15, e] = z; c[r, g][15, e] = f; c[q, g][:, f] = h
                else:
                    c[r, g][:, e] = f; c[q, g][:15, f] = uh[m]; c[q, g][15, f] = h
            if g % 2 == 0: c[r, g][:, V - 1] = lq[4:20]
            else:
                c[r, g][:15, V - 1] = V - 1; c[r, g][15, V - 1] = lq[4]
    return pack((x, c, w, n, t))
def setup_inputs_corners(rng):
    d = parts(rng); x, c, w, n, t = d
    for r in range(N):
        for g in range(8):
            k = (g + r) % 8
            if k == 0: w[r, g] = w[r, g][:1].copy(); n[r, g] = 15
            if k == 1: w[r, g] = (V - 1) * rng.integers(0, 2, (16, L)); n[r, g] = 1
            if k == 2: n[r, g] = 13 + 2 * rng.integers(0, 2, L)
            if k == 3: c[r, g] = np.arange(V)[None, :]
            if k == 4: c[r, g] = c[r, g][:1].copy()
            if k == 5: w[r, g] = rng.choice(np.array([0, V // 2, V - 1]), (16, L))
            if k == 6: n[r, g] = 1 + 14 * rng.integers(0, 2, L); t[r, g] = 0
            if k < 6: t[r, g] = 4095 * rng.integers(0, 2, L)
    trap(rng, d, 12, [V - 1, V - ST, V - ST - 1, 0])
    o = np.argsort(rng.random((N, 8, V)), axis=2)
    for r in (0, 1):
        q = (r + S) % N
        for g in range(8):
            w[r, g][0] = o[r, g, :L]; w[r, g][1] = o[q, g, L:2 * L]; w[r, g][2] = o[r, g, 2 * L:3 * L]; n[r, g] = 3; t[r, g] = 4095
    q = S % N
    for g in range(8):
        x[0, g][:, o[0, g, :L]] = x[q, g][:, o[q, g, L:2 * L]]
        e = o[0, g, 2 * L:3 * L:2]; f = o[q, g, 2 * L:3 * L:2]; v = x[q, g][:, f].copy(); s = rng.integers(6, 41, len(e))
        v[0] = np.where(v[0] < 200, v[0] + s, v[0] - s)
        x[0, g][:, e] = v; c[0, g][:, e] = f[None, :]
    t[0] = rng.choice(np.array([1, 2, 5, 4095]), (8, L))
    M = int(rng.choice(np.array([31, 63, 95]))); pk = rng.permutation(8 * L)[:M]; pick = np.zeros(8 * L, np.int64); pick[pk] = 4095
    t[1] = pick.reshape(8, L); q = (1 + S) % N
    for u in pk[:16]:
        g = int(u) // L; l = int(u) % L
        c[1, g][:, o[1, g, 2 * L + l]] = o[q, g, L + l]
    return pack(d)
def setup_inputs_crowd(rng):
    d = parts(rng); x, c, w, n, t = d
    n[...] = np.maximum(n, 3); t[...] = np.maximum(t, 1); o = np.argsort(rng.random((N, 8, V)), axis=2)
    far = rng.permutation(V); rest = far[(RO + 1) * L:]; z = int(rng.integers(0, N))
    c[:, 7] = rest[c[:, 7] % len(rest)]; w[:, 7] = rest[w[:, 7] % len(rest)]
    for r in range(N): o[r, 7, :len(rest)] = rng.permutation(rest)
    for g in range(8):
        s = rng.integers(0, 255, (16, 1))
        for r in range(N):
            q = (r + S) % N; a = o[r, g, :L]; b = o[q, g, L:2 * L]
            if g == 6:
                c[r, g] = rng.permutation(V)[:16][:, None]; continue
            x[r, g][:, a] = s; x[q, g][:, b] = s
            aa = a.copy(); bb = b.copy()
            if g in (0, 1, 2, 5): aa[:] = a[0]
            if g in (0, 1, 3, 5): bb[:] = b[0]
            if g == 1:
                u = int(rng.integers(0, L)); aa[u] = a[1]; bb[u] = b[1]
            if g == 4: aa = a[rng.integers(0, 3, L)]; bb = b[rng.integers(0, 3, L)]
            if g == 5: t[r, g, 0] = 0
            if g == 7: aa[L - 1] = a[0]
            w[r, g][0] = aa; w[r, g][1] = bb
    q = (z + S) % N; hs = far[:(RO + 1) * L].reshape(RO + 1, L); bs = rng.permutation(far[:RO * L]).reshape(RO, L)
    for m in range(RO):
        x[z, 7][:, hs[m]] = x[q, 7][:, bs[m]]; w[z, 7][2 * m] = hs[m]; w[z, 7][2 * m + 1] = bs[m]
    w[z, 7][2 * RO] = hs[RO]; n[z, 7] = 2 * RO + 1
    return pack(d)
def setup_inputs_ties(rng):
    d = parts(rng); x, c, w, n, t = d
    pat = 64 * rng.integers(0, 2, (1, 8, 16, 10)); x[...] = np.take_along_axis(pat, rng.integers(0, 10, (N, 8, 1, V)), 3)
    c[:, :, 8:] = c[:, :, :8].copy()
    t[...] = np.maximum(64 * rng.integers(0, 11, (N, 8, L)) + rng.integers(-1, 2, (N, 8, L)), 0)
    K = 24; o = np.argsort(rng.random((N, 8, V)), axis=2); z = np.argsort(rng.random((N, 8, L)), axis=2)
    for r in range(N):
        q = (r + S) % N
        for g in range(8):
            la = z[r, g, :K]; a = o[r, g, :K]; e = o[r, g, K:2 * K]; b = o[q, g, 2 * K:3 * K]
            s = rng.integers(1, 64, (1, K)); near = rng.integers(1, 8, K)
            v = np.floor(s * rng.random((16, K))).astype(np.int64); hi = 254 - np.floor(s * rng.random((16, K))).astype(np.int64)
            u = v.copy(); u[3] = u[3] + near
            x[r, g][:, a] = v; x[r, g][:, e] = u; x[q, g][:, b] = hi
            turn = rng.random(K) < 0.5
            w[r, g][0, la] = np.where(turn, e, a); w[r, g][1, la] = b; w[r, g][2, la] = np.where(turn, a, e); n[r, g][la] = 3
            t[r, g][la] = np.add.reduce(hi - v, axis=0) - near + rng.integers(-1, 2, K)
    trap(rng, d, 12, [])
    return pack(d)
def check_inputs(d):
    bad = []
    for k, lo, hi in (("pts", 0, 254), ("cand", 0, V - 1), ("way", 0, V - 1), ("cnt", 1, 15), ("th", 0, 4095)):
        a = np.asarray(d[k]).astype(np.float64)
        if not (np.min(a) >= lo and np.max(a) <= hi): bad.append("range of " + k)
    a = np.asarray(d["pts"]).astype(np.float64)
    if not np.all(a == np.floor(a)): bad.append("pts not whole")
    if np.any((np.asarray(d["cnt"]).astype(np.int64) & 1) != 1): bad.append("cnt not odd")
    return bad
def hop(e, xa, ca, xb, old, use):
    c = np.take_along_axis(ca, e[:, None, :], 2); xe = np.take_along_axis(xa, e[:, None, :], 2)
    xc = np.take_along_axis(xb, c.reshape(8, 1, 16 * L), 2).reshape(8, 16, 16, L)
    s = np.add.reduce(np.abs(xc - xe[:, :, None, :]), axis=1)
    on = np.any((c[:, :, None, :] == old[:, None]) & use[:, None], axis=2)
    ok = (xc[:, 0] != 255) & ~on
    i = np.argmin(np.where(ok, s, 9999), axis=1)
    return np.any(ok, axis=1), np.take_along_axis(c, i[:, None, :], 1)[:, 0]
def reference(pts, cand, way, cnt, th):
    x = pts.astype(np.float32).astype(np.int32).reshape(N, 8, 16, V); c = cand.astype(np.int64).reshape(N, 8, 16, V)
    w = way.astype(np.int64).reshape(N, 8, 16, L); n = cnt.astype(np.int64); t = th.astype(np.int64)
    rows = np.arange(16)[None, :, None]; low = np.arange(L)[:, None] > np.arange(L)[None, :]; A = [0] * N
    for rnd in range(RO):
        wins = []
        for r in range(N):
            q = (r + S) % N; p = w[r]; k = n[r]
            v = np.zeros((8, 16, 16, L), np.int32)
            v[:, :, 0::2] = np.take_along_axis(x[r], p[:, 0::2].reshape(8, 1, 8 * L), 2).reshape(8, 16, 8, L)
            v[:, :, 1::2] = np.take_along_axis(x[q], p[:, 1::2].reshape(8, 1, 8 * L), 2).reshape(8, 16, 8, L)
            dead = (v[:, 0] == 255) & (rows < k[:, None, :]); cut = np.any(dead, axis=1); j = np.argmax(dead, axis=1)
            pre = np.where((j & 1) == 1, j, np.maximum(j - 1, 0)); s = j + 2 - (j & 1); post = np.maximum(k - s, 0); first = pre >= post
            start = np.where(cut & ~first, s, 0); m = np.where(cut, np.where(first, pre, post), k); none = m == 0
            ix = np.minimum(rows + start[:, None, :], 15)
            p2 = np.take_along_axis(p, ix, 1); v = np.take_along_axis(v, ix[:, None], 2)
            new = p[:, 0] + ST; new = np.where(new >= V, new - V, new)
            p2[:, 0] = np.where(none, new, p2[:, 0]); m = np.where(none, 1, m)
            live = (v[:, 0] != 255) & (rows < m[:, None, :])
            d = np.add.reduce(np.abs(v[:, :, :15] - v[:, :, 1:]), axis=1)
            d = np.where(live[:, :15] & live[:, 1:], d, 9999)
            i = np.argmin(d, axis=1); least = np.min(d, axis=1); prop = least < t[r] + 8 * (A[r] & 31)
            a = np.take_along_axis(p2, (i + (i & 1))[:, None, :], 1)[:, 0]; b = np.take_along_axis(p2, (i + 1 - (i & 1))[:, None, :], 1)[:, 0]
            same = (a[:, :, None] == a[:, None, :]) | (b[:, :, None] == b[:, None, :])
            win = prop & ~np.any(same & low[None] & prop[:, None, :], axis=2)
            mid = (np.take_along_axis(x[r], a[:, None, :], 2) + np.take_along_axis(x[q], b[:, None, :], 2)) >> 1
            wins.append((win, a, b, mid)); w[r] = p2; n[r] = m
        for r in range(N):
            win, a, b, mid = wins[r]; A[r] = int(np.count_nonzero(win))
            for g in range(8): x[r, g][:, a[g][win[g]]] = mid[g][:, win[g]]
        for r in range(N):
            win, a, b, mid = wins[r]; q = (r + S) % N
            for g in range(8): x[q, g][:, b[g][win[g]]] = 255
        for r in range(N):
            q = (r + S) % N
            for h in range(HP):
                p = w[r]; k = n[r]; use = rows < k[:, None, :]
                e = np.take_along_axis(p, k[:, None, :] - 1, 1)[:, 0]
                f1, u1 = hop(e, x[r], c[r], x[q], p[:, 1::2], use[:, 1::2])
                f2, u2 = hop(u1, x[q], c[q], x[r], p[:, 0::2], use[:, 0::2])
                go = f1 & f2 & (k <= 13)
                p = np.where(go[:, None, :] & (rows == k[:, None, :]), u1[:, None, :], p)
                p = np.where(go[:, None, :] & (rows == k[:, None, :] + 1), u2[:, None, :], p)
                w[r] = p; n[r] = np.where(go, k + 2, k)
    w = np.where(np.arange(16)[None, None, :, None] < n[:, :, None, :], w, 0)
    return {"yx": x.reshape(N, 128, V).astype(np.float32).astype(BF), "yw": w.reshape(N, 128, L).astype(np.float32), "yn": n.astype(np.float32)}

@@ -1,0 +1,880 @@
+import numpy as np
+from concourse.bass import DstId, RemoteDMATransfer
+from concourse.mybir import AluOpType as A, AxisListType, ActivationFunctionType as F
+
+V, L, RO, SH, ST = 3328, 256, 4, 3, 61
+VP = V + L
+CEN = V // 2
+BIG = float(2 ** 20)
+THR = 70000.0
+PEN = 98304.0
+M1 = 1.5 * 2 ** 23
+M2 = 1.5 * 2 ** 24
+M16 = 1.5 * 2 ** 27
+GC = 32
+NV1, NV2 = 96, 96
+XV1, XV2 = 32, 0
+SB1, SB2, SB3 = "347", "34", "346"
+VG = 7
+FS = 4
+PB = 3000.0
+SEED, TRIES = 0, 2500
+LLV = [(0, 0), (0, 1), (1, 0)]
+EV = ["VSVVVSVV", "VSVSVSVS", "VSVSVSVS", "VSVSVSVS"]
+NCH = 4
+CW = V // NCH
+
+SCRATCH = {}
+for _d, _l in (
+        ("bfloat16", (("X", 2 * VP), ("XO", V), ("CT", VP), ("VV", 4096), ("XC", 4096), ("ED", 14 * 256), ("L2", 1536), ("IL", 160), ("K16", 768),
+                      ("nIb", 128), ("PENI", 128), ("Bx", 128), ("nB16", 128), ("BB", 64), ("NST", 768), ("KI", 512), ("KH", 256), ("DP", 256),
+                      ("DN", 256), ("negL", 32), ("SELN", 256), ("cb", 256), ("GB", 1024), ("Q", 96), ("QT", 128), ("Me", 256), ("Mf", 256),
+                      ("Mn", 256), ("Mz", 256), ("xs", 256), ("EQ", 7 * 256), ("OH", 512), ("D1", 768), ("U", 768), ("PN", 768), ("D3", 256),
+                      ("U3", 256), ("RR", 512), ("LL", 1024), ("junk", 1536), ("m2", 256), ("mid", 1024), ("rmid", 1024), ("Lo", 64),
+                      ("cm", 128), ("ones", 128), ("wn", 16))),
+        ("float16", (("Ih", 128), ("nIh", 128), ("SEL", 13 * 128), ("LB", 3 * 144), ("DS", 3 * 128), ("Bo", 256), ("B2", 24), ("DA", 256), ("DB", 256), ("Wa", 256),
+                     ("Wn", 256), ("Wz", 256), ("Wf", 256), ("TT", 256), ("TS", 768), ("Y1", 256), ("Y2", 256), ("Ye", 256), ("Yl", 256), ("Cc", 512),
+                     ("D2", 256), ("T1", 256), ("T2", 256))),
+        ("float32", (("Li", 256), ("RST", 512), ("CR", 512), ("KM", 16), ("col", 32), ("thr", 16), ("tf", 256), ("I8", 8), ("pm", 512), ("pe", 512),
+                     ("km", 256), ("sm", 1024), ("xa", 256), ("xb", 256), ("abf", 32), ("ef", 32), ("Hi", 64), ("tq", 256), ("yo", 256),
+                     ("yq", 256), ("yc", 256))),
+        ("int32", (("CA", V), ("CP", V), ("si", 64), ("wi", 256), ("ci", 256), ("ti", 256), ("pi", 4))),
+        ("uint16", (("WO", 256), ("CO", 256), ("el", 16), ("fl", 64), ("rs", 256), ("CU", V), ("CQ", V), ("ab", 32), ("eff", 128), ("rl", 128)))):
+    for _n, _c in _l:
+        SCRATCH[_n] = ("sbuf", [128, _c], _d)
+SCRATCH["MM"] = ("sbuf", [128, 16, 256], "bfloat16")
+for _n in range(8):
+    SCRATCH["P%d" % _n] = ("psum", [128, 512], "float32")
+
+SEMAPHORES = (["sV", "sS", "sP", "sG", "ls0", "ls1", "xarr", "lw", "lc", "lt", "ox", "ow", "on"]
+              + ["%s%d" % (s, i) for s in ("lx", "hx", "hc", "lk", "ca") for i in range(NCH)]
+              + ["%s%d" % (s, r) for s in ("am", "aa", "ak") for r in range(RO)])
+TWO = ("bfloat16", "float16", "uint16")
+
+
+def a(name, c0=0, c1=None, st=1, p=None):
+    return ("a", name, c0, SCRATCH[name][1][1] if c1 is None else c1, st, p)
+
+
+def rev(name, c0, c1):
+    return ("r", name, c0, c1)
+
+
+def m3(i0, i1, l0, l1):
+    return ("m", "MM", i0, i1, l0, l1)
+
+
+def ind(w, o):
+    return ("i", w, o)
+
+
+def isop(x):
+    return isinstance(x, tuple)
+
+
+def regs(x):
+    if x[0] == "i":
+        return regs(x[1]) + regs(x[2])
+    if x[0] == "m":
+        return [("MM", 256 * i + x[4], 256 * i + x[5]) for i in range(x[2], x[3])]
+    return [(x[1], x[2], x[3])]
+
+
+def cnt(x):
+    if x[0] == "i":
+        return 16 * cnt(x[2])
+    if x[0] == "m":
+        return (x[3] - x[2]) * (x[5] - x[4])
+    if x[0] == "r":
+        return x[3] - x[2]
+    return len(range(x[2], x[3], x[4]))
+
+
+def dty(x):
+    return SCRATCH[x[1][1] if x[0] == "i" else x[1]][2]
+
+
+def ps(x):
+    return x[0] != "i" and SCRATCH[x[1]][0] == "psum"
+
+
+def mk(T, x):
+    if not isop(x):
+        return x
+    if x[0] == "i":
+        return mk(T, x[1]).indirect(mk(T, x[2]))
+    if x[0] == "m":
+        if x[3] - x[2] == 1:
+            return T["MM"][:, x[2], x[4]:x[5]]
+        return T["MM"][:, x[2]:x[3], x[4]:x[5]]
+    if x[0] == "r":
+        return T[x[1]][:, x[3] - 1:(x[2] - 1 if x[2] else None):-1]
+    p = slice(None) if x[5] is None else slice(x[5][0], x[5][1])
+    if x[4] == 1:
+        return T[x[1]][p, x[2]:x[3]]
+    return T[x[1]][p, x[2]:x[3]:x[4]]
+
+
+OPS = []
+CY, GA, SCA, PEC, VF, SF, SL, RI, RL = 1.04, 1.56, 3.8, 0.52, 30.0, 60.0, 120.0, 700.0, 2500.0
+
+
+def op(eng, emit, rd, wr, cost, tok=None, lat=0.0, track=True, after=()):
+    r = [q for x in rd if isop(x) for q in regs(x)]
+    w = [q for x in wr for q in regs(x)]
+    o = {"eng": eng, "emit": emit, "r": r, "w": w, "cost": cost, "tok": tok, "lat": lat, "track": track, "after": list(after), "n": len(OPS)}
+    OPS.append(o)
+    return o
+
+
+def _vc(out, ins, base):
+    n = cnt(out)
+    if out[0] == "i":
+        return 50 + SCA * CY * n
+    if ins[0][0] == "i":
+        return 50 + GA * CY * n
+    return VF + max(64, n * base) * CY
+
+
+def _half(*xs):
+    return 0.5 if all(dty(x) in TWO for x in xs) else 1.0
+
+
+def cp(out, in_):
+    return op("V", lambda g, T, c: g.vector.tensor_copy(mk(T, out), mk(T, in_)), [in_] + ([out[2]] if out[0] == "i" else []),
+              [out[1] if out[0] == "i" else out], _vc(out, [in_], _half(out, in_)))
+
+
+def ts(out, in_, s1, o1, s2=None, o2=None):
+    if o2 is None:
+        e = lambda g, T, c: g.vector.tensor_scalar(mk(T, out), mk(T, in_), mk(T, s1), None, o1)
+    else:
+        e = lambda g, T, c: g.vector.tensor_scalar(mk(T, out), mk(T, in_), mk(T, s1), mk(T, s2), o1, o2)
+    return op("V", e, [in_, s1, s2], [out], _vc(out, [in_], _half(out, in_)))
+
+
+def tt(out, x, y, o):
+    b = 1.0 if (ps(x) or ps(y) or x[0] == "i") else 2.0
+    return op("V", lambda g, T, c: g.vector.tensor_tensor(mk(T, out), mk(T, x), mk(T, y), o), [x, y], [out], _vc(out, [x], b))
+
+
+def scan(out, d0, d1, init, o0, o1):
+    return op("V", lambda g, T, c: g.vector.tensor_tensor_scan(mk(T, out), mk(T, d0), mk(T, d1), init, o0, o1), [d0, d1], [out],
+              _vc(out, [d0], _half(out, d0, d1)))
+
+
+def red(out, in_, o):
+    return op("V", lambda g, T, c: g.vector.tensor_reduce(mk(T, out), mk(T, in_), AxisListType.X, o), [in_], [out], VF + max(64, cnt(in_)) * CY)
+
+
+def ms(out, v):
+    return op("V", lambda g, T, c: g.vector.memset(mk(T, out), v), [], [out], VF + max(64, cnt(out) * _half(out)) * CY)
+
+
+def act(out, in_, f, bias=0.0, scale=1.0, acc=None):
+    n = cnt(in_)
+    co = 65 + GA * CY * n if in_[0] == "i" else SF + max(64, n) * CY
+    if acc is None:
+        e = lambda g, T, c: g.scalar.activation(mk(T, out), mk(T, in_), f, mk(T, bias), mk(T, scale))
+    else:
+        e = lambda g, T, c: g.scalar.activation(mk(T, out), mk(T, in_), f, mk(T, bias), mk(T, scale), accum_out=mk(T, acc))
+    return op("S", e, [in_, bias, scale], [out] + ([acc] if acc else []), co)
+
+
+def pe(ml):
+    def e(g, T, c):
+        for m in ml:
+            r = g.tensor.matmul(mk(T, m[0]), mk(T, m[1]), mk(T, m[2]), m[3], m[4])
+        return r
+    co = 40 + sum(max(min(64, cnt(m[1])), cnt(m[2])) * (4 if dty(m[1]) == "float32" else 1) * PEC for m in ml)
+    return op("P", e, [x for m in ml for x in m[1:3]], [m[0] for m in ml], co)
+
+
+def iota(out, pat, base, cm):
+    if dty(out) == "int32":
+        e = lambda g, T, c: g.iota(mk(T, out), pat, base, cm)
+    else:
+        e = lambda g, T, c: g.iota(mk(T, out), pat, base, cm, allow_small_or_imprecise_dtypes=True)
+    return op("G", e, [], [out], 130 + 2 * CY * cnt(out))
+
+
+def load(q, out, src, sem, lat):
+    def e(g, T, c):
+        (g.sync if q == "Y" else g.scalar).dma_start(mk(T, out), src(T)).then_inc(T.sem[sem], 16)
+    return op(q, e, [], [out], 100, tok=(sem, 16), lat=lat)
+
+
+def store(dst, src, reg, sem, lat):
+    def e(g, T, c):
+        g.sync.dma_start(dst(T), src(T)).then_inc(T.sem[sem], 16)
+    return op("Y", e, [reg], [], 100, tok=(sem, 16), lat=lat)
+
+
+def sm(i, n=16, o=0):
+    return a("sm", 16 * i + o, 16 * i + o + n)
+
+
+def col(i):
+    return a("col", i, i + 1)
+
+
+def blk(name, i, w=256, o=0, n=None):
+    return a(name, w * i + o, w * i + o + (w if n is None else n))
+
+
+I_ = a("IL", 16, 144)
+B32, Bm16, B16, Bm1, B1 = [a("BB", 8 * i, 8 * i + 8) for i in range(5)]
+(KC, KC1, KK, OFF, M15, IS15, MG0, MG1, VB0, VB1, DU0, DU1, SC, MLO, MHI, M12, EVN, ODD, PF, R0, AC, CM5, MA0, MA1, MB0, MB1, KF) = range(27)
+(NL, BND, TH16, JJ, CUT, T0, FL, S_, CE, PRE, QQ, NS, KEY0, KEYX, C2, K1, PEN1, TT_, UU, GB_, GO2, KS, T1_, T2_, T3_, NP_, MA, CB,
+ T4_, T5_, MM_, ED_, H1, H2, H4, E1, E2, E3, E4, E5, E6, C1, C3, C5, W0, W1, W2, W3, KF_, KB_, U1, U2, U4) = range(53)
+OWN, PAR, OWND, PARD = a("X", 0, V), a("X", VP, VP + V), a("X", 0, VP), a("X", VP, 2 * VP)
+WP = a("P5", 0, 256)
+rot = [0]
+
+
+def sbank(sb):
+    rot[0] += 1
+    return "P" + sb[rot[0] % len(sb)]
+
+
+def tolist(out0, w, y, bk="P2"):
+    return [(a(bk, out0, out0 + 16), a("LB", 144 * w + 15 - b, 144 * w + 143 - b), a(y, b, 256, 16), b == 0, b == 15) for b in range(16)]
+
+
+def consts():
+    iota(a("pi", 0, 1), [[0, 1]], 0, 1)
+    iota(a("IL"), [[1, 160]], -16, -1)
+    iota(a("K16", 0, 256), [[0, 16], [1, 16]], 0, 0)
+    iota(a("Li"), [[1, 256]], 0, 0)
+    for i in range(3):
+        iota(blk("L2", i, 512), [[1, 32], [0, 16]], 32 * i, -1)
+        ts(blk("L2", i, 512), blk("L2", i, 512), 0.0, A.is_equal)
+    cp(col(PF), a("pi", 0, 1))
+    ts(a("pi", 1, 2), a("pi", 0, 1), 15, A.bitwise_and)
+    cp(col(KC), a("pi", 1, 2))
+    ts(a("pi", 2, 3), a("pi", 0, 1), 1, A.bitwise_and)
+    cp(col(ODD), a("pi", 2, 3))
+    ts(a("pi", 3, 4), a("pi", 0, 1), 16, A.bitwise_and)
+    ts(col(MG1), a("pi", 3, 4), 1.0 / 16, A.mult)
+    ts(col(MG0), col(MG1), -1.0, A.mult, 1.0, A.add)
+    ts(col(KC1), col(KC), 1.0, A.add)
+    ts(col(IS15), col(KC), 15.0, A.is_equal)
+    ts(col(M15), col(KC), 15.0, A.not_equal)
+    ts(col(OFF), col(ODD), float(VP), A.mult, float(CEN), A.add)
+    ts(col(EVN), col(ODD), -1.0, A.mult, 1.0, A.add)
+    ts(col(KK), col(KC), col(EVN), A.subtract, col(M15), A.mult)
+    ts(col(EVN), col(EVN), col(IS15), A.add)
+    ts(col(VB0), col(PF), 1.0 / 128, A.mult, -12.0, A.add)
+    ts(col(VB1), col(PF), 1.0 / 128, A.mult, -11.0, A.add)
+    ts(col(DU0), col(PF), float(CEN), A.add)
+    ts(col(DU1), col(PF), float(CEN + 128), A.add)
+    ts(col(R0), col(KC), 0.0, A.is_equal)
+    ts(col(MLO), col(KC), 6.0, A.is_lt)
+    ts(col(M12), col(KC), 12.0, A.is_equal)
+    ts(col(MHI), col(KC), 12.0, A.is_lt, col(MLO), A.subtract)
+    ms(col(CM5), -0.5)
+    ts(col(KF), col(KC1), 3584.0, A.mult)
+    for gm in range(2):
+        tt(col(MB0 + gm), col(MG0 + gm), col(M12), A.mult)
+        tt(col(MA0 + gm), col(MG0 + gm), col(MB0 + gm), A.subtract)
+    ts(a("IL"), a("IL"), 0.0, A.is_equal)
+    cp(blk("K16", 1), blk("K16", 0))
+    cp(blk("K16", 2), blk("K16", 0))
+    ts(a("nIb"), I_, -1.0, A.mult)
+    ts(a("PENI"), I_, PEN, A.mult)
+    cp(a("Ih"), I_)
+    cp(a("nIh"), a("nIb"))
+    cp(a("I8"), a("IL", 16, 24))
+    pe([(a("P2", 0, 128), a("L2", 0, 128, p=(0, 8)), a("L2", 0, 128, p=(0, 8)), True, True)])
+    cp(a("Bx"), a("P2", 0, 128))
+    ts(a("nB16"), a("Bx"), -16.0, A.mult)
+    for x, v in ((B32, 32.0), (Bm16, -16.0), (Bm1, -1.0), (B1, 1.0), (a("BB", 48, 56), 16.0), (a("BB", 56, 64), 16.0),
+                 (a("B2", 0, 8), 2.0), (a("B2", 8, 16), -2.0), (a("B2", 16, 24), col(R0))):
+        ts(x, a("Bx", 0, 128, 16), v, A.mult)
+    ts(a("KM"), a("K16", 0, 16), col(KC), A.is_equal)
+    for k in range(13):
+        act(blk("EQ", k, 128), a("Bx"), F.Identity, 0.0, a("KM", k, k + 1))
+    cp(a("SEL"), a("EQ", 0, 13 * 128))
+    ms(a("LB"), 0.0)
+    cp(a("LB", 15, 143, 16), B1)
+    ts(a("LB", 144 + 15, 144 + 143, 16), B1, col(EVN), A.mult)
+    ts(a("LB", 288 + 15, 288 + 143, 16), B1, col(ODD), A.mult)
+    ms(a("Bo"), 0.0)
+    cp(a("Bo", 1, 128, 2), a("Bx", 1, 128, 2))
+    cp(a("Bo", 128, 256, 2), a("Bx", 0, 128, 2))
+    for i, s in enumerate((2, 4, 8)):
+        d = blk("DS", i, 128)
+        tt(d, a("IL", 16 + s, 144 + s), I_, A.subtract)
+        ts(a("cm"), a("K16", 0, 128), 14.0 - s, A.is_le)
+        tt(d, d, a("cm"), A.mult)
+    ts(a("RST"), a("K16", 0, 512), 0.0, A.is_equal, 16 * BIG, A.mult)
+    ts(a("NST"), a("K16"), 0.0, A.not_equal)
+    ts(a("KI"), a("K16", 0, 512), -7.5, A.add)
+    ts(a("KH"), blk("K16", 0), 1.0 / 16, A.mult)
+    ts(a("DB"), blk("K16", 0), col(KC), A.is_lt)
+    ts(a("DA"), blk("K16", 0), col(KC), A.is_le)
+    ms(a("DA", 0, 256, 16), 0.0)
+    for x, v in ((a("DP"), 1024.0), (a("DN"), -1024.0), (a("X", V, VP), 0.0), (a("X", VP + V, 2 * VP), 0.0), (a("CT", V, VP), 0.0), (a("D1"), -1.0),
+                 (a("D3"), -1.0), (a("D2"), 0.0), (a("Q"), 0.0), (a("ones"), 1.0), (a("SELN"), 0.0), (sm(T2_), 0.5), (sm(T3_), 0.0)):
+        ms(x, v)
+    for h in range(2):
+        ts(blk("negL", h, 16), a("Li", 0, 256, 16), col(KC), A.add, -1.0, A.mult)
+        ts(blk("thr", h, 8), a("K16", 0, 8), VG - 0.5, A.is_lt, col(VB0 + h), A.mult)
+        ts(blk("CR", h), a("Li"), 128.0, A.add, col(M12), A.mult)
+        b1, b2 = 16 * (48 + 8 * h), 16 * (64 + 8 * h)
+        ts(sm(T0, 8), a("L2", b1, b1 + 128, 16), float(ST), A.mult)
+        ts(sm(T1_, 8), a("L2", b2, b2 + 128, 16), float(-V), A.mult)
+        tt(a("SELN", 128 * h, 128 * h + 128, 16), sm(T0, 8), sm(T1_, 8), A.add)
+    act(a("CR"), a("CR"), F.Identity, 0.0, -1.0 / 128)
+    scan(sm(T4_, 6), sm(T2_, 6), sm(T3_, 6), 1.0, A.mult, A.add)
+    cp(sm(T4_, 6, 6), sm(T4_, 6))
+    tt(sm(T5_, 12), sm(T4_, 12), a("KM", 0, 12), A.mult)
+    red(col(SC), sm(T5_, 12), A.add)
+    ts(blk("tq", 0, 64), a("Li", 0, 64), 0.5, A.add, col(SC), A.mult)
+    ts(blk("tq", 1, 64), blk("tq", 0, 64), M1, A.add, M1, A.subtract)
+    tt(blk("tq", 2, 64), blk("tq", 0, 64), blk("tq", 1, 64), A.is_gt)
+    ts(blk("tq", 3, 64), blk("tq", 2, 64), 2.0, A.mult, -1.0, A.add)
+    ts(a("Lo"), blk("tq", 3, 64), col(MLO), A.mult, col(M12), A.add)
+    ts(a("Hi"), blk("tq", 3, 64), col(MHI), A.mult)
+    for c in range(V // 64):
+        act(blk("CT", c, 64), a("Lo"), F.Identity, a("Hi", c, c + 1))
+
+
+def post_cut():
+    nG = blk("GB", 3)
+    ts(a("Me"), nG, col(KC1), A.is_equal)
+    tt(a("Yl"), WP, a("Me"), A.mult)
+    pe(tolist(0, 0, "Yl", "P1"))
+    ts(a("el"), a("P1", 0, 16), float(CEN), A.add)
+    cp(a("CO"), ind(a("CA"), a("el")))
+    ts(blk("Cc", 0), a("CO"), float(-CEN), A.add)
+    act(a("Mf"), nG, F.Relu, col(KF), -3584.0)
+    tt(a("Wf"), WP, a("Mf"), A.add)
+    ts(a("Mn"), nG, col(KK), A.is_equal)
+    act(a("Mz"), a("Mn"), F.Identity, 1.0, -1.0)
+    tt(a("Wz"), WP, a("Mz"), A.mult)
+    ts(a("WO"), WP, col(OFF), A.add)
+
+
+def fit(rows, cc, ns=0):
+    pe([(a("P0", 0, 256), I_, a("KH"), True, False)])
+    rows = list(rows)
+    for j in range(0, ns, 2):
+        bk = sbank("34")
+        pe([m for u in range(2) for m in ((blk(bk, u), blk("SEL", rows[j + u], 128), a("Wf"), True, False), (blk(bk, u), a("nIh"), cc, False, True))])
+        act(blk("junk", j // 2, 512), a(bk), F.Abs)
+        act(blk("EQ", j // 2, 512), blk("junk", j // 2, 512), F.Relu, 1.0, -1.0)
+        pe([(blk("P0", h, 128), blk("EQ", 2 * (j + u) + h, 128), a("PENI"), False, False) for u in range(2) for h in range(2)])
+    for j, k in list(enumerate(rows))[ns:]:
+        bk = "P7" if j % 2 == 0 else "P6"
+        pe([(a(bk, 0, 256), blk("SEL", k, 128), a("Wf"), True, True)])
+        tt(blk("EQ", j), a(bk, 0, 256), cc, A.is_equal)
+        pe([(blk("P0", h, 128), blk("EQ", 2 * j + h, 128), a("PENI"), False, False) for h in range(2)])
+
+
+def gather(eng, out, src):
+    return cp(out, src) if eng == "V" else act(out, src, F.Copy)
+
+
+def hop(win, co, cc, nv, xv, sb, y, lout):
+    for u in range(0, 256, GC):
+        gather("V" if u < nv or u >= 256 - xv else "S", a("XC", 16 * u, 16 * (u + GC)), ind(win, a(co, u, u + GC)))
+    xe = a("P2", 384, 384 + nv)
+    if nv:
+        pe([(xe, I_, a("xs", 0, nv), True, True)])
+    l0 = nv
+    while l0 < 256:
+        l1 = min(256, (l0 // 64 + 1) * 64)
+        w = l1 - l0
+        ni = 512 // w
+        for i0 in range(0, 16, ni):
+            bk = sbank(sb)
+            ml = []
+            for i in range(i0, i0 + ni):
+                o = blk(bk, i - i0, w)
+                ml += [(o, I_, a("XC", 16 * l0 + i, 16 * l1, 16), True, False), (o, a("nIb"), a("xs", l0, l1), False, True)]
+            pe(ml)
+            act(m3(i0, i0 + ni, l0, l1), a(bk), F.Abs, 0.0, 0.5)
+        l0 = l1
+    if nv:
+        for i in range(16):
+            tt(m3(i, i + 1, 0, nv), a("XC", i, 16 * nv, 16), xe, A.max)
+        pe([(a("P0", 0, 128, p=(0, nv)), a("xs", 0, nv), a("nB16"), False, False)]
+           + [(a("P0", i, 128, 16, p=(0, nv)), a("XC", i, 16 * nv, 16), Bm16, False, False) for i in range(16)])
+    pe([(a("P0", 128 + i, 256, 16), m3(i, i + 1, 128, 256), B32, False, False) for i in range(16)])
+    pe([(a("P0", i, 128, 16), m3(i, i + 1, 0, 128), B32, False, i == 15) for i in range(16)])
+    key = a("P0", 0, 256)
+    scan(blk("pm", 0), blk("RST", 0), key, 0.0, A.add, A.min)
+    scan(rev("km", 0, 256), blk("RST", 0), rev("pm", 0, 256), 0.0, A.add, A.min)
+    tt(blk("OH", 0), key, a("km"), A.is_equal)
+    pe([(blk("P2", h, 128), blk("OH", h, 128), I_, True, True) for h in range(2)])
+    tt(a(y), a("P2", 0, 256), cc, A.mult)
+    if lout is not None:
+        pe(tolist(256, 0, y))
+        ts(lout, a("P2", 256, 272), float(CEN), A.add)
+
+
+def edges(r):
+    for j, l0 in enumerate(range(0, 256, GC)):
+        gather(EV[r][j], a("VV", 16 * l0, 16 * (l0 + GC)), ind(a("X"), a("WO", l0, l0 + GC)))
+    row = lambda h, k: a("VV", 2048 * h + k, 2048 * h + 2048, 16)
+    if r > 0:
+        pe([(a("P7", 0, 256), I_, blk("KI", 0), True, False)]
+           + [(a("P7", 128 * h + k, 128 * h + 128, 16), row(h, k), B1 if k & 1 else Bm1, False, h == 1 and k == 14) for h in range(2) for k in range(15)])
+        scan(blk("pm", 1), blk("RST", 0), a("P7", 0, 256), 0.0, A.add, A.min)
+        ts(sm(JJ), a("pm", 256 + 15, 512, 16), 16391.5, A.add, 16.0, A.min)
+        tt(sm(CUT), sm(JJ), sm(NL), A.is_lt)
+        act(sm(E1), sm(JJ), F.Identity, -0.25, 0.5)
+        ts(sm(FL), sm(E1), M1, A.add, M1, A.subtract)
+        act(sm(E2), sm(FL), F.Identity, 2.0, 2.0)
+        tt(sm(S_), sm(E2), sm(CUT), A.mult)
+        tt(sm(CE), sm(JJ), sm(FL), A.subtract)
+        act(sm(E3), sm(CE), F.Relu, -1.0, 2.0)
+        tt(sm(PRE), sm(E3), sm(CUT), A.mult)
+        act(a("D1", 0, 256, 16), sm(PRE), F.Identity, -1.0)
+        act(a("D1", 512, 768, 16), sm(S_), F.Copy)
+        cp(a("si", 0, 16), sm(S_))
+        for j in range(3):
+            ts(blk("si", j + 1, 16), a("si", 0, 16), 2 << j, A.bitwise_and)
+        tt(sm(NS), sm(NL), sm(S_), A.subtract)
+        tt(sm(QQ), sm(PRE), sm(NS), A.subtract)
+        act(sm(W0), sm(QQ), F.Relu, 0.0, -BIG)
+        act(sm(W1), sm(QQ), F.Relu, BIG, BIG)
+        act(sm(W2), sm(QQ), F.Relu, 2 * BIG, -BIG)
+        act(sm(W3), sm(QQ), F.Relu, -BIG, BIG)
+        tt(sm(E4), sm(K1), sm(W3), A.add)
+        act(sm(E5), sm(NS), F.Relu, 0.0, -BIG)
+        tt(sm(E5), sm(E5), sm(W3), A.add)
+        act(sm(E6), sm(NL), F.Identity, -7.5)
+        tt(sm(C2), sm(E5), sm(E6), A.add)
+    act(a("D1", 256, 512, 16), sm(NL), F.Identity, -1.0)
+    c0, c1 = (0, 768) if r > 0 else (256, 512)
+    js = (0, 1, 2) if r > 0 else (1,)
+    scan(a("U", c0, c1), a("NST", c0, c1), a("D1", c0, c1), 0.0, A.mult, A.add)
+    act(a("PN", c0, 512), a("U", c0, 512), F.Relu, BIG, -BIG)
+    if r > 0:
+        act(blk("PN", 2), blk("U", 2), F.Relu, 0.0, BIG)
+    pe([(a("P1"), I_, a("KI"), True, False)])
+    for h in range(2):
+        for k0 in range(0, 14, 4):
+            bk = sbank(SB3)
+            ks = range(k0, min(k0 + 4, 14))
+            ml = []
+            for k in ks:
+                o = blk(bk, k - k0, 128)
+                ml += [(o, I_, row(h, k), True, False), (o, a("nIb"), row(h, k + 1), False, True)]
+            pe(ml)
+            act(blk("ED", 14 * h + k0, 128, 0, 128 * len(ks)), a(bk, 0, 128 * len(ks)), F.Abs)
+            pe([(a("P1", 256 * h + k, 256 * h + 256, 16), blk("ED", 14 * h + k, 128), a("BB", 48, 64), False, False) for k in ks])
+    pe([(blk("P1", 2 * h + min(j, 1), 128), I_, blk("PN", 2 * j + h, 128), False, h == 1 and j == js[-1]) for h in range(2) for j in js])
+    if r == 0:
+        for h in range(2):
+            scan(blk("pm", h, 128), a("RST", 0, 128), blk("P1", 2 * h + 1, 128), 0.0, A.add, A.min)
+    else:
+        scan(a("pe"), a("RST"), a("P1"), 0.0, A.add, A.min)
+        for h in range(2):
+            kf, kb = a("pe", 256 * h + 15, 256 * h + 128, 16), a("pe", 256 * h + 143, 256 * h + 256, 16)
+            for w, k in ((W0, kf), (W1, kb), (W2, kf), (W3, kb)):
+                tt(sm(w, 8, 8 * h), k, sm(w, 8, 8 * h), A.add)
+        tt(sm(KEY0), sm(W0), sm(W1), A.min)
+        tt(sm(E4), sm(E4), sm(W2), A.min)
+        tt(sm(KEYX), sm(E4), sm(W3), A.min)
+
+
+def bcast(qs):
+    p = (0, 96)
+    pe([(a("P0", 384, 512, p=p), a("Q"), I_, True, True)])
+    act(a("QT", p=p), a("P0", 384, 512, p=p), F.Copy)
+    for bk, js in (("P1", [j for j in qs if j >= 2]), ("P0", [j for j in qs if j < 2])):
+        if js:
+            b = lambda j, h: 16 * (16 * (0, 1, 2, 5)[j] + 8 * h)
+            pe([(blk(bk, 2 * (j % 2) + h, 128), a("L2", b(j, h), b(j, h) + 128, p=p), a("QT", p=p), True, True) for j in js for h in range(2)])
+            for j in js:
+                act(blk("GB", j), blk(bk, j % 2), F.Identity, 0.0, (0.5, 0.25, 0.125, 1.0)[j])
+
+
+def program():
+    for i in range(NCH):
+        load("Y", blk("X", i, CW), (lambda i: lambda T: T.pts[:, CW * i:CW * i + CW])(i), "lx%d" % i, 2200 + 400 * i)
+    load("S", a("wi"), lambda T: T.way[:, :], "lw", 2200)
+    load("S", a("ci", p=(0, 8)), lambda T: T.cnt[:, :], "lc", 2200)
+    load("S", a("ti", p=(0, 8)), lambda T: T.th[:, :], "lt", 2200)
+    for i in range(NCH):
+        load("Y", blk("CA", i, CW), (lambda i: lambda T: T.cand[:, CW * i:CW * i + CW])(i), "lk%d" % i, 4000 + 800 * i)
+    ss = []
+    for i in range(NCH):
+        ss.append(op("G", (lambda i: lambda g, T, c: c["big"]("X", i))(i), [blk("X", i, CW)], [], 1500 if i == 0 else RI, track=False))
+        ss[-1]["prio"] = 1e9
+    op(None, None, [OWN], [], 0, tok=("ls0", None), lat=9000, after=ss)
+    op(None, None, [], [PAR], 0, tok=("xarr", None), lat=12000, after=ss)
+    for i in range(NCH):
+        cp(blk("CU", i, CW), blk("CA", i, CW))
+        sc = op("G", (lambda i: lambda g, T, c: c["big"]("C", i))(i), [blk("CU", i, CW), PAR], [], RI, track=False, after=ss)
+        op(None, None, [], [blk("CQ", i, CW)], 0, tok=("ca%d" % i, None), lat=7000 + 2000 * i, after=[sc])
+        for j in range(2):
+            cp(blk("CP", 2 * i + j, CW // 2), blk("CQ", 2 * i + j, CW // 2))
+    consts()
+    ts(a("Wa"), a("wi"), float(-CEN), A.add, col(M15), A.mult)
+    ts(a("TT"), a("Li"), float(CEN), A.add, col(IS15), A.mult)
+    pe([(WP, a("Ih"), a("Wa"), True, False), (WP, a("Ih"), a("TT"), False, True)])
+    cp(a("Wn"), WP)
+    p8 = (0, 8)
+    cp(a("cb", p=p8), a("ci", p=p8))
+    ts(a("tf", p=p8), a("ti", p=p8), 16.0, A.mult, -8.0, A.add)
+    pe([(a("P0", 0, 256), a("L2", 0, 128, p=p8), a("cb", p=p8), True, True)])
+    act(blk("GB", 3), a("P0", 0, 256), F.Copy)
+    pe([(blk("P2", h, 8), a("cb", 128 * h, 128 * h + 128, p=p8), a("IL", 16, 24, p=p8), True, True) for h in range(2)]
+       + [(blk("P2", 2 + h, 8), a("tf", 128 * h, 128 * h + 128, p=p8), a("I8", p=p8), True, True) for h in range(2)])
+    cp(sm(NL), a("P2", 0, 16))
+    cp(sm(TH16), a("P2", 16, 32))
+    cp(sm(BND), a("P2", 16, 32))
+    post_cut()
+    fit(range(1, 13, 2), blk("Cc", 0))
+    edges(0)
+    for r in range(RO):
+        last = r == RO - 1
+        ks = a("pm", 15, 256, 16) if r == 0 else sm(KS)
+        ts(sm(T1_), ks, M16, A.add, M16, A.subtract)
+        tt(sm(NP_), ks, sm(BND), A.is_ge)
+        tt(sm(T2_), ks, sm(T1_), A.subtract)
+        ts(sm(T3_), sm(NP_), 16.0, A.mult, -8.5, A.add)
+        tt(a("D3", 0, 256, 16), sm(T2_), sm(T3_), A.max)
+        scan(a("U3"), blk("NST", 0), a("D3"), 0.0, A.mult, A.add)
+        ts(blk("OH", 0), a("U3"), -8.5, A.is_ge)
+        ts(blk("OH", 1), a("U3"), -6.5, A.is_ge)
+        pe([(blk("P2", h, 128), blk("OH", 2 * z + h, 128), a("nIb") if z else I_, z == 0, z == 1) for h in range(2) for z in range(2)])
+        tt(a("Ye"), a("P2", 0, 256), a("Wn"), A.mult)
+        pe(tolist(272, 2, "Ye") + tolist(256, 1, "Ye"))
+        ts(a("ab"), a("P2", 256, 288), float(CEN), A.add)
+        ts(a("abf"), a("P2", 256, 288), float(CEN), A.add)
+        if r > 0:
+            tt(sm(C1), sm(NS), sm(GO2), A.add)
+            tt(sm(MM_), sm(C1), sm(PRE), A.max)
+            tt(sm(C3), sm(QQ), sm(GO2), A.is_lt)
+            for j in range(3):
+                tt(blk("Q", j, 16), blk("si", j + 1, 16), sm(C3), A.mult)
+            ts(blk("Q", 3, 16), sm(MM_), 0.0, A.is_equal)
+            pe([(a("P0", 368 + 8 * h, 376 + 8 * h), blk("Wn", h, 128), a("B2", 16, 24), True, True) for h in range(2)])
+            ts(sm(C5), a("P0", 368, 384), float(V - ST - CEN), A.is_ge)
+            tt(blk("Q", 4, 16), sm(C5), blk("Q", 3, 16), A.mult)
+            ts(sm(NL), sm(MM_), 1.0, A.max)
+            act(blk("Q", 5, 16), sm(NL), F.Copy)
+            bcast([0, 1, 2, 3])
+            new = [(blk("P5", h, 128), a("SELN", 128 * h, 128 * h + 128, p=(0, 96)), a("QT", p=(0, 96)), False, False) for h in range(2)]
+            for j in (2, 1, 0):
+                tt(blk("TS", j), WP, blk("GB", j), A.mult)
+                pe([(WP, a("Ih"), a("Wn"), True, False)] + (new if j == 0 else [])
+                   + [(WP, blk("DS", u, 128), blk("TS", u), False, u == j) for u in range(2, j - 1, -1)])
+            OPS[-1]["prio"] = PB
+            post_cut()
+        for z in (1, 0):
+            tt(blk("RR", z), ind(a("CT"), blk("ab", z, 16)), blk("CR", z), A.add)
+            for gm in range(2):
+                if (z, gm) in LLV:
+                    ts(blk("LL", 2 * gm + z), blk("RR", z), col(MA0 + gm), A.mult, col(MB0 + gm), A.add)
+                else:
+                    act(blk("LL", 2 * gm + z), blk("RR", z), F.Identity, col(MB0 + gm), col(MA0 + gm))
+        mid, rmid = blk("mid", r), blk("rmid", r)
+        act(a("xa"), ind(OWND, blk("ab", 0, 16)), F.Identity, col(CM5))
+        tt(a("xb"), ind(PARD, blk("ab", 1, 16)), a("xa"), A.add)
+        ts(a("m2"), a("xb"), M2, A.add, M2, A.subtract)
+        act(mid, a("m2"), F.Identity, 0.0, 0.5)
+
+        def e(g, T, c, r=r, mid=mid, rmid=rmid):
+            g.remote_dma(mk(T, rmid), mk(T, mid), T.sem["am%d" % r], T.sem.ls1, c["p"]["pid"], c["p"]["rid"], c["p"]["m8"])
+            c["ls1"][0] += c["ne"]
+        s = op("G", e, [mid], [], RI, track=False)
+        op(None, None, [], [rmid], 0, tok=("am%d" % r, None), lat=RL + 1000, after=[s])
+        vb = [0, 0]
+        for g_ in range(8):
+            pp = (32 * (g_ // 2), 32 * (g_ // 2) + 32)
+            for z in range(2):
+                onv = z == 0 and g_ < VG
+                vb[onv] += 1
+                bk = "P%d" % ((3, 6)[onv] + vb[onv] % 2)
+                b = 512 * (g_ % 2) + 256 * z
+                pe([(a(bk, 0, 128), a("LL", b, b + 128, p=pp), a("RR", 256 * z, 256 * z + 128, p=pp), True, True),
+                    (a(bk, 128, 384), a("LL", b + 128, b + 256, p=pp), a("RR", 256 * z, 256 * z + 256, p=pp), True, True)])
+                for h in range(2):
+                    src = a(bk, 128 * h, 128 + 256 * h)
+                    if onv:
+                        red(sm(MA, 1, 8 * h + g_), src, A.max)
+                    else:
+                        act(blk("junk", 2 * (vb[0] % 3) + h, 256, 0, 128 + 128 * h), src, F.Relu, col(VB0 + h), 1.0, sm((MA, CB)[z], 1, 8 * h + g_))
+        tt(sm(T4_), sm(MA), a("thr"), A.add)
+        tt(sm(T5_), sm(T4_), sm(CB), A.max)
+        for h in range(2):
+            ts(a("D2", 128 * h, 128 * h + 128, 16), sm(T5_, 8, 8 * h), 0.0, A.is_gt, col(DU0 + h), A.mult)
+        scan(a("T1"), a("DA"), a("D2"), 0.0, A.mult, A.add)
+        scan(a("T2"), a("D2"), a("DB"), 0.0, A.add, A.mult)
+        pe([(a("P2", 320, 352), I_, a("negL"), True, False)]
+           + [(blk("P2", 40 + 2 * z + h, 8), blk(t, h, 128), blk("B2", s, 8), False, z + h + s == 3)
+              for z in range(2) for h in range(2) for s, t in enumerate(("T1", "T2"))])
+        tt(a("ef"), a("P2", 320, 352), a("abf"), A.max)
+        cp(blk("eff", r, 32), a("ef"))
+        ea, eb, ra, rk = blk("eff", 2 * r, 16), blk("eff", 2 * r + 1, 16), blk("rl", 2 * r, 16), blk("rl", 2 * r + 1, 16)
+
+        def e(g, T, c, r=r, ea=ea, eb=eb, ra=ra, rk=rk):
+            g.remote_dma_fused([RemoteDMATransfer(dst_ids=[DstId(rid=c[to]["rid"], pnc=c[to]["pid"])], dma_engine_mask=c[to][m],
+                                                  remote_sem=T.sem[sem % r], src=mk(T, x), dst=mk(T, y))
+                                for to, m, sem, x, y in (("p", "m4a", "aa%d", ea, ra), ("q", "m4b", "ak%d", eb, rk))], local_sem=T.sem.ls1)
+            c["ls1"][0] += c["ne"]
+        s = op("G", e, [ea, eb], [], RI, track=False)
+        op(None, None, [], [ra], 0, tok=("aa%d" % r, None), lat=RL, after=[s])
+        op(None, None, [], [rk], 0, tok=("ak%d" % r, None), lat=RL, after=[s])
+        if not last:
+            ts(a("wn"), a("ef", 0, 16), float(V), A.is_lt)
+            pe([(a("P1", 352, 368), a("ones"), a("wn"), True, True)])
+            act(a("junk", 0, 16), a("P1", 352, 368), F.Identity, 0.0, 1.0, col(AC))
+            cp(a("pi", 0, 1), col(AC))
+            ts(a("pi", 1, 2), a("pi", 0, 1), 31, A.bitwise_and)
+            ts(col(AC), a("pi", 1, 2), 128.0, A.mult)
+            act(sm(BND), sm(TH16), F.Identity, col(AC))
+        if r > 0:
+            fit(range(1, 13, 2), blk("Cc", 0), FS)
+        cp(ind(OWND, ea), mid)
+        cp(ind(PARD, ra), rmid)
+        cp(ind(PARD, eb), a("DN"))
+        cp(ind(OWND, rk), a("DP"))
+        ts(a("xs"), ind(OWN, a("el")), 255.0, A.min)
+        if not last:
+            pe([(a("P1", 368 + 8 * h, 376 + 8 * h), blk("xs", h, 128), B1, True, True) for h in range(2)])
+            act(sm(ED_), a("P1", 368, 384), F.Relu, -4079.0 * BIG, BIG)
+        fl = blk("fl", r, 16)
+        hop(PAR, "CO", blk("Cc", 0), NV1, XV1, SB1, "Y1", fl)
+        cp(a("rs"), ind(a("CP"), fl))
+        k1 = a("pm", 15, 256, 16)
+        act(sm(H1), k1, F.Relu, -16.0 * THR, 16.0)
+        act(sm(H2), sm(NL), F.Relu, -13.0 * BIG, BIG)
+        tt(sm(PEN1), sm(H1), sm(H2), A.add)
+        if not last:
+            act(sm(H4), sm(NL), F.Identity, -8.5)
+            tt(sm(H4), sm(H4), sm(ED_), A.add)
+            tt(sm(K1), k1, sm(H4), A.add)
+        ts(a("xs"), ind(PAR, fl), 0.0, A.max)
+        if not last:
+            edges(r + 1)
+        else:
+            for i in range(NCH):
+                ts(blk("XO", i, CW), blk("X", i, CW), 255.0, A.min)
+            store(lambda T: T.yx[:, :], lambda T: T.XO[:, :], a("XO"), "ox", 5000)
+        ts(blk("Cc", 1), a("rs"), float(-CEN), A.add)
+        fit(range(0, 13, 2), blk("Cc", 1))
+        hop(OWN, "rs", blk("Cc", 1), NV2, XV2, SB2, "Y2", None)
+        tt(sm(TT_), a("pm", 15, 256, 16), sm(PEN1), A.add)
+        ts(sm(GO2), sm(TT_), THR, A.is_lt, 2.0, A.mult)
+        if not last:
+            ts(sm(UU), sm(TT_), -65536.0, A.add, 4.0, A.mult)
+            ts(sm(GB_), sm(TT_), THR, A.is_lt, BIG, A.mult)
+            tt(sm(U1), sm(TT_), sm(C2), A.add)
+            tt(sm(U2), sm(UU), sm(KEYX), A.max)
+            tt(sm(U4), sm(GB_), sm(KEY0), A.add)
+            tt(sm(U1), sm(U1), sm(U2), A.min)
+            tt(sm(KS), sm(U1), sm(U4), A.min)
+        pe([(a("P7", 0, 256), blk("Bo", 0, 128), a("Y1"), True, False), (a("P7", 0, 256), blk("Bo", 1, 128), a("Y2"), False, True)])
+        tt(a("TT"), a("P7", 0, 256), a("Mn"), A.mult)
+        pe([(WP, a("Ih"), a("Wz"), True, False), (WP, a("Ih"), a("TT"), False, True)])
+        if not last:
+            cp(a("Wn"), WP)
+    tt(blk("Q", 5, 16), sm(NL), sm(GO2), A.add)
+    bcast([3])
+    act(a("yc"), blk("GB", 3), F.Copy)
+    ts(a("Me"), blk("GB", 3), col(KC), A.is_gt)
+    act(a("yq"), WP, F.Identity, float(CEN))
+    tt(a("yo"), a("yq"), a("Me"), A.mult)
+    store(lambda T: T.yw[:, :], lambda T: T.yo[:, :], a("yo"), "ow", 2500)
+    store(lambda T: T.yn[:, :], lambda T: T.yc[0:128:16, :], a("yc"), "on", 2500)
+
+
+def plan():
+    program()
+    last_w, last_r = {}, {}
+    bank = lambda q: SCRATCH[q[0]][0] == "psum"
+    for o in OPS:
+        raw, oth = set(), set()
+        for q in o["r"]:
+            raw.update(d for (c0, c1, d) in last_w.get(q[0], []) if bank(q) or (c0 < q[2] and q[1] < c1))
+            if bank(q):
+                oth.update(d for (c0, c1, d) in last_r.get(q[0], []) if OPS[d]["eng"] != o["eng"])
+        for q in o["w"]:
+            oth.update(d for (c0, c1, d) in last_w.get(q[0], []) + last_r.get(q[0], []) if bank(q) or (c0 < q[2] and q[1] < c1))
+        for q in o["w"]:
+            keep = lambda t: not (bank(q) or (q[1] <= t[0] and t[1] <= q[2]))
+            last_w[q[0]] = [t for t in last_w.get(q[0], []) if keep(t)]
+            last_r[q[0]] = [t for t in last_r.get(q[0], []) if keep(t)]
+        for q in o["w"]:
+            last_w[q[0]].append((q[1], q[2], o["n"]))
+        if o["track"]:
+            for q in o["r"]:
+                last_r.setdefault(q[0], []).append((q[1], q[2], o["n"]))
+        if o["eng"] is None:
+            raw, oth = set(), set()
+        o["deps"] = (raw | oth | set(x["n"] for x in o["after"])) - {o["n"]}
+        o["wait"] = set(d for d in o["deps"] if not (OPS[d]["eng"] == o["eng"] and o["eng"] in "PG"))
+    N = len(OPS)
+    eng = [o["eng"] for o in OPS]
+    cost = [o["cost"] for o in OPS]
+    tail = [o["cost"] + o["lat"] for o in OPS]
+    dl = [[(d, tail[d] + SL if d in o["wait"] else cost[d]) for d in sorted(o["deps"])] for o in OPS]
+    pr = list(tail)
+    for n in range(N - 1, -1, -1):
+        pr[n] += OPS[n].get("prio", 0.0)
+        for d, w in dl[n]:
+            pr[d] = max(pr[d], pr[n] + w + 1.0)
+
+    def place(pr):
+        slots = {e: [] for e in "VSPGY"}
+        beg, rdy = [0.0] * N, [0.0] * N
+        for n in sorted(range(N), key=lambda n: (-pr[n], n)):
+            t = max([beg[d] + w for d, w in dl[n]] + [0.0])
+            rdy[n] = t
+            if eng[n] is not None:
+                sl = slots[eng[n]]
+                i = len(sl)
+                while i > 0 and sl[i - 1][1] > t:
+                    i -= 1
+                while i < len(sl) and sl[i][0] < t + cost[n]:
+                    t = max(t, sl[i][1])
+                    i += 1
+                sl.insert(i, (t, t + cost[n], n))
+            beg[n] = t
+        return max(beg[n] + tail[n] for n in range(N)), slots, beg, rdy
+
+    rs = np.random.RandomState(SEED)
+    cur = best = place(pr)
+    for it in range(TRIES):
+        fin, slots, beg, rdy = cur
+        prev = {sl[i][2]: sl[i - 1][2] for sl in slots.values() for i in range(1, len(sl))}
+        n = max(range(N), key=lambda n: beg[n] + tail[n])
+        held = []
+        while beg[n] > 0:
+            if beg[n] > rdy[n] + 1.0:
+                if pr[prev[n]] > pr[n]:
+                    held.append((n, beg[n] - rdy[n]))
+                n = prev[n]
+            else:
+                n = max(dl[n], key=lambda x: beg[x[0]] + x[1])[0]
+        if not held:
+            break
+        p2 = list(pr)
+        for j in range(int(rs.randint(1, 4))):
+            n, w = held[int(rs.randint(len(held)))]
+            p2[n] = max(p2[n] + w * float(rs.rand()), pr[prev[n]] + 1.0)
+        for n in range(N - 1, -1, -1):
+            for d, w in dl[n]:
+                if p2[d] <= p2[n]:
+                    p2[d] = p2[n] + 1.0
+        t2 = place(p2)
+        if t2[0] <= fin + 400.0 * (1.0 - it / TRIES) * float(rs.rand()):
+            cur, pr = t2, p2
+            if t2[0] < best[0]:
+                best = t2
+    for o in OPS:
+        o["t"] = best[2][o["n"]]
+    order = {e: [x[2] for x in best[1][e]] for e in best[1]}
+    pos = {n: i for e in order for i, n in enumerate(order[e])}
+    need = set()
+    for e in order:
+        seen = {}
+        for n in order[e]:
+            o = OPS[n]
+            o["toks"] = [d for d in o["wait"] if OPS[d]["tok"]]
+            far = {}
+            for d in o["wait"]:
+                de = OPS[d]["eng"]
+                if OPS[d]["tok"] is None and pos[d] > seen.get(de, -1) and pos[d] > far.get(de, (-1, 0))[0]:
+                    far[de] = (pos[d], d)
+            o["cw"] = [d for (p_, d) in far.values()]
+            for de in far:
+                seen[de] = far[de][0]
+            need.update(o["cw"])
+    total = {}
+    for e in order:
+        total[e] = 0
+        for n in order[e]:
+            if n in need:
+                total[e] += 1
+                OPS[n]["inc"] = total[e]
+    return order, total, best[0]
+
+
+ORDER, TOTAL, EST = plan()
+
+
+def bits(es):
+    return sum(1 << x for x in es)
+
+
+def helper_of(topo, cores, c):
+    mine = [x for x in cores if topo.chip(x) == topo.chip(c)]
+    free = [x for x in topo.cores_of(c) if x not in cores and topo.die(x) != topo.die(c)]
+    return free[mine.index(c)]
+
+
+def rank_program(g, core, T, topo):
+    cores = list(T.cores)
+    n = len(cores)
+    rank = T.rank_of(core)
+    far = lambda r: topo.chip(cores[r]) != topo.chip(cores[(r - SH) % n])
+    via = [i for i in range(NCH) if i % 2 == 0]
+    spare = lambda c, h, d: [x for x in topo.engines(c, h) if x not in topo.engines(c, d)]
+    if rank is None:
+        for r in range(n):
+            if far(r) and topo.chip(cores[r]) == topo.chip(core) and helper_of(topo, cores, cores[r]) == core:
+                d = cores[(r - SH) % n]
+                for nm, sem, src, dst, off in (("hx", "xarr", T.X, T.X, VP), ("hc", None, T.CU, T.CQ, 0)):
+                    for i in via:
+                        g.wait_ge(T.sem["%s%d" % (nm, i)], len(spare(cores[r], core, d)))
+                        g.remote_dma(dst[:, off + CW * i:off + CW * i + CW], src[:, CW * i:CW * i + CW], T.sem[sem or "ca%d" % i], T.sem.ls0,
+                                     topo.addr(d)[1], topo.addr(d)[0], topo.mask(core, d))
+                g.wait_ge(T.sem.ls0, 2 * len(via) * len(topo.engines(core, d)))
+        return
+    p, q = cores[(rank - SH) % n], cores[(rank + SH) % n]
+    off = [x for x in cores if topo.chip(x) != topo.chip(core)][0]
+    es = topo.engines(core, off)
+    h = len(es) // 2
+    c = {"ls1": [0], "ne": len(es)}
+    for nm, d in (("p", p), ("q", q)):
+        c[nm] = {"rid": topo.addr(d)[0], "pid": topo.addr(d)[1], "m8": bits(es), "m4a": bits(es[:h]), "m4b": bits(es[h:])}
+    sent = [0]
+
+    def big(what, i):
+        cs = slice(CW * i, CW * i + CW)
+        src, ls, num = (T.X, T.sem.ls0, sent) if what == "X" else (T.CU, T.sem.ls1, c["ls1"])
+        if far(rank) and i in via:
+            hc = helper_of(topo, cores, core)
+            m = spare(core, hc, p)
+            g.remote_dma(src[:, cs], src[:, cs], T.sem[("hx%d" if what == "X" else "hc%d") % i], ls, topo.addr(hc)[1], topo.addr(hc)[0], bits(m))
+        else:
+            m = topo.engines(core, p)
+            dst, sem = (T.X[:, VP + CW * i:VP + CW * i + CW], T.sem.xarr) if what == "X" else (T.CQ[:, cs], T.sem["ca%d" % i])
+            g.remote_dma(dst, src[:, cs], sem, ls, c["p"]["pid"], c["p"]["rid"], bits(m))
+        num[0] += len(m)
+    c["big"] = big
+    vals = {"xarr": len(topo.engines(q, core)) * NCH}
+    for i in range(NCH):
+        vals["ca%d" % i] = len(topo.engines(q, core))
+    for r in range(RO):
+        vals["am%d" % r], vals["aa%d" % r], vals["ak%d" % r] = len(es), h, len(es) - h
+    qs = {"V": g.vector, "S": g.scalar, "P": g.tensor, "G": g, "Y": g.sync}
+    for e in "GYSPV":
+        got = set()
+        vals["ls0"] = sent[0]
+        for k in ORDER[e]:
+            o = OPS[k]
+            for d in o["toks"]:
+                s, v = OPS[d]["tok"]
+                if s not in got:
+                    got.add(s)
+                    qs[e].wait_ge(T.sem[s], vals[s] if v is None else v)
+            for d in o["cw"]:
+                qs[e].wait_ge(T.sem["s" + OPS[d]["eng"]], OPS[d]["inc"])
+            r = o["emit"](g, T, c)
+            if "inc" in o:
+                r.then_inc(T.sem["s" + e], 1)
+    for e in "VSPG":
+        if TOTAL[e]:
+            g.wait_ge(T.sem["s" + e], TOTAL[e])
+    g.wait_ge(T.sem.ls1, c["ls1"][0])
+    for s in ("ox", "ow", "on"):
+        g.wait_ge(T.sem[s], 16)

@@ -18,9 +18,12 @@ SB1, SB2, SB3 = "347", "34", "346"
 VG = 7
 FS = 4
 PB = 3000.0
-SEED, TRIES = 0, 2500
+SEED, TRIES = 2, 7000
 LLV = [(0, 0), (0, 1), (1, 0)]
-EV = ["VSVVVSVV", "VSVSVSVS", "VSVSVSVS", "VSVSVSVS"]
+EV = ["SSSSVSVS", "SSVSSVVV", "SSVSSVVV", "SSVSSVVV"]
+VB = ["342", "67"]
+TURN = 8
+SIM = 64
 NCH = 4
 CW = V // NCH
 
@@ -30,13 +33,13 @@ for _d, _l in (
                       ("nIb", 128), ("PENI", 128), ("Bx", 128), ("nB16", 128), ("BB", 64), ("NST", 768), ("KI", 512), ("KH", 256), ("DP", 256),
                       ("DN", 256), ("negL", 32), ("SELN", 256), ("cb", 256), ("GB", 1024), ("Q", 96), ("QT", 128), ("Me", 256), ("Mf", 256),
                       ("Mn", 256), ("Mz", 256), ("xs", 256), ("EQ", 7 * 256), ("OH", 512), ("D1", 768), ("U", 768), ("PN", 768), ("D3", 256),
-                      ("U3", 256), ("RR", 512), ("LL", 1024), ("junk", 1536), ("m2", 256), ("mid", 1024), ("rmid", 1024), ("Lo", 64),
+                      ("U3", 256), ("RR", 512), ("LL", 1024), ("junk", 1536), ("m2", 256), ("mid", 1024), ("rmid", 1024), ("Lo", 256),
                       ("cm", 128), ("ones", 128), ("wn", 16))),
         ("float16", (("Ih", 128), ("nIh", 128), ("SEL", 13 * 128), ("LB", 3 * 144), ("DS", 3 * 128), ("Bo", 256), ("B2", 24), ("DA", 256), ("DB", 256), ("Wa", 256),
-                     ("Wn", 256), ("Wz", 256), ("Wf", 256), ("TT", 256), ("TS", 768), ("Y1", 256), ("Y2", 256), ("Ye", 256), ("Yl", 256), ("Cc", 512),
+                     ("Wn", 256), ("Wz", 256), ("Wf", 256), ("TT", 256), ("TS", 768), ("PZ", 512), ("Y1", 256), ("Y2", 256), ("Ye", 256), ("Yl", 256), ("Cc", 512),
                      ("D2", 256), ("T1", 256), ("T2", 256))),
-        ("float32", (("Li", 256), ("RST", 512), ("CR", 512), ("KM", 16), ("col", 32), ("thr", 16), ("tf", 256), ("I8", 8), ("pm", 512), ("pe", 512),
-                     ("km", 256), ("sm", 1024), ("xa", 256), ("xb", 256), ("abf", 32), ("ef", 32), ("Hi", 64), ("tq", 256), ("yo", 256),
+        ("float32", (("Li", 256), ("RST", 512), ("CR", 512), ("KM", 16), ("col", 32), ("thr", 16), ("tf", 256), ("I32", 128), ("pm", 512), ("pe", 512),
+                     ("km", 256), ("sm", 1024), ("xa", 256), ("xb", 256), ("abf", 32), ("ef", 32), ("Hi", 16), ("tq", 256), ("yo", 256),
                      ("yq", 256), ("yc", 256))),
         ("int32", (("CA", V), ("CP", V), ("si", 64), ("wi", 256), ("ci", 256), ("ti", 256), ("pi", 4))),
         ("uint16", (("WO", 256), ("CO", 256), ("el", 16), ("fl", 64), ("rs", 256), ("CU", V), ("CQ", V), ("ab", 32), ("eff", 128), ("rl", 128)))):
@@ -116,7 +119,7 @@ def mk(T, x):
 
 
 OPS = []
-CY, GA, SCA, PEC, VF, SF, SL, RI, RL = 1.04, 1.56, 3.8, 0.52, 30.0, 60.0, 120.0, 700.0, 2500.0
+CY, GA, SCA, PEC, VF, SF, SL, RI, RL = 0.9, 1.56, 3.8, 0.46, 30.0, 50.0, 120.0, 700.0, 2500.0
 
 
 def op(eng, emit, rd, wr, cost, tok=None, lat=0.0, track=True, after=()):
@@ -224,7 +227,7 @@ def blk(name, i, w=256, o=0, n=None):
 
 I_ = a("IL", 16, 144)
 B32, Bm16, B16, Bm1, B1 = [a("BB", 8 * i, 8 * i + 8) for i in range(5)]
-(KC, KC1, KK, OFF, M15, IS15, MG0, MG1, VB0, VB1, DU0, DU1, SC, MLO, MHI, M12, EVN, ODD, PF, R0, AC, CM5, MA0, MA1, MB0, MB1, KF) = range(27)
+(KC, KC1, KK, OFF, M15, IS15, MG0, MG1, VB0, VB1, DU0, DU1, SC, MLO, MHI, M12, EVN, ODD, PF, R0, AC, CM5, MA0, MA1, MB0, MB1, KF, N12, N128) = range(29)
 (NL, BND, TH16, JJ, CUT, T0, FL, S_, CE, PRE, QQ, NS, KEY0, KEYX, C2, K1, PEN1, TT_, UU, GB_, GO2, KS, T1_, T2_, T3_, NP_, MA, CB,
  T4_, T5_, MM_, ED_, H1, H2, H4, E1, E2, E3, E4, E5, E6, C1, C3, C5, W0, W1, W2, W3, KF_, KB_, U1, U2, U4) = range(53)
 OWN, PAR, OWND, PARD = a("X", 0, V), a("X", VP, VP + V), a("X", 0, VP), a("X", VP, 2 * VP)
@@ -260,16 +263,15 @@ def consts():
     ts(col(KC1), col(KC), 1.0, A.add)
     ts(col(IS15), col(KC), 15.0, A.is_equal)
     ts(col(M15), col(KC), 15.0, A.not_equal)
-    ts(col(OFF), col(ODD), float(VP), A.mult, float(CEN), A.add)
     ts(col(EVN), col(ODD), -1.0, A.mult, 1.0, A.add)
     ts(col(KK), col(KC), col(EVN), A.subtract, col(M15), A.mult)
     ts(col(EVN), col(EVN), col(IS15), A.add)
-    ts(col(VB0), col(PF), 1.0 / 128, A.mult, -12.0, A.add)
-    ts(col(VB1), col(PF), 1.0 / 128, A.mult, -11.0, A.add)
-    ts(col(DU0), col(PF), float(CEN), A.add)
-    ts(col(DU1), col(PF), float(CEN + 128), A.add)
+    act(col(VB0), col(PF), F.Identity, -12.0, 1.0 / 128)
+    act(col(VB1), col(PF), F.Identity, -11.0, 1.0 / 128)
+    act(col(DU0), col(PF), F.Identity, float(CEN))
+    act(col(DU1), col(PF), F.Identity, float(CEN + 128))
     ts(col(R0), col(KC), 0.0, A.is_equal)
-    ts(col(MLO), col(KC), 6.0, A.is_lt)
+    ts(col(MLO), col(KC), 8.0, A.is_lt)
     ts(col(M12), col(KC), 12.0, A.is_equal)
     ts(col(MHI), col(KC), 12.0, A.is_lt, col(MLO), A.subtract)
     ms(col(CM5), -0.5)
@@ -277,19 +279,22 @@ def consts():
     for gm in range(2):
         tt(col(MB0 + gm), col(MG0 + gm), col(M12), A.mult)
         tt(col(MA0 + gm), col(MG0 + gm), col(MB0 + gm), A.subtract)
+    act(col(N12), col(M12), F.Identity, 0.0, -1.0)
+    act(col(N128), col(M12), F.Identity, 0.0, -1.0 / 128)
     ts(a("IL"), a("IL"), 0.0, A.is_equal)
-    cp(blk("K16", 1), blk("K16", 0))
-    cp(blk("K16", 2), blk("K16", 0))
-    ts(a("nIb"), I_, -1.0, A.mult)
-    ts(a("PENI"), I_, PEN, A.mult)
+    act(blk("K16", 1), blk("K16", 0), F.Copy)
+    act(blk("K16", 2), blk("K16", 0), F.Copy)
+    act(a("nIb"), I_, F.Identity, 0.0, -1.0)
+    act(a("PENI"), I_, F.Identity, 0.0, PEN)
     cp(a("Ih"), I_)
     cp(a("nIh"), a("nIb"))
-    cp(a("I8"), a("IL", 16, 24))
+    act(a("I32"), I_, F.Copy)
     pe([(a("P2", 0, 128), a("L2", 0, 128, p=(0, 8)), a("L2", 0, 128, p=(0, 8)), True, True)])
     cp(a("Bx"), a("P2", 0, 128))
-    ts(a("nB16"), a("Bx"), -16.0, A.mult)
-    for x, v in ((B32, 32.0), (Bm16, -16.0), (Bm1, -1.0), (B1, 1.0), (a("BB", 48, 56), 16.0), (a("BB", 56, 64), 16.0),
-                 (a("B2", 0, 8), 2.0), (a("B2", 8, 16), -2.0), (a("B2", 16, 24), col(R0))):
+    act(a("nB16"), a("Bx"), F.Identity, 0.0, -16.0)
+    for x, v in ((B32, 32.0), (Bm16, -16.0), (Bm1, -1.0), (B1, 1.0), (a("BB", 48, 56), 16.0), (a("BB", 56, 64), 16.0)):
+        act(x, a("Bx", 0, 128, 16), F.Identity, 0.0, v)
+    for x, v in ((a("B2", 0, 8), 2.0), (a("B2", 8, 16), -2.0), (a("B2", 16, 24), col(R0))):
         ts(x, a("Bx", 0, 128, 16), v, A.mult)
     ts(a("KM"), a("K16", 0, 16), col(KC), A.is_equal)
     for k in range(13):
@@ -299,6 +304,10 @@ def consts():
     cp(a("LB", 15, 143, 16), B1)
     ts(a("LB", 144 + 15, 144 + 143, 16), B1, col(EVN), A.mult)
     ts(a("LB", 288 + 15, 288 + 143, 16), B1, col(ODD), A.mult)
+    for z in range(2):
+        for u in range(2):
+            iota(blk("LL", 2 * z + u, 128), [[16, 8], [200, 2], [2, 8]], z - 200 * u, -1)
+    ts(a("PZ"), a("LL", 0, 512), 0.0, A.is_equal)
     ms(a("Bo"), 0.0)
     cp(a("Bo", 1, 128, 2), a("Bx", 1, 128, 2))
     cp(a("Bo", 128, 256, 2), a("Bx", 0, 128, 2))
@@ -307,37 +316,43 @@ def consts():
         tt(d, a("IL", 16 + s, 144 + s), I_, A.subtract)
         ts(a("cm"), a("K16", 0, 128), 14.0 - s, A.is_le)
         tt(d, d, a("cm"), A.mult)
-    ts(a("RST"), a("K16", 0, 512), 0.0, A.is_equal, 16 * BIG, A.mult)
-    ts(a("NST"), a("K16"), 0.0, A.not_equal)
-    ts(a("KI"), a("K16", 0, 512), -7.5, A.add)
-    ts(a("KH"), blk("K16", 0), 1.0 / 16, A.mult)
+    act(a("RST"), a("K16", 0, 512), F.Relu, 16 * BIG, -16 * BIG)
+    act(a("NST"), a("K16"), F.Sign)
+    act(a("KI"), a("K16", 0, 512), F.Identity, -7.5)
+    act(a("KH"), blk("K16", 0), F.Identity, 0.0, 1.0 / 16)
     ts(a("DB"), blk("K16", 0), col(KC), A.is_lt)
     ts(a("DA"), blk("K16", 0), col(KC), A.is_le)
     ms(a("DA", 0, 256, 16), 0.0)
-    for x, v in ((a("DP"), 1024.0), (a("DN"), -1024.0), (a("X", V, VP), 0.0), (a("X", VP + V, 2 * VP), 0.0), (a("CT", V, VP), 0.0), (a("D1"), -1.0),
-                 (a("D3"), -1.0), (a("D2"), 0.0), (a("Q"), 0.0), (a("ones"), 1.0), (a("SELN"), 0.0), (sm(T2_), 0.5), (sm(T3_), 0.0)):
+    for x, v in ((a("X", V, VP), 0.0), (a("X", VP + V, 2 * VP), 0.0), (a("D2"), 0.0), (sm(U1), 0.5), (sm(U2), 0.0)):
         ms(x, v)
+    for x, v in ((a("DP"), 1024.0), (a("DN"), -1024.0), (a("CT", V, VP), 0.0), (a("D1"), -1.0), (a("D3"), -1.0), (a("Q"), 0.0), (a("ones"), 1.0),
+                 (a("SELN"), 0.0)):
+        act(x, a("K16", 0, cnt(x)), F.Identity, v, 0.0)
     for h in range(2):
         ts(blk("negL", h, 16), a("Li", 0, 256, 16), col(KC), A.add, -1.0, A.mult)
         ts(blk("thr", h, 8), a("K16", 0, 8), VG - 0.5, A.is_lt, col(VB0 + h), A.mult)
-        ts(blk("CR", h), a("Li"), 128.0, A.add, col(M12), A.mult)
+        act(blk("CR", h), a("Li"), F.Identity, col(N12), col(N128))
         b1, b2 = 16 * (48 + 8 * h), 16 * (64 + 8 * h)
-        ts(sm(T0, 8), a("L2", b1, b1 + 128, 16), float(ST), A.mult)
-        ts(sm(T1_, 8), a("L2", b2, b2 + 128, 16), float(-V), A.mult)
-        tt(a("SELN", 128 * h, 128 * h + 128, 16), sm(T0, 8), sm(T1_, 8), A.add)
-    act(a("CR"), a("CR"), F.Identity, 0.0, -1.0 / 128)
-    scan(sm(T4_, 6), sm(T2_, 6), sm(T3_, 6), 1.0, A.mult, A.add)
-    cp(sm(T4_, 6, 6), sm(T4_, 6))
+        act(sm(H1, 8, 8 * h), a("L2", b1, b1 + 128, 16), F.Identity, 0.0, float(ST))
+        act(sm(H2, 8, 8 * h), a("L2", b2, b2 + 128, 16), F.Identity, 0.0, float(-V))
+        tt(a("SELN", 128 * h, 128 * h + 128, 16), sm(H1, 8, 8 * h), sm(H2, 8, 8 * h), A.add)
+    scan(sm(T4_, 8), sm(U1, 8), sm(U2, 8), 1.0, A.mult, A.add)
+    cp(sm(T4_, 4, 8), sm(T4_, 4))
     tt(sm(T5_, 12), sm(T4_, 12), a("KM", 0, 12), A.mult)
     red(col(SC), sm(T5_, 12), A.add)
-    ts(blk("tq", 0, 64), a("Li", 0, 64), 0.5, A.add, col(SC), A.mult)
-    ts(blk("tq", 1, 64), blk("tq", 0, 64), M1, A.add, M1, A.subtract)
-    tt(blk("tq", 2, 64), blk("tq", 0, 64), blk("tq", 1, 64), A.is_gt)
-    ts(blk("tq", 3, 64), blk("tq", 2, 64), 2.0, A.mult, -1.0, A.add)
-    ts(a("Lo"), blk("tq", 3, 64), col(MLO), A.mult, col(M12), A.add)
-    ts(a("Hi"), blk("tq", 3, 64), col(MHI), A.mult)
-    for c in range(V // 64):
-        act(blk("CT", c, 64), a("Lo"), F.Identity, a("Hi", c, c + 1))
+    ts(a("tq"), a("Li"), 0.5, A.add, col(SC), A.mult)
+    ts(a("xa"), a("tq"), M1, A.add, M1, A.subtract)
+    act(a("xb"), a("xa"), F.Identity, 0.0, -1.0)
+    pe([(a("P3", 0, 256), a("I32"), a("tq"), True, False), (a("P3", 0, 256), a("I32"), a("xb"), False, True)])
+    act(a("m2"), a("P3", 0, 256), F.Sign)
+    act(a("Lo"), a("m2"), F.Identity, col(M12), col(MLO))
+    act(a("Hi"), a("m2", 0, 16), F.Identity, 0.0, col(MHI))
+    for c in range(V // 256):
+        if c % 2:
+            act(blk("CT", c), a("Lo"), F.Identity, a("Hi", c, c + 1))
+        else:
+            ts(blk("CT", c), a("Lo"), a("Hi", c, c + 1), A.add)
+        OPS[-1]["prio"] = 4000.0
 
 
 def post_cut():
@@ -353,7 +368,9 @@ def post_cut():
     ts(a("Mn"), nG, col(KK), A.is_equal)
     act(a("Mz"), a("Mn"), F.Identity, 1.0, -1.0)
     tt(a("Wz"), WP, a("Mz"), A.mult)
-    ts(a("WO"), WP, col(OFF), A.add)
+    for z in range(2):
+        pe([(blk("P1", 1 + z, 128), blk("PZ", 2 * z + u, 128), a("Wz", u, 256, 2), u == 0, u == 1) for u in range(2)])
+    ts(a("WO"), a("P1", 128, 384), float(CEN), A.add)
 
 
 def fit(rows, cc, ns=0):
@@ -416,8 +433,8 @@ def hop(win, co, cc, nv, xv, sb, y, lout):
 
 def edges(r):
     for j, l0 in enumerate(range(0, 256, GC)):
-        gather(EV[r][j], a("VV", 16 * l0, 16 * (l0 + GC)), ind(a("X"), a("WO", l0, l0 + GC)))
-    row = lambda h, k: a("VV", 2048 * h + k, 2048 * h + 2048, 16)
+        gather(EV[r][j], a("VV", 16 * l0, 16 * (l0 + GC)), ind(OWND if l0 < 128 else PARD, a("WO", l0, l0 + GC)))
+    row = lambda h, k: a("VV", 2048 * (k & 1) + 1024 * h + k // 2, 2048 * (k & 1) + 1024 * h + 1024, 8)
     if r > 0:
         pe([(a("P7", 0, 256), I_, blk("KI", 0), True, False)]
            + [(a("P7", 128 * h + k, 128 * h + 128, 16), row(h, k), B1 if k & 1 else Bm1, False, h == 1 and k == 14) for h in range(2) for k in range(15)])
@@ -499,18 +516,18 @@ def program():
     load("S", a("wi"), lambda T: T.way[:, :], "lw", 2200)
     load("S", a("ci", p=(0, 8)), lambda T: T.cnt[:, :], "lc", 2200)
     load("S", a("ti", p=(0, 8)), lambda T: T.th[:, :], "lt", 2200)
-    for i in range(NCH):
-        load("Y", blk("CA", i, CW), (lambda i: lambda T: T.cand[:, CW * i:CW * i + CW])(i), "lk%d" % i, 4000 + 800 * i)
     ss = []
     for i in range(NCH):
         ss.append(op("G", (lambda i: lambda g, T, c: c["big"]("X", i))(i), [blk("X", i, CW)], [], 1500 if i == 0 else RI, track=False))
         ss[-1]["prio"] = 1e9
-    op(None, None, [OWN], [], 0, tok=("ls0", None), lat=9000, after=ss)
-    op(None, None, [], [PAR], 0, tok=("xarr", None), lat=12000, after=ss)
+    left = op(None, None, [OWN], [], 0, tok=("ls0", None), lat=5000, after=ss)
+    for i in range(NCH):
+        load("Y", blk("CA", i, CW), (lambda i: lambda T: T.cand[:, CW * i:CW * i + CW])(i), "lk%d" % i, 3000 + 1500 * i)["after"].append(left)
+    op(None, None, [], [PAR], 0, tok=("xarr", None), lat=8000, after=ss)
     for i in range(NCH):
         cp(blk("CU", i, CW), blk("CA", i, CW))
         sc = op("G", (lambda i: lambda g, T, c: c["big"]("C", i))(i), [blk("CU", i, CW), PAR], [], RI, track=False, after=ss)
-        op(None, None, [], [blk("CQ", i, CW)], 0, tok=("ca%d" % i, None), lat=7000 + 2000 * i, after=[sc])
+        op(None, None, [], [blk("CQ", i, CW)], 0, tok=("ca%d" % i, None), lat=13000 + 1000 * i, after=[sc])
         for j in range(2):
             cp(blk("CP", 2 * i + j, CW // 2), blk("CQ", 2 * i + j, CW // 2))
     consts()
@@ -524,12 +541,11 @@ def program():
     pe([(a("P0", 0, 256), a("L2", 0, 128, p=p8), a("cb", p=p8), True, True)])
     act(blk("GB", 3), a("P0", 0, 256), F.Copy)
     pe([(blk("P2", h, 8), a("cb", 128 * h, 128 * h + 128, p=p8), a("IL", 16, 24, p=p8), True, True) for h in range(2)]
-       + [(blk("P2", 2 + h, 8), a("tf", 128 * h, 128 * h + 128, p=p8), a("I8", p=p8), True, True) for h in range(2)])
+       + [(blk("P2", 2 + h, 8), a("tf", 128 * h, 128 * h + 128, p=p8), a("I32", 0, 8, p=p8), True, True) for h in range(2)])
     cp(sm(NL), a("P2", 0, 16))
     cp(sm(TH16), a("P2", 16, 32))
     cp(sm(BND), a("P2", 16, 32))
     post_cut()
-    fit(range(1, 13, 2), blk("Cc", 0))
     edges(0)
     for r in range(RO):
         last = r == RO - 1
@@ -544,9 +560,10 @@ def program():
         ts(blk("OH", 1), a("U3"), -6.5, A.is_ge)
         pe([(blk("P2", h, 128), blk("OH", 2 * z + h, 128), a("nIb") if z else I_, z == 0, z == 1) for h in range(2) for z in range(2)])
         tt(a("Ye"), a("P2", 0, 256), a("Wn"), A.mult)
-        pe(tolist(272, 2, "Ye") + tolist(256, 1, "Ye"))
-        ts(a("ab"), a("P2", 256, 288), float(CEN), A.add)
-        ts(a("abf"), a("P2", 256, 288), float(CEN), A.add)
+        for z, bk in ((1, "P3"), (0, "P6")):
+            pe(tolist(0, 1 + z, "Ye", bk))
+            ts(blk("ab", z, 16), a(bk, 0, 16), float(CEN), A.add)
+        cp(a("abf"), a("ab"))
         if r > 0:
             tt(sm(C1), sm(NS), sm(GO2), A.add)
             tt(sm(MM_), sm(C1), sm(PRE), A.max)
@@ -584,14 +601,15 @@ def program():
             g.remote_dma(mk(T, rmid), mk(T, mid), T.sem["am%d" % r], T.sem.ls1, c["p"]["pid"], c["p"]["rid"], c["p"]["m8"])
             c["ls1"][0] += c["ne"]
         s = op("G", e, [mid], [], RI, track=False)
-        op(None, None, [], [rmid], 0, tok=("am%d" % r, None), lat=RL + 1000, after=[s])
+        s["prio"] = 1500.0
+        op(None, None, [], [rmid], 0, tok=("am%d" % r, None), lat=RL + 2000, after=[s])
         vb = [0, 0]
         for g_ in range(8):
             pp = (32 * (g_ // 2), 32 * (g_ // 2) + 32)
             for z in range(2):
                 onv = z == 0 and g_ < VG
                 vb[onv] += 1
-                bk = "P%d" % ((3, 6)[onv] + vb[onv] % 2)
+                bk = "P" + (VB[onv][vb[onv] % len(VB[onv])])
                 b = 512 * (g_ % 2) + 256 * z
                 pe([(a(bk, 0, 128), a("LL", b, b + 128, p=pp), a("RR", 256 * z, 256 * z + 128, p=pp), True, True),
                     (a(bk, 128, 384), a("LL", b + 128, b + 256, p=pp), a("RR", 256 * z, 256 * z + 256, p=pp), True, True)])
@@ -630,8 +648,7 @@ def program():
             ts(a("pi", 1, 2), a("pi", 0, 1), 31, A.bitwise_and)
             ts(col(AC), a("pi", 1, 2), 128.0, A.mult)
             act(sm(BND), sm(TH16), F.Identity, col(AC))
-        if r > 0:
-            fit(range(1, 13, 2), blk("Cc", 0), FS)
+        fit(range(1, 13, 2), blk("Cc", 0), FS)
         cp(ind(OWND, ea), mid)
         cp(ind(PARD, ra), rmid)
         cp(ind(PARD, eb), a("DN"))
@@ -657,7 +674,7 @@ def program():
         else:
             for i in range(NCH):
                 ts(blk("XO", i, CW), blk("X", i, CW), 255.0, A.min)
-            store(lambda T: T.yx[:, :], lambda T: T.XO[:, :], a("XO"), "ox", 5000)
+            store(lambda T: T.yx[:, :], lambda T: T.XO[:, :], a("XO"), "ox", 9000)
         ts(blk("Cc", 1), a("rs"), float(-CEN), A.add)
         fit(range(0, 13, 2), blk("Cc", 1))
         hop(OWN, "rs", blk("Cc", 1), NV2, XV2, SB2, "Y2", None)
@@ -710,6 +727,7 @@ def plan():
         if o["eng"] is None:
             raw, oth = set(), set()
         o["deps"] = (raw | oth | set(x["n"] for x in o["after"])) - {o["n"]}
+        o["know"] = {}
         o["wait"] = set(d for d in o["deps"] if not (OPS[d]["eng"] == o["eng"] and o["eng"] in "PG"))
     N = len(OPS)
     eng = [o["eng"] for o in OPS]
@@ -722,11 +740,31 @@ def plan():
         for d, w in dl[n]:
             pr[d] = max(pr[d], pr[n] + w + 1.0)
 
-    def place(pr):
+    rl = [[] for o in OPS]
+    for n in range(N):
+        for d, w in dl[n]:
+            rl[d].append((n, cost[n] + w - cost[d]))
+    zero, lat = [0.0] * N, [tail[n] - cost[n] for n in range(N)]
+
+    def turn(sch):
+        back = place([sch[2][n] + cost[n] + 1e-6 * n for n in range(N)], rl, lat, True)
+        p = [back[2][n] + cost[n] - 1e-6 * n for n in range(N)]
+        for n in range(N - 1, -1, -1):
+            for d, w in dl[n]:
+                if p[d] <= p[n]:
+                    p[d] = p[n] + 1e-3
+        return place(p), p
+
+    def place(pr, dl=dl, base=zero, back=False):
+        if back:
+            for n in range(N):
+                for d, w in dl[n]:
+                    if pr[d] <= pr[n]:
+                        pr[d] = pr[n] + 1e-3
         slots = {e: [] for e in "VSPGY"}
         beg, rdy = [0.0] * N, [0.0] * N
         for n in sorted(range(N), key=lambda n: (-pr[n], n)):
-            t = max([beg[d] + w for d, w in dl[n]] + [0.0])
+            t = max([beg[d] + w for d, w in dl[n]] + [base[n]])
             rdy[n] = t
             if eng[n] is not None:
                 sl = slots[eng[n]]
@@ -765,7 +803,9 @@ def plan():
                 if p2[d] <= p2[n]:
                     p2[d] = p2[n] + 1.0
         t2 = place(p2)
-        if t2[0] <= fin + 400.0 * (1.0 - it / TRIES) * float(rs.rand()):
+        if it % TURN == 0:
+            t2, p2 = turn(t2)
+        if t2[0] <= fin + 800.0 * (1.0 - it / TRIES) * float(rs.rand()):
             cur, pr = t2, p2
             if t2[0] < best[0]:
                 best = t2
@@ -774,20 +814,20 @@ def plan():
     order = {e: [x[2] for x in best[1][e]] for e in best[1]}
     pos = {n: i for e in order for i, n in enumerate(order[e])}
     need = set()
-    for e in order:
-        seen = {}
-        for n in order[e]:
-            o = OPS[n]
-            o["toks"] = [d for d in o["wait"] if OPS[d]["tok"]]
-            far = {}
-            for d in o["wait"]:
-                de = OPS[d]["eng"]
-                if OPS[d]["tok"] is None and pos[d] > seen.get(de, -1) and pos[d] > far.get(de, (-1, 0))[0]:
-                    far[de] = (pos[d], d)
-            o["cw"] = [d for (p_, d) in far.values()]
-            for de in far:
-                seen[de] = far[de][0]
-            need.update(o["cw"])
+    seen = {e: {} for e in order}
+    for o in sorted((o for o in OPS if o["eng"] is not None), key=lambda o: (o["t"], pos[o["n"]])):
+        sn = seen[o["eng"]]
+        o["toks"] = [d for d in o["wait"] if OPS[d]["tok"]]
+        o["cw"] = []
+        for d in sorted((d for d in o["wait"] if OPS[d]["tok"] is None), key=lambda d: -OPS[d]["t"]):
+            de = OPS[d]["eng"]
+            if pos[d] > sn.get(de, -1):
+                o["cw"].append(d)
+                sn[de] = pos[d]
+                for x, y in OPS[d]["know"].items():
+                    sn[x] = max(sn.get(x, -1), y)
+        o["know"] = dict(sn)
+        need.update(o["cw"])
     total = {}
     for e in order:
         total[e] = 0
@@ -805,29 +845,68 @@ def bits(es):
     return sum(1 << x for x in es)
 
 
-def helper_of(topo, cores, c):
-    mine = [x for x in cores if topo.chip(x) == topo.chip(c)]
-    free = [x for x in topo.cores_of(c) if x not in cores and topo.die(x) != topo.die(c)]
-    return free[mine.index(c)]
+def routes(topo, cores):
+    n = len(cores)
+    used, ways = set(cores), []
+
+    def take(ok):
+        x = [x for x in range(SIM) if x not in used and ok(x)][0]
+        used.add(x)
+        return x
+    turn = {}
+    for r in range(n):
+        s, d = cores[r], cores[(r - SH) % n]
+        if topo.chip(s) == topo.chip(d):
+            ways.append({"X": [[s, d]] * NCH, "C": [[s, d]] * NCH})
+            continue
+        mate = lambda x: topo.mates(topo.chip(x), topo.chip(d)) and topo.may_write(x, d)
+        probe = [x for x in range(SIM) if mate(x)][0]
+        if topo.may_write(s, probe):
+            w2 = [s, take(lambda x: mate(x) and topo.die(x) == topo.die(s)), d]
+            ways.append({"X": [w2, w2, w2, [s, d]], "C": [w2] * NCH})
+            continue
+        here = lambda x: topo.chip(x) == topo.chip(s) and topo.die(x) != topo.die(s)
+        o = take(lambda x: here(x) and topo.may_write(x, probe))
+        w3 = [s, o, take(lambda x: mate(x) and topo.die(x) == topo.die(o)), d]
+        w1 = [s, take(lambda x: here(x) and not topo.may_write(x, probe)), d]
+        turn[topo.chip(s)] = 1 - turn.get(topo.chip(s), 0)
+        ways.append({"X": [w3, w1, w1 if turn[topo.chip(s)] else [s, d], [s, d]], "C": [w3, w1, w3, w1]})
+    return ways
+
+
+def step(topo, w, j):
+    es = topo.engines(w[j], w[j + 1])
+    if j + 2 < len(w) and topo.chip(w[j]) == topo.chip(w[j + 1]):
+        es = [x for x in es if x not in topo.engines(w[j], w[-1])]
+    return es
 
 
 def rank_program(g, core, T, topo):
     cores = list(T.cores)
     n = len(cores)
     rank = T.rank_of(core)
-    far = lambda r: topo.chip(cores[r]) != topo.chip(cores[(r - SH) % n])
-    via = [i for i in range(NCH) if i % 2 == 0]
-    spare = lambda c, h, d: [x for x in topo.engines(c, h) if x not in topo.engines(c, d)]
+    ways = routes(topo, cores)
+
+    def hand(what, i, w, j, ls):
+        cs = slice(CW * i, CW * i + CW)
+        src, es, d = (T.X if what == "X" else T.CU)[:, cs], step(topo, w, j), w[j + 1]
+        if j + 2 < len(w):
+            dst, sem = src, T.sem[("hx%d" if what == "X" else "hc%d") % i]
+        else:
+            dst, sem = (T.X[:, VP + CW * i:VP + CW * i + CW], T.sem.xarr) if what == "X" else (T.CQ[:, cs], T.sem["ca%d" % i])
+        g.remote_dma(dst, src, sem, ls, topo.addr(d)[1], topo.addr(d)[0], bits(es))
+        return len(es)
     if rank is None:
-        for r in range(n):
-            if far(r) and topo.chip(cores[r]) == topo.chip(core) and helper_of(topo, cores, cores[r]) == core:
-                d = cores[(r - SH) % n]
-                for nm, sem, src, dst, off in (("hx", "xarr", T.X, T.X, VP), ("hc", None, T.CU, T.CQ, 0)):
-                    for i in via:
-                        g.wait_ge(T.sem["%s%d" % (nm, i)], len(spare(cores[r], core, d)))
-                        g.remote_dma(dst[:, off + CW * i:off + CW * i + CW], src[:, CW * i:CW * i + CW], T.sem[sem or "ca%d" % i], T.sem.ls0,
-                                     topo.addr(d)[1], topo.addr(d)[0], topo.mask(core, d))
-                g.wait_ge(T.sem.ls0, 2 * len(via) * len(topo.engines(core, d)))
+        out = 0
+        for what in "XC":
+            for r in range(n):
+                for i, w in enumerate(ways[r][what]):
+                    if core in w:
+                        j = w.index(core)
+                        g.wait_ge(T.sem[("hx%d" if what == "X" else "hc%d") % i], len(step(topo, w, j - 1)))
+                        out += hand(what, i, w, j, T.sem.ls0)
+        if out:
+            g.wait_ge(T.sem.ls0, out)
         return
     p, q = cores[(rank - SH) % n], cores[(rank + SH) % n]
     off = [x for x in cores if topo.chip(x) != topo.chip(core)][0]
@@ -839,21 +918,12 @@ def rank_program(g, core, T, topo):
     sent = [0]
 
     def big(what, i):
-        cs = slice(CW * i, CW * i + CW)
-        src, ls, num = (T.X, T.sem.ls0, sent) if what == "X" else (T.CU, T.sem.ls1, c["ls1"])
-        if far(rank) and i in via:
-            hc = helper_of(topo, cores, core)
-            m = spare(core, hc, p)
-            g.remote_dma(src[:, cs], src[:, cs], T.sem[("hx%d" if what == "X" else "hc%d") % i], ls, topo.addr(hc)[1], topo.addr(hc)[0], bits(m))
-        else:
-            m = topo.engines(core, p)
-            dst, sem = (T.X[:, VP + CW * i:VP + CW * i + CW], T.sem.xarr) if what == "X" else (T.CQ[:, cs], T.sem["ca%d" % i])
-            g.remote_dma(dst, src[:, cs], sem, ls, c["p"]["pid"], c["p"]["rid"], bits(m))
-        num[0] += len(m)
+        ls, num = (T.sem.ls0, sent) if what == "X" else (T.sem.ls1, c["ls1"])
+        num[0] += hand(what, i, ways[rank][what][i], 0, ls)
     c["big"] = big
-    vals = {"xarr": len(topo.engines(q, core)) * NCH}
-    for i in range(NCH):
-        vals["ca%d" % i] = len(topo.engines(q, core))
+    vals = {"xarr": sum(len(step(topo, w, len(w) - 2)) for w in ways[(rank + SH) % n]["X"])}
+    for i, w in enumerate(ways[(rank + SH) % n]["C"]):
+        vals["ca%d" % i] = len(step(topo, w, len(w) - 2))
     for r in range(RO):
         vals["am%d" % r], vals["aa%d" % r], vals["ak%d" % r] = len(es), h, len(es) - h
     qs = {"V": g.vector, "S": g.scalar, "P": g.tensor, "G": g, "Y": g.sync}

@@ -3,68 +3,83 @@ from concourse.bass import DstId, RemoteDMATransfer
 from concourse.mybir import AluOpType as A, AxisListType, ActivationFunctionType as F
 
 V, L, RO, SH, ST = 3328, 256, 4, 3, 61
-VP = V + L
+NUL = V + L
+VP = NUL + 16
 CEN = V // 2
 BIG = float(2 ** 20)
-THR = 70000.0
-PEN = 98304.0
+DEAD = 2048.0
+OFF = 128 * DEAD
+THR = 135168.0
+PEN = 262144.0
+K0 = 8.0 - 1.0 / 32
 M1 = 1.5 * 2 ** 23
 M2 = 1.5 * 2 ** 24
 M16 = 1.5 * 2 ** 27
-GC = 32
-NV1, NV2 = 96, 96
-XV1, XV2 = 32, 0
-SB1, SB2, SB3 = "347", "34", "346"
-VG = 7
-FS = 4
-PB = 3000.0
-SEED, TRIES = 2, 7000
-LLV = [(0, 0), (0, 1), (1, 0)]
-EV = ["SSSSVSVS", "SSVSSVVV", "SSVSSVVV", "SSVSSVVV"]
-VB = ["342", "67"]
-TURN = 8
+HV = [[12, 12], [8, 8]]
+HVL = [[8, 8], [8, 8]]
+EA = ["VV", "SS", "SS", "SS"]
+VQ = "VVSSVSSVSVVSSVSV"
+STEPS = "rc0A1kBbe"
+XS = 4
+OS = 6
+SEED, TRIES = 3, 600
+FIRST = 110000
+MOVES = 70000
+FAR = 12
+TURN, LEAN = 8, 1500.0
+LEAN0 = 900.0
+HEAT = 200.0
+RAND = 0.3
+COOL = 45.0
+SLACK = 60.0
 SIM = 64
 NCH = 4
 CW = V // NCH
 
 SCRATCH = {}
 for _d, _l in (
-        ("bfloat16", (("X", 2 * VP), ("XO", V), ("CT", VP), ("VV", 4096), ("XC", 4096), ("ED", 14 * 256), ("L2", 1536), ("IL", 160), ("K16", 768),
-                      ("nIb", 128), ("PENI", 128), ("Bx", 128), ("nB16", 128), ("BB", 64), ("NST", 768), ("KI", 512), ("KH", 256), ("DP", 256),
-                      ("DN", 256), ("negL", 32), ("SELN", 256), ("cb", 256), ("GB", 1024), ("Q", 96), ("QT", 128), ("Me", 256), ("Mf", 256),
-                      ("Mn", 256), ("Mz", 256), ("xs", 256), ("EQ", 7 * 256), ("OH", 512), ("D1", 768), ("U", 768), ("PN", 768), ("D3", 256),
-                      ("U3", 256), ("RR", 512), ("LL", 1024), ("junk", 1536), ("m2", 256), ("mid", 1024), ("rmid", 1024), ("Lo", 256),
-                      ("cm", 128), ("ones", 128), ("wn", 16))),
-        ("float16", (("Ih", 128), ("nIh", 128), ("SEL", 13 * 128), ("LB", 3 * 144), ("DS", 3 * 128), ("Bo", 256), ("B2", 24), ("DA", 256), ("DB", 256), ("Wa", 256),
-                     ("Wn", 256), ("Wz", 256), ("Wf", 256), ("TT", 256), ("TS", 768), ("PZ", 512), ("Y1", 256), ("Y2", 256), ("Ye", 256), ("Yl", 256), ("Cc", 512),
-                     ("D2", 256), ("T1", 256), ("T2", 256))),
-        ("float32", (("Li", 256), ("RST", 512), ("CR", 512), ("KM", 16), ("col", 32), ("thr", 16), ("tf", 256), ("I32", 128), ("pm", 512), ("pe", 512),
-                     ("km", 256), ("sm", 1024), ("xa", 256), ("xb", 256), ("abf", 32), ("ef", 32), ("Hi", 16), ("tq", 256), ("yo", 256),
-                     ("yq", 256), ("yc", 256))),
-        ("int32", (("CA", V), ("CP", V), ("si", 64), ("wi", 256), ("ci", 256), ("ti", 256), ("pi", 4))),
-        ("uint16", (("WO", 256), ("CO", 256), ("el", 16), ("fl", 64), ("rs", 256), ("CU", V), ("CQ", V), ("ab", 32), ("eff", 128), ("rl", 128)))):
+        ("bfloat16", (("X", 2 * VP), ("XO", V), ("CT", NUL), ("VV", 4112), ("XC", 4096), ("MM", 4096), ("ED", 4096), ("BB", 32), ("nB", 17 * 128), ("L2", 128),
+                      ("IL", 160), ("K16", 256), ("nIb", 128), ("PENI", 128), ("nPEN", 128), ("CI", 128), ("Bx", 128), ("NST", 768), ("NS8", 256), ("KN", 128),
+                      ("KI", 256), ("KH", 256), ("CC", 1024), ("DN", 256), ("xs", 512), ("EQ", 7 * 256), ("eq", 512), ("OH", 512), ("DM", 768), ("UM", 768),
+                      ("G0", 256), ("G1", 512), ("OA", 256), ("NU", 256), ("en", 128), ("sb", 256), ("xm", 512), ("GU", 512), ("PQ", 144), ("de", 128),
+                      ("RR", 512), ("CR", 512), ("junk", 1536), ("mid", 1024), ("rmid", 1024), ("Lo", 256), ("ones", 128), ("wn", 32), ("m2", 256), ("Me", 256),
+                      ("R1", 320))),
+        ("float16", (("Ih", 128), ("nIh", 128), ("I2", 256), ("B2", 96), ("CU", V), ("CQ", V), ("ZW", 512), ("RC", 160), ("DA", 512), ("DB", 512), ("DL", 1808),
+                     ("TL", 1808), ("Wn", 272), ("Wf", 256), ("Wb", 256), ("Cc", 256), ("Y", 256), ("YS", 512), ("DK", 512), ("UK", 512), ("XV", 256),
+                     ("es", 128), ("NV", 32), ("YE", 512), ("YA", 512))),
+        ("float32", (("Li", 256), ("RST", 256), ("RF", 256), ("RB", 256), ("KM", 16), ("col", 32), ("abf", 32), ("XF", VP), ("DF", 256), ("CP", V), ("cth", 512),
+                     ("I32", 128), ("pm", 512), ("pd", 272), ("pe", 512), ("sm", 1024), ("xa", 256), ("xb", 256), ("xc", 256), ("ra", 160), ("RS5", 160),
+                     ("ef", 32), ("Hi", 16), ("tq", 256), ("TS", 256), ("yo", 256), ("yc", 256))),
+        ("int32", (("CA", V), ("wi", 256), ("ci", 256), ("ti", 256), ("pi", 8))),
+        ("uint16", (("WO", 256), ("CO", 512), ("el", 16), ("fl", 16), ("ab", 32), ("eff", 128), ("rl", 128)))):
     for _n, _c in _l:
         SCRATCH[_n] = ("sbuf", [128, _c], _d)
-SCRATCH["MM"] = ("sbuf", [128, 16, 256], "bfloat16")
-for _n in range(8):
-    SCRATCH["P%d" % _n] = ("psum", [128, 512], "float32")
+for _n, _s, _d in (("LL", [8, 128], "bfloat16"), ("TA", [16, 32], "float16"), ("TB", [16, 32], "float16"), ("WXo", [16, 24], "float32"), ("WXe", [16, 28], "float32")):
+    SCRATCH[_n] = ("sbuf", [128] + _s, _d)
+for _n in ("KA", "KB", "PE"):
+    SCRATCH[_n] = ("psum", [128, 512], "float32")
+for _n in ("PT", "PW", "D0", "D1", "D2"):
+    SCRATCH[_n] = ("psum", [128, 32, 16], "float32")
 
 SEMAPHORES = (["sV", "sS", "sP", "sG", "ls0", "ls1", "xarr", "lw", "lc", "lt", "ox", "ow", "on"]
               + ["%s%d" % (s, i) for s in ("lx", "hx", "hc", "lk", "ca") for i in range(NCH)]
               + ["%s%d" % (s, r) for s in ("am", "aa", "ak") for r in range(RO)])
 TWO = ("bfloat16", "float16", "uint16")
+SCR, BANK = dict(SCRATCH), {}
 
 
 def a(name, c0=0, c1=None, st=1, p=None):
-    return ("a", name, c0, SCRATCH[name][1][1] if c1 is None else c1, st, p)
+    return ("a", name, c0, SCR[name][1][1] if c1 is None else c1, st, p)
 
 
 def rev(name, c0, c1):
     return ("r", name, c0, c1)
 
 
-def m3(i0, i1, l0, l1):
-    return ("m", "MM", i0, i1, l0, l1)
+def t3(name, r=None, c=None, p=None):
+    s = SCR[name][1]
+    f = lambda x, n: (0, n, 1) if x is None else x if isinstance(x, int) else (x[0], x[1], x[2] if len(x) > 2 else 1)
+    return ("t", name, f(r, s[1]), f(c, s[2]), p)
 
 
 def ind(w, o):
@@ -75,30 +90,35 @@ def isop(x):
     return isinstance(x, tuple)
 
 
+def rng(x):
+    return [x] if isinstance(x, int) else range(*x)
+
+
 def regs(x):
     if x[0] == "i":
         return regs(x[1]) + regs(x[2])
-    if x[0] == "m":
-        return [("MM", 256 * i + x[4], 256 * i + x[5]) for i in range(x[2], x[3])]
+    if x[0] == "t":
+        w, c = SCR[x[1]][1][2], rng(x[3])
+        return [(x[1], w * i + c[0], w * i + c[-1] + 1) for i in rng(x[2])]
     return [(x[1], x[2], x[3])]
 
 
 def cnt(x):
     if x[0] == "i":
         return 16 * cnt(x[2])
-    if x[0] == "m":
-        return (x[3] - x[2]) * (x[5] - x[4])
+    if x[0] == "t":
+        return len(rng(x[2])) * len(rng(x[3]))
     if x[0] == "r":
         return x[3] - x[2]
     return len(range(x[2], x[3], x[4]))
 
 
 def dty(x):
-    return SCRATCH[x[1][1] if x[0] == "i" else x[1]][2]
+    return SCR[x[1][1] if x[0] == "i" else x[1]][2]
 
 
 def ps(x):
-    return x[0] != "i" and SCRATCH[x[1]][0] == "psum"
+    return x[0] != "i" and SCR[x[1]][0] == "psum"
 
 
 def mk(T, x):
@@ -106,26 +126,29 @@ def mk(T, x):
         return x
     if x[0] == "i":
         return mk(T, x[1]).indirect(mk(T, x[2]))
-    if x[0] == "m":
-        if x[3] - x[2] == 1:
-            return T["MM"][:, x[2], x[4]:x[5]]
-        return T["MM"][:, x[2]:x[3], x[4]:x[5]]
+    t = T[BANK.get(x[1], x[1])]
     if x[0] == "r":
-        return T[x[1]][:, x[3] - 1:(x[2] - 1 if x[2] else None):-1]
-    p = slice(None) if x[5] is None else slice(x[5][0], x[5][1])
-    if x[4] == 1:
-        return T[x[1]][p, x[2]:x[3]]
-    return T[x[1]][p, x[2]:x[3]:x[4]]
+        return t[:, x[3] - 1:(x[2] - 1 if x[2] else None):-1]
+    p = slice(None) if x[-1] is None else slice(x[-1][0], x[-1][1])
+    f = lambda y: y if isinstance(y, int) else slice(y[0], y[1]) if y[2] == 1 else slice(*y)
+    if x[0] == "t":
+        return t[p, f(x[2]), f(x[3])]
+    return t[p, f(x[2:5])]
 
 
-OPS = []
-CY, GA, SCA, PEC, VF, SF, SL, RI, RL = 0.9, 1.56, 3.8, 0.46, 30.0, 50.0, 120.0, 700.0, 2500.0
+OPS, SEEN = [], {}
+CY = 0.9
+PEC = 0.53
+GA, SCA, VF, SF, PF, SL, RI, RL = 1.56, 3.8, 30.0, 50.0, 40.0, 120.0, 700.0, 2500.0
 
 
-def op(eng, emit, rd, wr, cost, tok=None, lat=0.0, track=True, after=()):
+def op(eng, emit, rd, wr, cost, tok=None, lat=0.0, track=True, after=(), acc=False):
     r = [q for x in rd if isop(x) for q in regs(x)]
     w = [q for x in wr for q in regs(x)]
-    o = {"eng": eng, "emit": emit, "r": r, "w": w, "cost": cost, "tok": tok, "lat": lat, "track": track, "after": list(after), "n": len(OPS)}
+    o = {"eng": eng, "emit": emit, "r": r, "w": w, "cost": cost, "tok": tok, "lat": lat, "track": track, "after": list(after), "n": len(OPS), "acc": acc, "alt": None}
+    k = (eng, ("D",) + tuple(sorted(set(q[0] for q in r))) if w and w[0][0][:2] == "D#" else w[0][:1 if w[0][0] in ("X", "XF", "mid", "eff", "rl", "rmid") else 2] if w else ())
+    SEEN[k] = SEEN.get(k, 0) + 1
+    o["kind"] = k + (SEEN[k],)
     OPS.append(o)
     return o
 
@@ -181,16 +204,36 @@ def act(out, in_, f, bias=0.0, scale=1.0, acc=None):
         e = lambda g, T, c: g.scalar.activation(mk(T, out), mk(T, in_), f, mk(T, bias), mk(T, scale))
     else:
         e = lambda g, T, c: g.scalar.activation(mk(T, out), mk(T, in_), f, mk(T, bias), mk(T, scale), accum_out=mk(T, acc))
+        co += 20
     return op("S", e, [in_, bias, scale], [out] + ([acc] if acc else []), co)
 
 
-def pe(ml):
+def either(v, s):
+    x = OPS.pop()
+    SEEN[x["kind"][:2]] -= 1
+    v["alt"] = (x["eng"], x["emit"], x["cost"])
+    return v
+
+
+def lin(out, in_, scale, bias=0.0):
+    return either(ts(out, in_, scale, A.mult, bias, A.add), act(out, in_, F.Identity, bias, scale))
+
+
+def gather(out, src):
+    return either(cp(out, src), act(out, src, F.Copy))
+
+
+def pe(ml, acc=False):
     def e(g, T, c):
         for m in ml:
             r = g.tensor.matmul(mk(T, m[0]), mk(T, m[1]), mk(T, m[2]), m[3], m[4])
         return r
-    co = 40 + sum(max(min(64, cnt(m[1])), cnt(m[2])) * (4 if dty(m[1]) == "float32" else 1) * PEC for m in ml)
-    return op("P", e, [x for m in ml for x in m[1:3]], [m[0] for m in ml], co)
+    co = PF + sum(max(min(64, cnt(m[1])), cnt(m[2])) * (4 if dty(m[1]) == "float32" else 1) * PEC for m in ml)
+    return op("P", e, [x for m in ml for x in m[1:3]], [m[0] for m in ml], co, acc=acc)
+
+
+def group(out, terms):
+    pe([(out, w, x, i == 0, i == len(terms) - 1) for i, (w, x) in enumerate(terms)])
 
 
 def iota(out, pat, base, cm):
@@ -225,289 +268,356 @@ def blk(name, i, w=256, o=0, n=None):
     return a(name, w * i + o, w * i + o + (w if n is None else n))
 
 
+def sb(i):
+    return blk("sb", i, 16)
+
+
 I_ = a("IL", 16, 144)
-B32, Bm16, B16, Bm1, B1 = [a("BB", 8 * i, 8 * i + 8) for i in range(5)]
-(KC, KC1, KK, OFF, M15, IS15, MG0, MG1, VB0, VB1, DU0, DU1, SC, MLO, MHI, M12, EVN, ODD, PF, R0, AC, CM5, MA0, MA1, MB0, MB1, KF, N12, N128) = range(29)
-(NL, BND, TH16, JJ, CUT, T0, FL, S_, CE, PRE, QQ, NS, KEY0, KEYX, C2, K1, PEN1, TT_, UU, GB_, GO2, KS, T1_, T2_, T3_, NP_, MA, CB,
- T4_, T5_, MM_, ED_, H1, H2, H4, E1, E2, E3, E4, E5, E6, C1, C3, C5, W0, W1, W2, W3, KF_, KB_, U1, U2, U4) = range(53)
-OWN, PAR, OWND, PARD = a("X", 0, V), a("X", VP, VP + V), a("X", 0, VP), a("X", VP, 2 * VP)
-WP = a("P5", 0, 256)
-rot = [0]
+B1 = a("Bx", 0, 128, 16)
+B32, Bm16, B16 = [a("BB", 8 * i, 8 * i + 8) for i in range(3)]
+(KC, MG0, MG1, SC, MLO, MHI, M12, AC, AD, MV, N16, PP, K32, P64, MK) = range(15)
+(BND, BND2, TH16, TH2, NQ, NJ, E1, FL, S_, QQ, W0, W1, W2, W3, X0, X1, X2, X3, KZ, KO, KX, Z1, T1_, T2_, US, RED, FH, NW, PN, VB, VT, U1, U2, U3, C2, TH) = range(36)
+(CK, POS, PI, NEG, H1, H2, ED_, PF_, NP_, NP2, WEF, WFH) = range(12)
+NL, PC, PTH, KK = a("en", 7, 128, 8), sm(C2), sm(TH), ("KA", "KB")
+OWN, PAR = a("XF", 0, V), a("X", VP, VP + V)
+OWND, PARD = a("XF", 0, NUL), a("X", VP, VP + NUL)
+OWNN, PARN = a("XF", 0, VP), a("X", VP, 2 * VP)
+WP, WB = t3("PW", (0, 16)), t3("PW", (16, 32))
+WN = a("Wn", 0, 256)
+ZERO, CNUL = a("CC", 0, 16), a("NV", 0, 16)
 
 
-def sbank(sb):
-    rot[0] += 1
-    return "P" + sb[rot[0] % len(sb)]
+def dbank():
+    n = "D#%d" % len(SCR)
+    SCR[n] = SCR["D0"]
+    return n
 
 
-def tolist(out0, w, y, bk="P2"):
-    return [(a(bk, out0, out0 + 16), a("LB", 144 * w + 15 - b, 144 * w + 143 - b), a(y, b, 256, 16), b == 0, b == 15) for b in range(16)]
+def slot():
+    return t3(dbank(), 0)
+
+
+def flip(bk, src, r0=0, hs=(0, 2)):
+    pe([(t3(bk, (r0 + 8 * h, r0 + 8 * h + 8)), blk(src, h, 128), a("Ih"), True, True) for h in range(*hs)])
+
+
+def tolist(c0, n, nb=8):
+    scan(a("TL", c0, c0 + n), a("DA" if nb == 8 else "DB", 0, n), a("DL", c0, c0 + n), 0.0, A.mult, A.add)
+    bk = dbank()
+    o = lambda j: t3(bk, j * nb // 16, (j * nb % 16, j * nb % 16 + nb))
+    w = lambda j, z: a("B2", 8 * z, 8 * z + 8) if nb == 8 else a("B2", 32 + 16 * z + 4 * j, 36 + 16 * z + 4 * j)
+    ml = [m for j in range(n // 128) for m in ((o(j), a("TL", c0 + 128 * j, c0 + 128 * j + 128), w(j, 0), nb == 8, False),
+                                               (o(j), a("TL", c0 + 128 * j + 1, c0 + 128 * j + 129), w(j, 1), False, False),
+                                               (o(j), a("DL", c0 + 128 * j + 1, c0 + 128 * j + 129), w(j, 0), False, nb == 8 or j == 3))]
+    pe(ml if nb == 8 else [(t3(bk, 0), a("Ih"), a("B2", 64, 80), True, False)] + ml)
+    return bk
 
 
 def consts():
     iota(a("pi", 0, 1), [[0, 1]], 0, 1)
     iota(a("IL"), [[1, 160]], -16, -1)
-    iota(a("K16", 0, 256), [[0, 16], [1, 16]], 0, 0)
+    iota(a("K16"), [[0, 16], [1, 16]], 0, 0)
     iota(a("Li"), [[1, 256]], 0, 0)
-    for i in range(3):
-        iota(blk("L2", i, 512), [[1, 32], [0, 16]], 32 * i, -1)
-        ts(blk("L2", i, 512), blk("L2", i, 512), 0.0, A.is_equal)
-    cp(col(PF), a("pi", 0, 1))
-    ts(a("pi", 1, 2), a("pi", 0, 1), 15, A.bitwise_and)
-    cp(col(KC), a("pi", 1, 2))
-    ts(a("pi", 2, 3), a("pi", 0, 1), 1, A.bitwise_and)
-    cp(col(ODD), a("pi", 2, 3))
-    ts(a("pi", 3, 4), a("pi", 0, 1), 16, A.bitwise_and)
-    ts(col(MG1), a("pi", 3, 4), 1.0 / 16, A.mult)
+    iota(a("L2"), [[1, 8], [0, 16]], 0, -1)
+    iota(a("junk", 0, 512), [[0, 16], [1, 32]], 0, 0)
+    iota(a("NS8"), [[0, 32], [1, 8]], 0, 0)
+    iota(a("RS5"), [[0, 32], [1, 5]], 0, 0)
+    iota(a("KN"), [[0, 16], [2, 8]], 1, 0)
+    ts(a("L2"), a("L2"), 0.0, A.is_equal)
+    ts(a("IL"), a("IL"), 0.0, A.is_equal)
+    cp(col(PP), a("pi", 0, 1))
+    for j, (c, m) in enumerate(((KC, 15), (P64, 63), (MG1, 16))):
+        ts(a("pi", j + 1, j + 2), a("pi", 0, 1), m, A.bitwise_and)
+        cp(col(c), a("pi", j + 1, j + 2))
+    ts(col(MG1), col(MG1), 1.0 / 16, A.mult)
+    ts(col(K32), col(PP), 64.0, A.is_ge, 16.0, A.mult)
+    tt(col(K32), col(K32), col(KC), A.add)
     ts(col(MG0), col(MG1), -1.0, A.mult, 1.0, A.add)
-    ts(col(KC1), col(KC), 1.0, A.add)
-    ts(col(IS15), col(KC), 15.0, A.is_equal)
-    ts(col(M15), col(KC), 15.0, A.not_equal)
-    ts(col(EVN), col(ODD), -1.0, A.mult, 1.0, A.add)
-    ts(col(KK), col(KC), col(EVN), A.subtract, col(M15), A.mult)
-    ts(col(EVN), col(EVN), col(IS15), A.add)
-    act(col(VB0), col(PF), F.Identity, -12.0, 1.0 / 128)
-    act(col(VB1), col(PF), F.Identity, -11.0, 1.0 / 128)
-    act(col(DU0), col(PF), F.Identity, float(CEN))
-    act(col(DU1), col(PF), F.Identity, float(CEN + 128))
-    ts(col(R0), col(KC), 0.0, A.is_equal)
     ts(col(MLO), col(KC), 8.0, A.is_lt)
     ts(col(M12), col(KC), 12.0, A.is_equal)
     ts(col(MHI), col(KC), 12.0, A.is_lt, col(MLO), A.subtract)
-    ms(col(CM5), -0.5)
-    ts(col(KF), col(KC1), 3584.0, A.mult)
-    for gm in range(2):
-        tt(col(MB0 + gm), col(MG0 + gm), col(M12), A.mult)
-        tt(col(MA0 + gm), col(MG0 + gm), col(MB0 + gm), A.subtract)
-    act(col(N12), col(M12), F.Identity, 0.0, -1.0)
-    act(col(N128), col(M12), F.Identity, 0.0, -1.0 / 128)
-    ts(a("IL"), a("IL"), 0.0, A.is_equal)
-    act(blk("K16", 1), blk("K16", 0), F.Copy)
-    act(blk("K16", 2), blk("K16", 0), F.Copy)
     act(a("nIb"), I_, F.Identity, 0.0, -1.0)
     act(a("PENI"), I_, F.Identity, 0.0, PEN)
     cp(a("Ih"), I_)
-    cp(a("nIh"), a("nIb"))
+    ts(a("nIh"), I_, -1.0, A.mult)
+    ts(blk("I2", 0, 128), I_, 2.0, A.mult)
+    ts(blk("I2", 1, 128), I_, -2.0, A.mult)
     act(a("I32"), I_, F.Copy)
-    pe([(a("P2", 0, 128), a("L2", 0, 128, p=(0, 8)), a("L2", 0, 128, p=(0, 8)), True, True)])
-    cp(a("Bx"), a("P2", 0, 128))
-    act(a("nB16"), a("Bx"), F.Identity, 0.0, -16.0)
-    for x, v in ((B32, 32.0), (Bm16, -16.0), (Bm1, -1.0), (B1, 1.0), (a("BB", 48, 56), 16.0), (a("BB", 56, 64), 16.0)):
-        act(x, a("Bx", 0, 128, 16), F.Identity, 0.0, v)
-    for x, v in ((a("B2", 0, 8), 2.0), (a("B2", 8, 16), -2.0), (a("B2", 16, 24), col(R0))):
-        ts(x, a("Bx", 0, 128, 16), v, A.mult)
-    ts(a("KM"), a("K16", 0, 16), col(KC), A.is_equal)
-    for k in range(13):
-        act(blk("EQ", k, 128), a("Bx"), F.Identity, 0.0, a("KM", k, k + 1))
-    cp(a("SEL"), a("EQ", 0, 13 * 128))
-    ms(a("LB"), 0.0)
-    cp(a("LB", 15, 143, 16), B1)
-    ts(a("LB", 144 + 15, 144 + 143, 16), B1, col(EVN), A.mult)
-    ts(a("LB", 288 + 15, 288 + 143, 16), B1, col(ODD), A.mult)
+    pe([(a("KA", 0, 128), a("L2", p=(0, 8)), a("L2", p=(0, 8)), True, True)])
+    act(a("Bx"), a("KA", 0, 128), F.Copy)
+    for x, v in ((B32, 32.0), (Bm16, -16.0), (B16, 16.0)):
+        act(x, B1, F.Identity, 0.0, v)
+    cp(a("B2", 0, 8), B1)
+    ts(a("B2", 8, 16), B1, -1.0, A.mult)
+    tt(a("B2", 16, 20), a("Bx", 0, 64, 16), a("Bx", 64, 128, 16), A.add)
+    ts(a("B2", 20, 24), a("K16", 0, 4), 16.0, A.mult)
+    for q in range(4):
+        ts(a("B2", 24, 28), a("B2", 20, 24), float(V + 16 + 64 * q), A.add)
+        tt(a("B2", 32 + 4 * q, 36 + 4 * q), a("B2", 24, 28), a("B2", 16, 20), A.mult)
+    ts(a("B2", 48, 64), a("B2", 32, 48), -1.0, A.mult)
+    for nv in sorted(set(x for y in HV + HVL for x in y) - {0}):
+        ts(a("Me", 0, 128), a("K16", 0, 128), float(nv), A.is_lt, -16.0, A.mult)
+        tt(blk("nB", nv, 128), a("Me", 0, 128), a("Bx"), A.mult)
     for z in range(2):
-        for u in range(2):
-            iota(blk("LL", 2 * z + u, 128), [[16, 8], [200, 2], [2, 8]], z - 200 * u, -1)
-    ts(a("PZ"), a("LL", 0, 512), 0.0, A.is_equal)
-    ms(a("Bo"), 0.0)
-    cp(a("Bo", 1, 128, 2), a("Bx", 1, 128, 2))
-    cp(a("Bo", 128, 256, 2), a("Bx", 0, 128, 2))
-    for i, s in enumerate((2, 4, 8)):
-        d = blk("DS", i, 128)
-        tt(d, a("IL", 16 + s, 144 + s), I_, A.subtract)
-        ts(a("cm"), a("K16", 0, 128), 14.0 - s, A.is_le)
-        tt(d, d, a("cm"), A.mult)
-    act(a("RST"), a("K16", 0, 512), F.Relu, 16 * BIG, -16 * BIG)
-    act(a("NST"), a("K16"), F.Sign)
-    act(a("KI"), a("K16", 0, 512), F.Identity, -7.5)
-    act(a("KH"), blk("K16", 0), F.Identity, 0.0, 1.0 / 16)
-    ts(a("DB"), blk("K16", 0), col(KC), A.is_lt)
-    ts(a("DA"), blk("K16", 0), col(KC), A.is_le)
-    ms(a("DA", 0, 256, 16), 0.0)
-    for x, v in ((a("X", V, VP), 0.0), (a("X", VP + V, 2 * VP), 0.0), (a("D2"), 0.0), (sm(U1), 0.5), (sm(U2), 0.0)):
-        ms(x, v)
-    for x, v in ((a("DP"), 1024.0), (a("DN"), -1024.0), (a("CT", V, VP), 0.0), (a("D1"), -1.0), (a("D3"), -1.0), (a("Q"), 0.0), (a("ones"), 1.0),
-                 (a("SELN"), 0.0)):
-        act(x, a("K16", 0, cnt(x)), F.Identity, v, 0.0)
+        ts(blk("DA", z), a("K16"), col(KC), A.is_le)
+    ms(a("DA", 0, 512, 16), 0.0)
+    ts(a("DB"), a("junk", 0, 512), col(K32), A.is_le)
+    ms(a("DB", 0, 512, 32), 0.0)
+    ts(col(MV), col(KC), 12.0, A.is_lt, BIG, A.mult)
+    for z in range(2):
+        tt(col(MK + z), col(MG0 + z), col(MV), A.mult)
+        ts(col(MK + 2 + z), col(MG0 + z), col(M12), A.mult, 256.0, A.mult)
+    ts(col(N16), col(M12), -16.0, A.mult)
+    ts(a("KM"), a("K16", 0, 16), col(KC), A.is_equal)
+    act(blk("CC", 0), a("K16"), F.Identity, 0.0, 0.0)
+    ts(a("B2", 64, 80), ZERO, col(KC), A.add, -16.0, A.add)
     for h in range(2):
-        ts(blk("negL", h, 16), a("Li", 0, 256, 16), col(KC), A.add, -1.0, A.mult)
-        ts(blk("thr", h, 8), a("K16", 0, 8), VG - 0.5, A.is_lt, col(VB0 + h), A.mult)
-        act(blk("CR", h), a("Li"), F.Identity, col(N12), col(N128))
-        b1, b2 = 16 * (48 + 8 * h), 16 * (64 + 8 * h)
-        act(sm(H1, 8, 8 * h), a("L2", b1, b1 + 128, 16), F.Identity, 0.0, float(ST))
-        act(sm(H2, 8, 8 * h), a("L2", b2, b2 + 128, 16), F.Identity, 0.0, float(-V))
-        tt(a("SELN", 128 * h, 128 * h + 128, 16), sm(H1, 8, 8 * h), sm(H2, 8, 8 * h), A.add)
-    scan(sm(T4_, 8), sm(U1, 8), sm(U2, 8), 1.0, A.mult, A.add)
-    cp(sm(T4_, 4, 8), sm(T4_, 4))
-    tt(sm(T5_, 12), sm(T4_, 12), a("KM", 0, 12), A.mult)
-    red(col(SC), sm(T5_, 12), A.add)
+        ts(a("NV", 16 + 8 * h, 24 + 8 * h), a("CC", 0, 8), col(PP), A.add, float(CEN + 128 * h), A.add)
+    for x, v in ((a("ZW"), 0.0), (a("DL"), 0.0), (a("TL", 0, 1808, 128), 0.0), (a("RC"), 0.0), (a("R1"), 1.0)):
+        ms(x, v)
+    for z in range(2):
+        cp(a("RC", 80 * z + 4, 80 * z + 80, 5), a("NV", 16, 32))
+    for c0 in (1, 4, 160, 164):
+        ms(a("R1", c0, c0 // 160 * 160 + 160, 5), 0.0)
+    for q in range(4):
+        act(col(AD), col(P64), F.Identity, 4096.0 * (64 * q - 12 * 256), 4096.0)
+        act(sm(VB, 4, 4 * q), a("K16", 0, 4), F.Identity, col(AD), 0.0)
+    act(sm(VT), sm(VB), F.Identity, 0.0, -1.0)
+    for b in range(16):
+        if VQ[b] == "S" and (b == 0 or VQ[b - 1] == "V"):
+            n = len(VQ[b:]) - len(VQ[b:].lstrip("S"))
+            lin(sm(VT, n, b), sm(VB, n, b), 0.0)
+    for z in range(2):
+        act(blk("CR", z), a("Li"), F.Identity, 0.0, col(N16))
+    act(a("RS5"), a("RS5"), F.Relu, 16 * BIG, -16 * BIG)
+    act(a("NS8"), a("NS8"), F.Sign)
+    act(a("nPEN"), I_, F.Identity, 0.0, -PEN)
+    act(a("CI"), I_, F.Identity, 0.0, float(CEN))
+    act(a("RST"), a("K16"), F.Relu, 16 * BIG, -16 * BIG)
+    for i in range(3):
+        act(blk("NST", i), a("K16"), F.Sign)
+    act(a("KI"), a("K16"), F.Identity, -K0)
+    for k in (14, 15):
+        act(a("KI", k, 256, 16), a("K16", 0, 16), F.Identity, PEN, 0.0)
+    act(a("KH"), a("K16"), F.Identity, 0.0, 1.0 / 16)
+    for x, v in ((a("XF", V, NUL), 0.0), (a("X", VP + V, VP + NUL), 0.0), (a("XF", NUL, VP), DEAD), (a("X", VP + NUL, 2 * VP), -DEAD), (sm(U1), 0.5), (sm(U2), 0.0),
+                 (a("Wn", 256, 272), 0.0), (CNUL, float(NUL - CEN)), (a("DK"), 1.0), (t3("TA"), 0.0), (t3("TB"), 0.0), (a("pd", 0, 8), 0.0), (a("pd", 264, 272), 0.0)):
+        ms(x, v)
+    for x, v in ((a("xc"), DEAD), (a("DN"), -DEAD), (a("ones"), 1.0), (a("RF"), 0.0), (a("RB"), 0.0),
+                 (blk("DM", 0), 0.0), (blk("DM", 1), 0.0), (blk("DM", 2), 4096.0), (blk("G0", 0), 1.0), (blk("G1", 0), 0.0), (blk("G1", 1), -1.0), (blk("CC", 3), -0.5),
+                 (a("G0", 15, 256, 16), 0.0), (a("G1", 271, 512, 16), -40.0), (a("RF", 14, 256, 16), BIG), (sb(CK), -K0)):
+        either(ms(x, v), act(x, a("K16", 0, cnt(x)), F.Identity, v, 0.0))["r"] = regs(a("K16"))
+    act(a("DF"), a("xc"), F.Silu)["cost"] += 1300
+    act(a("CT", V, NUL), a("K16"), F.Identity, 0.0, 0.0)
+    scan(sm(U3, 8), sm(U1, 8), sm(U2, 8), 1.0, A.mult, A.add)
+    cp(sm(U3, 4, 8), sm(U3, 4))
+    tt(sm(Z1, 12), sm(U3, 12), a("KM", 0, 12), A.mult)
+    red(col(SC), sm(Z1, 12), A.add)
     ts(a("tq"), a("Li"), 0.5, A.add, col(SC), A.mult)
     ts(a("xa"), a("tq"), M1, A.add, M1, A.subtract)
     act(a("xb"), a("xa"), F.Identity, 0.0, -1.0)
-    pe([(a("P3", 0, 256), a("I32"), a("tq"), True, False), (a("P3", 0, 256), a("I32"), a("xb"), False, True)])
-    act(a("m2"), a("P3", 0, 256), F.Sign)
-    act(a("Lo"), a("m2"), F.Identity, col(M12), col(MLO))
+    pe([(a("KB", 0, 256), a("I32"), a("tq"), True, False), (a("KB", 0, 256), a("I32"), a("xb"), False, True)])
+    act(a("m2"), a("KB", 0, 256), F.Sign)
+    act(a("Lo"), a("m2"), F.Identity, 0.0, col(MLO))
     act(a("Hi"), a("m2", 0, 16), F.Identity, 0.0, col(MHI))
     for c in range(V // 256):
-        if c % 2:
-            act(blk("CT", c), a("Lo"), F.Identity, a("Hi", c, c + 1))
-        else:
-            ts(blk("CT", c), a("Lo"), a("Hi", c, c + 1), A.add)
-        OPS[-1]["prio"] = 4000.0
+        x = a("Hi", c, c + 1)
+        either(ts(blk("CT", c), a("Lo"), x, A.add), act(blk("CT", c), a("Lo"), F.Identity, x))["prio"] = 4000.0
 
 
-def post_cut():
-    nG = blk("GB", 3)
-    ts(a("Me"), nG, col(KC1), A.is_equal)
-    tt(a("Yl"), WP, a("Me"), A.mult)
-    pe(tolist(0, 0, "Yl", "P1"))
-    ts(a("el"), a("P1", 0, 16), float(CEN), A.add)
-    cp(a("CO"), ind(a("CA"), a("el")))
-    ts(blk("Cc", 0), a("CO"), float(-CEN), A.add)
-    act(a("Mf"), nG, F.Relu, col(KF), -3584.0)
-    tt(a("Wf"), WP, a("Mf"), A.add)
-    ts(a("Mn"), nG, col(KK), A.is_equal)
-    act(a("Mz"), a("Mn"), F.Identity, 1.0, -1.0)
-    tt(a("Wz"), WP, a("Mz"), A.mult)
+def cands(h, tab, lst, hs):
+    co = a("CO", 256 * h + 128 * hs[0], 256 * h + 128 * hs[1])
+    ts(co, ind(a(tab), a(lst, 8 * hs[0], 8 * hs[1])), float(CEN * h), A.add)
+    ts(a("Cc", 128 * hs[0], 128 * hs[1]), co, float(-CEN), A.add)
+    flip("PT", "Cc", 16 * h, hs)
+
+
+def paths():
+    act(a("de"), t3("PW", (0, 16), (0, 16, 2)), F.Identity, 1700.0 * 64, -64.0)
+    scan(a("es"), a("de"), a("Wn", 0, 256, 2), 0.0, A.max, A.min)
+    cp(a("DL", 0, 256, 16), a("es", 7, 128, 8))
+    ts(a("el"), t3(tolist(0, 256), 0), float(CEN), A.add)
+    scan(a("en"), a("de"), a("KN"), 0.0, A.max, A.min)
+    bk = dbank()
     for z in range(2):
-        pe([(blk("P1", 1 + z, 128), blk("PZ", 2 * z + u, 128), a("Wz", u, 256, 2), u == 0, u == 1) for u in range(2)])
-    ts(a("WO"), a("P1", 128, 384), float(CEN), A.add)
-
-
-def fit(rows, cc, ns=0):
-    pe([(a("P0", 0, 256), I_, a("KH"), True, False)])
-    rows = list(rows)
-    for j in range(0, ns, 2):
-        bk = sbank("34")
-        pe([m for u in range(2) for m in ((blk(bk, u), blk("SEL", rows[j + u], 128), a("Wf"), True, False), (blk(bk, u), a("nIh"), cc, False, True))])
-        act(blk("junk", j // 2, 512), a(bk), F.Abs)
-        act(blk("EQ", j // 2, 512), blk("junk", j // 2, 512), F.Relu, 1.0, -1.0)
-        pe([(blk("P0", h, 128), blk("EQ", 2 * (j + u) + h, 128), a("PENI"), False, False) for u in range(2) for h in range(2)])
-    for j, k in list(enumerate(rows))[ns:]:
-        bk = "P7" if j % 2 == 0 else "P6"
-        pe([(a(bk, 0, 256), blk("SEL", k, 128), a("Wf"), True, True)])
-        tt(blk("EQ", j), a(bk, 0, 256), cc, A.is_equal)
-        pe([(blk("P0", h, 128), blk("EQ", 2 * j + h, 128), a("PENI"), False, False) for h in range(2)])
-
-
-def gather(eng, out, src):
-    return cp(out, src) if eng == "V" else act(out, src, F.Copy)
-
-
-def hop(win, co, cc, nv, xv, sb, y, lout):
-    for u in range(0, 256, GC):
-        gather("V" if u < nv or u >= 256 - xv else "S", a("XC", 16 * u, 16 * (u + GC)), ind(win, a(co, u, u + GC)))
-    xe = a("P2", 384, 384 + nv)
-    if nv:
-        pe([(xe, I_, a("xs", 0, nv), True, True)])
-    l0 = nv
-    while l0 < 256:
-        l1 = min(256, (l0 // 64 + 1) * 64)
-        w = l1 - l0
-        ni = 512 // w
-        for i0 in range(0, 16, ni):
-            bk = sbank(sb)
-            ml = []
-            for i in range(i0, i0 + ni):
-                o = blk(bk, i - i0, w)
-                ml += [(o, I_, a("XC", 16 * l0 + i, 16 * l1, 16), True, False), (o, a("nIb"), a("xs", l0, l1), False, True)]
-            pe(ml)
-            act(m3(i0, i0 + ni, l0, l1), a(bk), F.Abs, 0.0, 0.5)
-        l0 = l1
-    if nv:
-        for i in range(16):
-            tt(m3(i, i + 1, 0, nv), a("XC", i, 16 * nv, 16), xe, A.max)
-        pe([(a("P0", 0, 128, p=(0, nv)), a("xs", 0, nv), a("nB16"), False, False)]
-           + [(a("P0", i, 128, 16, p=(0, nv)), a("XC", i, 16 * nv, 16), Bm16, False, False) for i in range(16)])
-    pe([(a("P0", 128 + i, 256, 16), m3(i, i + 1, 128, 256), B32, False, False) for i in range(16)])
-    pe([(a("P0", i, 128, 16), m3(i, i + 1, 0, 128), B32, False, i == 15) for i in range(16)])
-    key = a("P0", 0, 256)
-    scan(blk("pm", 0), blk("RST", 0), key, 0.0, A.add, A.min)
-    scan(rev("km", 0, 256), blk("RST", 0), rev("pm", 0, 256), 0.0, A.add, A.min)
-    tt(blk("OH", 0), key, a("km"), A.is_equal)
-    pe([(blk("P2", h, 128), blk("OH", h, 128), I_, True, True) for h in range(2)])
-    tt(a(y), a("P2", 0, 256), cc, A.mult)
-    if lout is not None:
-        pe(tolist(256, 0, y))
-        ts(lout, a("P2", 256, 272), float(CEN), A.add)
-
-
-def edges(r):
-    for j, l0 in enumerate(range(0, 256, GC)):
-        gather(EV[r][j], a("VV", 16 * l0, 16 * (l0 + GC)), ind(OWND if l0 < 128 else PARD, a("WO", l0, l0 + GC)))
-    row = lambda h, k: a("VV", 2048 * (k & 1) + 1024 * h + k // 2, 2048 * (k & 1) + 1024 * h + 1024, 8)
-    if r > 0:
-        pe([(a("P7", 0, 256), I_, blk("KI", 0), True, False)]
-           + [(a("P7", 128 * h + k, 128 * h + 128, 16), row(h, k), B1 if k & 1 else Bm1, False, h == 1 and k == 14) for h in range(2) for k in range(15)])
-        scan(blk("pm", 1), blk("RST", 0), a("P7", 0, 256), 0.0, A.add, A.min)
-        ts(sm(JJ), a("pm", 256 + 15, 512, 16), 16391.5, A.add, 16.0, A.min)
-        tt(sm(CUT), sm(JJ), sm(NL), A.is_lt)
-        act(sm(E1), sm(JJ), F.Identity, -0.25, 0.5)
-        ts(sm(FL), sm(E1), M1, A.add, M1, A.subtract)
-        act(sm(E2), sm(FL), F.Identity, 2.0, 2.0)
-        tt(sm(S_), sm(E2), sm(CUT), A.mult)
-        tt(sm(CE), sm(JJ), sm(FL), A.subtract)
-        act(sm(E3), sm(CE), F.Relu, -1.0, 2.0)
-        tt(sm(PRE), sm(E3), sm(CUT), A.mult)
-        act(a("D1", 0, 256, 16), sm(PRE), F.Identity, -1.0)
-        act(a("D1", 512, 768, 16), sm(S_), F.Copy)
-        cp(a("si", 0, 16), sm(S_))
-        for j in range(3):
-            ts(blk("si", j + 1, 16), a("si", 0, 16), 2 << j, A.bitwise_and)
-        tt(sm(NS), sm(NL), sm(S_), A.subtract)
-        tt(sm(QQ), sm(PRE), sm(NS), A.subtract)
-        act(sm(W0), sm(QQ), F.Relu, 0.0, -BIG)
-        act(sm(W1), sm(QQ), F.Relu, BIG, BIG)
-        act(sm(W2), sm(QQ), F.Relu, 2 * BIG, -BIG)
-        act(sm(W3), sm(QQ), F.Relu, -BIG, BIG)
-        tt(sm(E4), sm(K1), sm(W3), A.add)
-        act(sm(E5), sm(NS), F.Relu, 0.0, -BIG)
-        tt(sm(E5), sm(E5), sm(W3), A.add)
-        act(sm(E6), sm(NL), F.Identity, -7.5)
-        tt(sm(C2), sm(E5), sm(E6), A.add)
-    act(a("D1", 256, 512, 16), sm(NL), F.Identity, -1.0)
-    c0, c1 = (0, 768) if r > 0 else (256, 512)
-    js = (0, 1, 2) if r > 0 else (1,)
-    scan(a("U", c0, c1), a("NST", c0, c1), a("D1", c0, c1), 0.0, A.mult, A.add)
-    act(a("PN", c0, 512), a("U", c0, 512), F.Relu, BIG, -BIG)
-    if r > 0:
-        act(blk("PN", 2), blk("U", 2), F.Relu, 0.0, BIG)
-    pe([(a("P1"), I_, a("KI"), True, False)])
-    for h in range(2):
-        for k0 in range(0, 14, 4):
-            bk = sbank(SB3)
-            ks = range(k0, min(k0 + 4, 14))
-            ml = []
-            for k in ks:
-                o = blk(bk, k - k0, 128)
-                ml += [(o, I_, row(h, k), True, False), (o, a("nIb"), row(h, k + 1), False, True)]
-            pe(ml)
-            act(blk("ED", 14 * h + k0, 128, 0, 128 * len(ks)), a(bk, 0, 128 * len(ks)), F.Abs)
-            pe([(a("P1", 256 * h + k, 256 * h + 256, 16), blk("ED", 14 * h + k, 128), a("BB", 48, 64), False, False) for k in ks])
-    pe([(blk("P1", 2 * h + min(j, 1), 128), I_, blk("PN", 2 * j + h, 128), False, h == 1 and j == js[-1]) for h in range(2) for j in js])
-    if r == 0:
         for h in range(2):
-            scan(blk("pm", h, 128), a("RST", 0, 128), blk("P1", 2 * h + 1, 128), 0.0, A.add, A.min)
+            cp(a("ZW", 128 * (2 * z + h) + h, 128 * (2 * z + h) + 128, 2), a("Wn", 128 * h + z, 128 * h + 128, 2))
+    pe([(t3(bk, (8 * z, 8 * z + 8)), blk("ZW", 2 * z + h, 128), a("Ih"), h == 0, h == 1) for z in range(2) for h in range(2)])
+    for z in range(2):
+        ts(blk("WO", z, 128), t3(bk, (8 * z, 8 * z + 8)), float(CEN), A.add)
+    for nm, z, n in (("WXo", 1, 6), ("WXe", 0, 7)):
+        act(t3(nm, None, (0, n)), t3("PW", (0, 16), (z, z + 2 * n, 2)), F.Copy)
+        act(t3(nm, None, (n, 2 * n)), t3(nm, None, (0, n)), F.Copy)
+        act(t3(nm, None, (2 * n, 4 * n)), t3(nm, None, (0, 2 * n)), F.Copy)
+    cands(0, "CA", "el", (0, 2))
+
+
+def fit(h, hs):
+    for H in range(*hs):
+        pe([(a(KK[H], 0, 128), I_, a("KH", 0, 128), True, False)])
+    for s in range(6 + h):
+        tt(a("EQ", 256 * s + 128 * hs[0], 256 * s + 128 * hs[1]), t3("PT", (16 * h + 8 * hs[0], 16 * h + 8 * hs[1])),
+           t3(("WXo", "WXe")[h], (8 * hs[0], 8 * hs[1]), (s, s + 16)), A.is_equal)
+        pe([(a(KK[H], 0, 128), a("PENI"), blk("EQ", 2 * s + H, 128), False, False) for H in range(*hs)], True)
+
+
+def hop(h, H, win, nv):
+    for j in range(4 * H, 4 * H + 4):
+        gather(blk("XC", j, 512), ind(win, blk("CO", 8 * h + j, 32)))
+    xs, xc, mm = blk("xs", 2 * h + H, 128), lambda i: a("XC", 2048 * H + i, 2048 * H + 2048, 16), lambda i: blk("MM", 16 * H + i, 128)
+    key = lambda i: a(KK[H], i, 128, 16)
+    if nv:
+        pe([(a(KK[H], 0, 128), xs, blk("nB", nv, 128), False, False)] + [(key(i), xc(i), Bm16, False, False) for i in range(nv)], True)
+        for i0 in range(0, nv, XS):
+            xe = t3(dbank(), (0, 8))
+            pe([(xe, I_, xs, True, True)])
+            for i in range(i0, min(nv, i0 + XS)):
+                tt(mm(i), xc(i), xe, A.max)
+            pe([(key(i), mm(i), B32, False, False) for i in range(i0, min(nv, i0 + XS))], True)
+    for i0 in range(nv, 16, 4):
+        bk, js = dbank(), range(i0, min(16, i0 + 4))
+        o = lambda i: t3(bk, (8 * (i - i0), 8 * (i - i0) + 8))
+        pe([m for i in js for m in ((o(i), I_, xc(i), True, False), (o(i), a("nIb"), xs, False, True))])
+        act(blk("MM", 16 * H + i0, 128, 0, 128 * len(js)), t3(bk, (0, 8 * len(js))), F.Abs, 0.0, 0.5)
+        pe([(key(i), mm(i), B32, False, False) for i in js], True)
+    pe([(a(KK[H], 0, 16), I_, ZERO, False, True)])
+    key, pm, eq, ne, y = a(KK[H], 0, 128), blk("pm", 2 * h + H, 128), blk("eq", H, 128), blk("eq", 2 + H, 128), blk("Y", H, 128)
+    scan(pm, a("RST", 0, 128), key, 0.0, A.add, A.min)
+    tt(eq, key, pm, A.is_equal)
+    lin(ne, eq, -1.0, 1.0)
+    tt(y, t3("PT", (16 * h + 8 * H, 16 * h + 8 * H + 8)), eq, A.mult)
+    scan(blk("YS", 2 * h + H, 128), ne, y, 0.0, A.mult, A.add)
+
+
+def row(h, k, nm="VV"):
+    return a(nm, 2048 * (k & 1) + 2 * (k // 2) + h, 2048 * (k & 1) + 2048, 16)
+
+
+def rows(r):
+    for j in range(8):
+        gather(blk("VV", j, 512), ind(OWNN if j < 4 else PARN, blk("WO", j, 32)))
+    if r > 0:
+        pe([(a("PE", 0, 256), I_, a("K16"), True, False)]
+           + [(a("PE", 128 * h + k, 128 * h + 128, 16), row(h, k), Bm16, False, False) for h in range(2) for k in range(0, 16, 2)])
+        pe([(a("PE", 128 * h + k, 128 * h + 128, 16), row(h, k), B16, False, h == 1 and k == 15) for h in range(2) for k in range(1, 16, 2)])
+        scan(a("pd", 8, 264), a("RST"), a("PE", 0, 256), 0.0, A.add, A.min)
+
+
+def cut():
+    jj, ub = a("pd", 23, 264, 16), a("G1", 14, 256, 16)
+    act(a("RF", 1, 256, 2), a("pd", 12, 268, 2), F.Relu, -4 * OFF, -4.0)
+    act(a("RB", 0, 256, 2), a("pd", 5, 261, 2), F.Relu, 4 * OFF, 4.0)
+    act(a("RB", 2, 256, 16), a("K16", 0, 16), F.Identity, BIG, 0.0)
+    act(sb(PF_), a("pd", 10, 264, 16), F.Relu, -4 * OFF, -4.0)
+    act(a("PQ", 0, 129), a("pd", 8, 266, 2), F.Identity, -OFF / 32, -1.0 / 32)
+    act(sm(NQ), NL, F.Identity, -0.5 - 2 * OFF, 0.5)
+    act(sm(NJ), NL, F.Identity, -2 * OFF)
+    tt(sm(QQ), jj, sm(NQ), A.subtract)
+    act(sm(W0), sm(QQ), F.Relu, 0.0, -BIG)
+    act(sm(W1), sm(QQ), F.Relu, BIG, BIG)
+    act(sm(W2), sm(QQ), F.Relu, BIG, -BIG)
+    act(sm(W3), sm(QQ), F.Relu, 0.0, BIG)
+    ts(ub, sm(QQ), 0.5, A.is_lt)
+    ts(a("G1", 15, 256, 16), sm(QQ), 0.0, A.is_equal, -1.0, A.mult)
+    act(sm(E1), jj, F.Identity, OFF - 0.25, 0.5)
+    ts(sm(FL), sm(E1), M1, A.add, M1, A.subtract)
+    act(sm(S_), sm(FL), F.Identity, 2.0, 2.0)
+    tt(sm(US), ub, sm(S_), A.mult)
+    tt(sb(POS), NL, sm(US), A.subtract)
+    tt(sm(U1), sm(NJ), jj, A.subtract)
+    tt(sm(U1), sm(U1), sm(QQ), A.min)
+    act(sb(PI), sm(U1), F.Relu, 0.0, BIG)
+    act(sb(NEG), sb(POS), F.Relu, 0.0, -BIG)
+    pg = slot()
+    group(pg, [(I_, sb(x)) for x in (CK, POS, PI)])
+    act(a("G1", 270, 512, 16), pg, F.Identity, 13.5 - K0, -1.0)
+    act(sm(FH), sm(FL), F.Identity, 0.0, 0.5)
+    ts(a("DM", 256, 512, 16), sm(FL), 2.0, A.is_ge)
+    tt(a("DM", 0, 256, 16), sm(FH), a("DM", 256, 512, 16), A.subtract)
+    act(a("DM", 512, 768, 16), sm(FL), F.Identity, -55296.0, 8192.0)
+    scan(a("UM"), a("NST"), a("DM"), 0.0, A.mult, A.add)
+    sa = lambda d: [(a("Ih"), a("Wn", d, d + 256)), (blk("I2", 0, 128), t3("TA", None, (d + 2, d + 18))), (blk("I2", 1, 128), t3("TA", None, (d, d + 16)))]
+    tt(t3("TA", None, (0, 16)), WP, blk("UM", 0), A.mult)
+    group(WB, sa(0))
+    tt(t3("TB", None, (0, 16)), WB, blk("UM", 1), A.mult)
+    group(WB, sa(2) + [(a("Ih"), t3("TB", None, (6, 22))), (a("nIh"), t3("TB", None, (2, 18)))])
+    tt(a("Wb"), WB, blk("UM", 2), A.max)
+    for z in range(2):
+        tt(a("Wf", z, 256, 2), t3("PW", (0, 16), (z, 16, 2)), a("PQ", z, z + 128), A.max)
+    ec = a("es", 7, 128, 8)
+    ts(sm(NW), ec, float(V - ST - CEN), A.is_ge, float(-V), A.mult)
+    tt(sm(NW), sm(NW), ec, A.add)
+    act(sm(PN), sb(POS), F.Identity, ST + 4096.0, 4096.0)
+    tt(sm(NW), sm(NW), sm(PN), A.add)
+    tt(a("Wf", 0, 256, 16), a("Wf", 0, 256, 16), sm(NW), A.min)
+    w15 = t3("PW", (16, 32), 15)
+    pe([(WB, a("Ih"), a("Wb"), True, False), (WB, a("nIh"), a("Wf"), False, False), (w15, a("nIh"), a("Wb", 15, 256, 16), False, False),
+        (w15, a("Ih"), a("Wf", 15, 256, 16), False, True)])
+
+
+def edges(r, t):
+    if t == 0:
+        pe([(a("PE", 0, 256), I_, a("KI"), True, False)])
+        if r > 0:
+            pe([(a("PE", z, 256, 16), I_, sb(PF_), False, False) for z in range(2)], True)
+    key = lambda h, k: a("PE", 128 * h + k, 128 * h + 128, 16)
+    hk = [(h, k) for h in range(2) for k in range(t, 14, 2)]
+    if EA[r][t] == "S":
+        for j0 in range(0, 14, 4):
+            bk, js = dbank(), list(enumerate(hk[j0:j0 + 4]))
+            o = lambda j: t3(bk, (8 * j, 8 * j + 8))
+            pe([m for j, (h, k) in js for m in ((o(j), I_, row(h, k), True, False), (o(j), a("nIb"), row(h, k + 1), False, True))])
+            act(blk("ED", 16 * t + j0, 128, 0, 128 * len(js)), t3(bk, (0, 8 * len(js))), F.Abs)
+            pe([(key(h, k), blk("ED", 16 * t + j0 + j, 128), B16, False, False) for j, (h, k) in js], True)
     else:
-        scan(a("pe"), a("RST"), a("P1"), 0.0, A.add, A.min)
-        for h in range(2):
-            kf, kb = a("pe", 256 * h + 15, 256 * h + 128, 16), a("pe", 256 * h + 143, 256 * h + 256, 16)
-            for w, k in ((W0, kf), (W1, kb), (W2, kf), (W3, kb)):
-                tt(sm(w, 8, 8 * h), k, sm(w, 8, 8 * h), A.add)
-        tt(sm(KEY0), sm(W0), sm(W1), A.min)
-        tt(sm(E4), sm(E4), sm(W2), A.min)
-        tt(sm(KEYX), sm(E4), sm(W3), A.min)
+        for z in range(2):
+            pe([(key(h, k), row(h, k + z), Bm16, False, False) for h, k in hk], True)
+        for c in range(4 * (t == 0 or EA[r][0] == "S")):
+            bk = dbank()
+            pe([(t3(bk), I_, blk("VV", 4 + c, 512), True, True)])
+            for u in ((0, 1) if EA[r] == "VV" else (t,)):
+                tt(blk("ED", 4 * u + c, 512), blk("VV", c, 512, 2 * u, 512), t3(bk), A.max)
+        pe([(key(h, k), row(h, k, "ED"), B32, False, False) for h, k in hk], True)
 
 
-def bcast(qs):
-    p = (0, 96)
-    pe([(a("P0", 384, 512, p=p), a("Q"), I_, True, True)])
-    act(a("QT", p=p), a("P0", 384, 512, p=p), F.Copy)
-    for bk, js in (("P1", [j for j in qs if j >= 2]), ("P0", [j for j in qs if j < 2])):
-        if js:
-            b = lambda j, h: 16 * (16 * (0, 1, 2, 5)[j] + 8 * h)
-            pe([(blk(bk, 2 * (j % 2) + h, 128), a("L2", b(j, h), b(j, h) + 128, p=p), a("QT", p=p), True, True) for j in js for h in range(2)])
-            for j in js:
-                act(blk("GB", j), blk(bk, j % 2), F.Identity, 0.0, (0.5, 0.25, 0.125, 1.0)[j])
+def pick(z, c):
+    return a("PE", 256 + 80 * z + c, 336 + 80 * z, 5)
+
+
+def ends(r):
+    pe([(a("PE", 0, 16), I_, ZERO, False, True)])
+    if r == 0:
+        scan(a("pe", 0, 256), a("RST"), a("PE", 0, 256), 0.0, A.add, A.min)
+        ks, nv = a("pe", 15, 256, 16), 1
+    else:
+        scan(rev("pe", 0, 256), rev("RF", 0, 256), rev("PE", 0, 256), 0.0, A.add, A.min)
+        scan(a("pe", 241, 497), a("RB"), a("PE", 0, 256), 0.0, A.add, A.min)
+        for z in range(2):
+            tt(sm(X0 + 2 * z, 32), a("pe", 0, 512, 16), sm(W0 + 2 * z, 32), A.add)
+            tt(sm(KZ + z), sm(X0 + 2 * z), sm(X1 + 2 * z), A.min)
+        tt(sm(KX), sm(KO), sm(BND), A.min)
+        tt(sb(WEF), sm(U3), sm(KX), A.is_lt)
+        tt(sm(KX), sm(KX), sm(U3), A.min)
+        ks, nv = sm(KZ, 32), 2
+    ts(sm(T1_, 16 * nv), ks, M16, A.add, M16, A.subtract)
+    tt(a("DK", 0, 256 * nv, 16), sm(T1_, 16 * nv), ks, A.subtract)
+    tt(a("sb", 16 * NP_, 16 * (NP_ + nv)), ks, sm(BND, 16 * nv), A.is_ge)
+    scan(a("UK", 0, 256 * nv), a("NST", 0, 256 * nv), a("DK", 0, 256 * nv), 0.0, A.mult, A.add)
+    ts(a("OH", 0, 256 * nv), a("UK", 0, 256 * nv), M2, A.add, M2 + 8, A.is_equal)
+    for v in range(nv):
+        tt(blk("YE", v), WP, blk("OH", v), A.mult)
+    for z in range(2):
+        scan(blk("YA", z, 256, 0, 128 * nv), a("NS8", 0, 128 * nv), a("YE", z, 256 * nv, 2), 0.0, A.mult, A.add)
+    ya = lambda z, v: a("YA", 256 * z + 128 * v + 7, 256 * z + 128 * v + 128, 8)
+    ml = [(a("PE", 256, 416), a("PENI"), blk("R1", int(r > 0), 160))]
+    for z in range(2):
+        ml += [(pick(z, 1), a("Ih"), ya(z, 0)), (pick(z, 1), a("PENI"), sb(NP_))]
+        if r:
+            ml += [(pick(z, 0), a("Ih"), ya(z, 1)), (pick(z, 0), a("PENI"), sb(NP2)), (pick(z, 0), a("PENI"), sb(WEF)), (pick(z, 2), a("nPEN"), sb(WEF)),
+                   (pick(z, 2), a("Ih"), a("YS", 15, 256, 16) if z else a("es", 7, 128, 8))]
+    if r:
+        ml += [(pick(1, 3), a("Ih"), a("YS", 15, 256, 16))]
+    pe([(a("PE", 256, 416), a("Ih"), a("RC"), True, False)] + [m + (False, r == 0 and i == len(ml) - 1) for i, m in enumerate(ml)])
 
 
 def program():
@@ -520,203 +630,409 @@ def program():
     for i in range(NCH):
         ss.append(op("G", (lambda i: lambda g, T, c: c["big"]("X", i))(i), [blk("X", i, CW)], [], 1500 if i == 0 else RI, track=False))
         ss[-1]["prio"] = 1e9
-    left = op(None, None, [OWN], [], 0, tok=("ls0", None), lat=5000, after=ss)
+    left = op(None, None, [a("X", 0, V)], [], 0, tok=("ls0", None), lat=5000, after=ss)
     for i in range(NCH):
         load("Y", blk("CA", i, CW), (lambda i: lambda T: T.cand[:, CW * i:CW * i + CW])(i), "lk%d" % i, 3000 + 1500 * i)["after"].append(left)
     op(None, None, [], [PAR], 0, tok=("xarr", None), lat=8000, after=ss)
     for i in range(NCH):
-        cp(blk("CU", i, CW), blk("CA", i, CW))
+        ts(blk("CU", i, CW), blk("CA", i, CW), float(-CEN), A.add)
         sc = op("G", (lambda i: lambda g, T, c: c["big"]("C", i))(i), [blk("CU", i, CW), PAR], [], RI, track=False, after=ss)
         op(None, None, [], [blk("CQ", i, CW)], 0, tok=("ca%d" % i, None), lat=13000 + 1000 * i, after=[sc])
-        for j in range(2):
-            cp(blk("CP", 2 * i + j, CW // 2), blk("CQ", 2 * i + j, CW // 2))
+    for i in range(2 * NCH):
+        gather(blk("XF", i, CW // 2), blk("X", i, CW // 2))
     consts()
-    ts(a("Wa"), a("wi"), float(-CEN), A.add, col(M15), A.mult)
-    ts(a("TT"), a("Li"), float(CEN), A.add, col(IS15), A.mult)
-    pe([(WP, a("Ih"), a("Wa"), True, False), (WP, a("Ih"), a("TT"), False, True)])
-    cp(a("Wn"), WP)
+    for j in range(2 * NCH):
+        bk = t3(dbank(), (0, CW // 32))
+        pe([(bk, a("Ih"), blk("CQ", j, CW // 2), True, True)])
+        gather(blk("CP", j, CW // 2), bk)
     p8 = (0, 8)
-    cp(a("cb", p=p8), a("ci", p=p8))
-    ts(a("tf", p=p8), a("ti", p=p8), 16.0, A.mult, -8.0, A.add)
-    pe([(a("P0", 0, 256), a("L2", 0, 128, p=p8), a("cb", p=p8), True, True)])
-    act(blk("GB", 3), a("P0", 0, 256), F.Copy)
-    pe([(blk("P2", h, 8), a("cb", 128 * h, 128 * h + 128, p=p8), a("IL", 16, 24, p=p8), True, True) for h in range(2)]
-       + [(blk("P2", 2 + h, 8), a("tf", 128 * h, 128 * h + 128, p=p8), a("I32", 0, 8, p=p8), True, True) for h in range(2)])
-    cp(sm(NL), a("P2", 0, 16))
-    cp(sm(TH16), a("P2", 16, 32))
-    cp(sm(BND), a("P2", 16, 32))
-    post_cut()
-    edges(0)
+    ts(a("Cc"), a("wi"), float(-CEN), A.add)
+    flip("PW", "Cc")
+    cp(a("cth", 0, 256, p=p8), a("ci", p=p8))
+    ts(a("cth", 256, 512, p=p8), a("ti", p=p8), 16.0, A.mult, -8.0, A.add)
+    pe([(blk("KA", j, 8), a("cth", 128 * j, 128 * j + 128, p=p8), a("I32", 0, 8, p=p8), True, True) for j in range(4)])
+    act(a("DM", 512, 768, 16), a("KA", 0, 16), F.Identity, 2048.0, -4096.0)
+    for z in range(2):
+        act(sm(BND + z), a("KA", 16, 32), F.Copy)
+        act(sm(TH16 + z), a("KA", 16, 32), F.Identity, 128 * 15.5)
+    scan(blk("UM", 2), blk("NST", 0), blk("DM", 2), 0.0, A.mult, A.add)
+    tt(a("Wf"), WP, blk("UM", 2), A.max)
+    ts(WN, a("Wf"), float(NUL - CEN), A.min)
+    pe([(WP, a("Ih"), WN, True, True)])
+    paths()
+    rows(0)
+    edges(0, 0)
+    edges(0, 1)
+    ends(0)
     for r in range(RO):
         last = r == RO - 1
-        ks = a("pm", 15, 256, 16) if r == 0 else sm(KS)
-        ts(sm(T1_), ks, M16, A.add, M16, A.subtract)
-        tt(sm(NP_), ks, sm(BND), A.is_ge)
-        tt(sm(T2_), ks, sm(T1_), A.subtract)
-        ts(sm(T3_), sm(NP_), 16.0, A.mult, -8.5, A.add)
-        tt(a("D3", 0, 256, 16), sm(T2_), sm(T3_), A.max)
-        scan(a("U3"), blk("NST", 0), a("D3"), 0.0, A.mult, A.add)
-        ts(blk("OH", 0), a("U3"), -8.5, A.is_ge)
-        ts(blk("OH", 1), a("U3"), -6.5, A.is_ge)
-        pe([(blk("P2", h, 128), blk("OH", 2 * z + h, 128), a("nIb") if z else I_, z == 0, z == 1) for h in range(2) for z in range(2)])
-        tt(a("Ye"), a("P2", 0, 256), a("Wn"), A.mult)
-        for z, bk in ((1, "P3"), (0, "P6")):
-            pe(tolist(0, 1 + z, "Ye", bk))
-            ts(blk("ab", z, 16), a(bk, 0, 16), float(CEN), A.add)
-        cp(a("abf"), a("ab"))
+        SEEN.clear()
+        scan(a("ra"), a("RS5"), a("PE", 256, 416), 0.0, A.add, A.min)
+        cp(a("DL", 512, 1024, 16), a("ra", 4, 160, 5))
+        bk = t3(tolist(512, 512), (0, 2))
+        ts(a("ab"), bk, float(CEN), A.add)
+        lin(a("abf"), bk, 1.0, float(CEN))
         if r > 0:
-            tt(sm(C1), sm(NS), sm(GO2), A.add)
-            tt(sm(MM_), sm(C1), sm(PRE), A.max)
-            tt(sm(C3), sm(QQ), sm(GO2), A.is_lt)
-            for j in range(3):
-                tt(blk("Q", j, 16), blk("si", j + 1, 16), sm(C3), A.mult)
-            ts(blk("Q", 3, 16), sm(MM_), 0.0, A.is_equal)
-            pe([(a("P0", 368 + 8 * h, 376 + 8 * h), blk("Wn", h, 128), a("B2", 16, 24), True, True) for h in range(2)])
-            ts(sm(C5), a("P0", 368, 384), float(V - ST - CEN), A.is_ge)
-            tt(blk("Q", 4, 16), sm(C5), blk("Q", 3, 16), A.mult)
-            ts(sm(NL), sm(MM_), 1.0, A.max)
-            act(blk("Q", 5, 16), sm(NL), F.Copy)
-            bcast([0, 1, 2, 3])
-            new = [(blk("P5", h, 128), a("SELN", 128 * h, 128 * h + 128, p=(0, 96)), a("QT", p=(0, 96)), False, False) for h in range(2)]
-            for j in (2, 1, 0):
-                tt(blk("TS", j), WP, blk("GB", j), A.mult)
-                pe([(WP, a("Ih"), a("Wn"), True, False)] + (new if j == 0 else [])
-                   + [(WP, blk("DS", u, 128), blk("TS", u), False, u == j) for u in range(2, j - 1, -1)])
-            OPS[-1]["prio"] = PB
-            post_cut()
-        for z in (1, 0):
+            paths()
+        for z in range(2):
             tt(blk("RR", z), ind(a("CT"), blk("ab", z, 16)), blk("CR", z), A.add)
             for gm in range(2):
-                if (z, gm) in LLV:
-                    ts(blk("LL", 2 * gm + z), blk("RR", z), col(MA0 + gm), A.mult, col(MB0 + gm), A.add)
-                else:
-                    act(blk("LL", 2 * gm + z), blk("RR", z), F.Identity, col(MB0 + gm), col(MA0 + gm))
+                o, x = t3("LL", (4 * z, 4 * z + 4), (64 * gm, 64 * gm + 64)), blk("RR", z)
+                either(ts(o, x, col(MK + gm), A.mult, col(MK + 2 + gm), A.add), act(o, x, F.Identity, col(MK + 2 + gm), col(MK + gm)))
         mid, rmid = blk("mid", r), blk("rmid", r)
-        act(a("xa"), ind(OWND, blk("ab", 0, 16)), F.Identity, col(CM5))
-        tt(a("xb"), ind(PARD, blk("ab", 1, 16)), a("xa"), A.add)
-        ts(a("m2"), a("xb"), M2, A.add, M2, A.subtract)
-        act(mid, a("m2"), F.Identity, 0.0, 0.5)
+        for z in range(2):
+            gather(blk("xm", z), ind((OWND, PARD)[z], blk("ab", z, 16)))
+        bk = t3(dbank(), (0, 16))
+        group(bk, [(I_, blk("xm", 0)), (I_, blk("xm", 1)), (I_, blk("CC", 3))])
+        act(a("xc"), bk, F.Identity, M2)
+        act(mid, a("xc"), F.Identity, -0.5 * M2, 0.5)
 
         def e(g, T, c, r=r, mid=mid, rmid=rmid):
-            g.remote_dma(mk(T, rmid), mk(T, mid), T.sem["am%d" % r], T.sem.ls1, c["p"]["pid"], c["p"]["rid"], c["p"]["m8"])
-            c["ls1"][0] += c["ne"]
+            c["one"](mk(T, rmid), mk(T, mid), "am%d" % r)
         s = op("G", e, [mid], [], RI, track=False)
-        s["prio"] = 1500.0
         op(None, None, [], [rmid], 0, tok=("am%d" % r, None), lat=RL + 2000, after=[s])
-        vb = [0, 0]
-        for g_ in range(8):
-            pp = (32 * (g_ // 2), 32 * (g_ // 2) + 32)
-            for z in range(2):
-                onv = z == 0 and g_ < VG
-                vb[onv] += 1
-                bk = "P" + (VB[onv][vb[onv] % len(VB[onv])])
-                b = 512 * (g_ % 2) + 256 * z
-                pe([(a(bk, 0, 128), a("LL", b, b + 128, p=pp), a("RR", 256 * z, 256 * z + 128, p=pp), True, True),
-                    (a(bk, 128, 384), a("LL", b + 128, b + 256, p=pp), a("RR", 256 * z, 256 * z + 256, p=pp), True, True)])
-                for h in range(2):
-                    src = a(bk, 128 * h, 128 + 256 * h)
-                    if onv:
-                        red(sm(MA, 1, 8 * h + g_), src, A.max)
-                    else:
-                        act(blk("junk", 2 * (vb[0] % 3) + h, 256, 0, 128 + 128 * h), src, F.Relu, col(VB0 + h), 1.0, sm((MA, CB)[z], 1, 8 * h + g_))
-        tt(sm(T4_), sm(MA), a("thr"), A.add)
-        tt(sm(T5_), sm(T4_), sm(CB), A.max)
-        for h in range(2):
-            ts(a("D2", 128 * h, 128 * h + 128, 16), sm(T5_, 8, 8 * h), 0.0, A.is_gt, col(DU0 + h), A.mult)
-        scan(a("T1"), a("DA"), a("D2"), 0.0, A.mult, A.add)
-        scan(a("T2"), a("D2"), a("DB"), 0.0, A.add, A.mult)
-        pe([(a("P2", 320, 352), I_, a("negL"), True, False)]
-           + [(blk("P2", 40 + 2 * z + h, 8), blk(t, h, 128), blk("B2", s, 8), False, z + h + s == 3)
-              for z in range(2) for h in range(2) for s, t in enumerate(("T1", "T2"))])
-        tt(a("ef"), a("P2", 320, 352), a("abf"), A.max)
+        nv = ns = 0
+        for b in range(15, -1, -1):
+            n, pp = 64 * (b // 4 + 1), (32 * (b % 4), 32 * (b % 4) + 32)
+            if VQ[b] == "V":
+                nv += 1
+                bk = ("PE", "KA", "KB")[nv % 3]
+                part = lambda c0, c1: a(bk, c0, c1)
+            else:
+                ns += 1
+                bk = dbank()
+                part = lambda c0, c1: t3(bk, (c0 // 16, c1 // 16))
+            pe([(part(n * z, n * z + n), t3("LL", 4 * z + b // 4, p=pp), a("RR", 256 * z, 256 * z + n, p=pp), True, True) for z in range(2)])
+            if VQ[b] == "V":
+                red(sm(RED, 1, b), part(0, 2 * n), A.max)
+            else:
+                act(blk("junk", ns % 3, 512, 0, 2 * n), part(0, 2 * n), F.Relu, sm(VB, 1, b), 1.0, sm(RED, 1, b))
+        tt(a("DL", 1280, 1792, 32), sm(RED), sm(VT), A.is_gt)
+        bk = t3(tolist(1280, 512, 4), 0)
+        for z in range(2):
+            tt(blk("ef", z, 16), bk, blk("abf", z, 16), A.max)
         cp(blk("eff", r, 32), a("ef"))
         ea, eb, ra, rk = blk("eff", 2 * r, 16), blk("eff", 2 * r + 1, 16), blk("rl", 2 * r, 16), blk("rl", 2 * r + 1, 16)
 
         def e(g, T, c, r=r, ea=ea, eb=eb, ra=ra, rk=rk):
-            g.remote_dma_fused([RemoteDMATransfer(dst_ids=[DstId(rid=c[to]["rid"], pnc=c[to]["pid"])], dma_engine_mask=c[to][m],
-                                                  remote_sem=T.sem[sem % r], src=mk(T, x), dst=mk(T, y))
-                                for to, m, sem, x, y in (("p", "m4a", "aa%d", ea, ra), ("q", "m4b", "ak%d", eb, rk))], local_sem=T.sem.ls1)
-            c["ls1"][0] += c["ne"]
+            c["two"](mk(T, ra), mk(T, ea), "aa%d" % r, mk(T, rk), mk(T, eb), "ak%d" % r)
         s = op("G", e, [ea, eb], [], RI, track=False)
         op(None, None, [], [ra], 0, tok=("aa%d" % r, None), lat=RL, after=[s])
         op(None, None, [], [rk], 0, tok=("ak%d" % r, None), lat=RL, after=[s])
         if not last:
-            ts(a("wn"), a("ef", 0, 16), float(V), A.is_lt)
-            pe([(a("P1", 352, 368), a("ones"), a("wn"), True, True)])
-            act(a("junk", 0, 16), a("P1", 352, 368), F.Identity, 0.0, 1.0, col(AC))
-            cp(a("pi", 0, 1), col(AC))
-            ts(a("pi", 1, 2), a("pi", 0, 1), 31, A.bitwise_and)
-            ts(col(AC), a("pi", 1, 2), 128.0, A.mult)
-            act(sm(BND), sm(TH16), F.Identity, col(AC))
-        fit(range(1, 13, 2), blk("Cc", 0), FS)
+            act(a("wn", 0, 16), a("ef", 0, 16), F.Sign, V - 0.5, -1.0)
+            o = slot()
+            pe([(o, a("ones"), a("wn", 0, 16), True, True)])
+            act(sm(U2), o, F.Identity, (1024 - 15.5) / 16, 0.5, col(AC))
+            act(col(AD), col(AC), F.Identity, M1, 1.0 / 32)
+            act(col(AD), col(AD), F.Identity, 4096 * M1, -4096.0)
+            act(col(AC), col(AC), F.Identity, col(AD), 128.0)
+            act(sm(BND, 32), sm(TH16, 32), F.Identity, col(AC))
+        fit(0, (0, 2))
         cp(ind(OWND, ea), mid)
         cp(ind(PARD, ra), rmid)
         cp(ind(PARD, eb), a("DN"))
-        cp(ind(OWND, rk), a("DP"))
-        ts(a("xs"), ind(OWN, a("el")), 255.0, A.min)
+        x = ind(OWND, rk)
+        either(cp(x, a("DF")), op("S", lambda g, T, c, x=x: g.scalar.activation(mk(T, x), mk(T, a("DF")), F.Silu), [a("DF"), rk], [OWND],
+                                  65 + SCA * CY * 256))
+        hv = HVL if last else HV
+        ts(blk("xs", 0), ind(OWN, a("el")), 255.0, A.min)
         if not last:
-            pe([(a("P1", 368 + 8 * h, 376 + 8 * h), blk("xs", h, 128), B1, True, True) for h in range(2)])
-            act(sm(ED_), a("P1", 368, 384), F.Relu, -4079.0 * BIG, BIG)
-        fl = blk("fl", r, 16)
-        hop(PAR, "CO", blk("Cc", 0), NV1, XV1, SB1, "Y1", fl)
-        cp(a("rs"), ind(a("CP"), fl))
-        k1 = a("pm", 15, 256, 16)
-        act(sm(H1), k1, F.Relu, -16.0 * THR, 16.0)
-        act(sm(H2), sm(NL), F.Relu, -13.0 * BIG, BIG)
-        tt(sm(PEN1), sm(H1), sm(H2), A.add)
-        if not last:
-            act(sm(H4), sm(NL), F.Identity, -8.5)
-            tt(sm(H4), sm(H4), sm(ED_), A.add)
-            tt(sm(K1), k1, sm(H4), A.add)
-        ts(a("xs"), ind(PAR, fl), 0.0, A.max)
-        if not last:
-            edges(r + 1)
-        else:
-            for i in range(NCH):
-                ts(blk("XO", i, CW), blk("X", i, CW), 255.0, A.min)
+            bk = dbank()
+            pe([(t3(bk, 0, (8 * H, 8 * H + 8)), blk("xs", H, 128), Bm16, True, True) for H in range(2)])
+            act(sb(ED_), t3(bk, 0), F.Relu, -65200.0 * 4096, -4096.0)
+        for H in range(2):
+            hop(0, H, PAR, hv[0][H])
+            fl = a("fl", 8 * H, 8 * H + 8)
+            c0 = 256 + 768 * H
+            cp(a("DL", c0, c0 + 128, 16), a("YS", 128 * H + 15, 128 * H + 128, 16))
+            ts(fl, t3(tolist(c0, 128), 0, (0, 8)), float(CEN), A.add)
+            cands(1, "CP", "fl", (H, H + 1))
+            x = blk("xs", 2 + H, 128)
+            either(ts(x, ind(PAR, fl), 0.0, A.max), act(x, ind(PAR, fl), F.Relu))
+        k1, k2 = a("pm", 15, 256, 16), a("pm", 271, 512, 16)
+        act(sb(H1), k1, F.Relu, -16.0 * THR, 16.0)
+        act(sb(H2), NL, F.Relu, -13.0 * BIG, BIG)
+
+        def keys():
+            o = slot()
+            group(o, [(I_, NL), (a("nIb"), a("ones", 0, 16))] + [(I_, sb(x)) for x in (CK, PI, ED_)])
+            tt(sm(U3), o, k1, A.add)
+
+        def bounds():
+            if not last:
+                o = slot()
+                group(o, [(I_, NL)] + [(I_, sb(x)) for x in (CK, PI, NEG, H1, H2)])
+                lin(PC, o, 1.0)
+            o = slot()
+            group(o, [(a("nIb"), sb(H1)), (a("nIb"), sb(H2))])
+            lin(PTH, o, 1.0, THR)
+
+        def second(H):
+            if H == 0:
+                fit(1, (0, 2))
+            hop(1, H, OWN, hv[1][H])
+        if last:
+            act(a("G1", 270, 512, 16), NL, F.Identity, 13.5, -1.0)
+            ts(a("Me"), WN, float(V - CEN), A.is_lt)
+            tt(a("Wf"), WP, a("Me"), A.mult)
+            for i in range(2 * NCH):
+                if i < OS:
+                    act(blk("X", i, CW // 2), blk("XF", i, CW // 2), F.Copy)
+                ts(blk("XO", i, CW // 2), blk("X" if i < OS else "XF", i, CW // 2), 255.0, A.min)
             store(lambda T: T.yx[:, :], lambda T: T.XO[:, :], a("XO"), "ox", 9000)
-        ts(blk("Cc", 1), a("rs"), float(-CEN), A.add)
-        fit(range(0, 13, 2), blk("Cc", 1))
-        hop(OWN, "rs", blk("Cc", 1), NV2, XV2, SB2, "Y2", None)
-        tt(sm(TT_), a("pm", 15, 256, 16), sm(PEN1), A.add)
-        ts(sm(GO2), sm(TT_), THR, A.is_lt, 2.0, A.mult)
+        steps = {"r": lambda: rows(r + 1), "c": cut, "k": keys, "0": lambda: edges(r + 1, 0), "1": lambda: edges(r + 1, 1), "e": lambda: ends(r + 1),
+                 "b": bounds, "A": lambda: second(0), "B": lambda: second(1)}
+        for x in ("AbB" if last else STEPS):
+            steps[x]()
+        ng = a("G0", 14, 256, 16)
+        vb = dbank()
+        pe([(t3(vb, (0, 16), k), a("Ih"), CNUL if k == 15 else a("YS", 271 - 256 * (k & 1), 512 - 256 * (k & 1), 16), True, True) for k in range(16)])
+        tt(ng, k2, PTH, A.is_gt)
         if not last:
-            ts(sm(UU), sm(TT_), -65536.0, A.add, 4.0, A.mult)
-            ts(sm(GB_), sm(TT_), THR, A.is_lt, BIG, A.mult)
-            tt(sm(U1), sm(TT_), sm(C2), A.add)
-            tt(sm(U2), sm(UU), sm(KEYX), A.max)
-            tt(sm(U4), sm(GB_), sm(KEY0), A.add)
-            tt(sm(U1), sm(U1), sm(U2), A.min)
-            tt(sm(KS), sm(U1), sm(U4), A.min)
-        pe([(a("P7", 0, 256), blk("Bo", 0, 128), a("Y1"), True, False), (a("P7", 0, 256), blk("Bo", 1, 128), a("Y2"), False, True)])
-        tt(a("TT"), a("P7", 0, 256), a("Mn"), A.mult)
-        pe([(WP, a("Ih"), a("Wz"), True, False), (WP, a("Ih"), a("TT"), False, True)])
-        if not last:
-            cp(a("Wn"), WP)
-    tt(blk("Q", 5, 16), sm(NL), sm(GO2), A.add)
-    bcast([3])
-    act(a("yc"), blk("GB", 3), F.Copy)
-    ts(a("Me"), blk("GB", 3), col(KC), A.is_gt)
-    act(a("yq"), WP, F.Identity, float(CEN))
-    tt(a("yo"), a("yq"), a("Me"), A.mult)
+            tt(sm(Z1), k2, PC, A.add)
+            tt(sb(WFH), sm(Z1), sm(KX), A.is_lt)
+            pe([(pick(z, c), a(w), x, False, False) for z in range(2) for c, w, x in
+                ((0, "PENI", ng), (1, "nPEN", ng), (2, "PENI", ng), (0, "PENI", sb(WFH)), (2, "PENI", sb(WFH)), (3, "nPEN", sb(WFH)))])
+            pe([(pick(0, 3), a("Ih"), a("YS", 271, 512, 16), False, True)])
+            scan(rev("GU", 0, 256), rev("G0", 0, 256), rev("G1", 0, 256), 0.0, A.mult, A.add)
+            tt(a("TS"), WB, blk("GU", 0), A.mult)
+            pe([(WP, a("Ih"), a("Wf"), True, False), (WP, a("I32"), a("TS"), False, True)])
+        scan(rev("GU", 256, 512), rev("G0", 0, 256), rev("G1", 256, 512), 0.0, A.mult, A.add)
+        ts(a("OA"), blk("GU", 1), M2, A.add, M2, A.is_equal)
+        if last:
+            tt(a("XV"), t3(vb, (0, 16)), a("OA"), A.mult)
+        else:
+            lin(a("NU"), a("OA"), -3968.0, float(NUL - CEN))
+            tt(a("XV"), t3(vb, (0, 16)), a("NU"), A.max)
+            tt(WN, WP, a("XV"), A.min)
+            pe([(WP, a("Ih"), WN, True, True)])
+    act(sm(U1), ng, F.Identity, 2.0, -2.0)
+    tt(a("wn", 16, 32), sm(U1), NL, A.add)
+    pe([(a("KA", 128 * h, 128 * h + 128, p=p8), a("wn", 16 + 8 * h, 24 + 8 * h), I_, True, True) for h in range(2)])
+    act(a("yc", p=p8), a("KA", 0, 256, p=p8), F.Copy)
+    bk = dbank()
+    pe([(t3(bk, (8 * h, 8 * h + 8)), blk(x, h, 128), w, i == 0, i == 3) for h in range(2)
+        for i, (x, w) in enumerate((("Wf", a("Ih")), ("Me", a("CI")), ("XV", a("Ih")), ("OA", a("CI"))))])
+    gather(a("yo"), t3(bk, (0, 16)))
     store(lambda T: T.yw[:, :], lambda T: T.yo[:, :], a("yo"), "ow", 2500)
-    store(lambda T: T.yn[:, :], lambda T: T.yc[0:128:16, :], a("yc"), "on", 2500)
+    store(lambda T: T.yn[:, :], lambda T: T.yc[0:8, :], a("yc"), "on", 2500)
+
+
+def polish(sch, dl, ways, lat, head, rs, moves):
+    N = len(dl)
+    way = list(sch[5])
+    eng, cost = [ways[n][way[n]][0] for n in range(N)], [ways[n][way[n]][1] for n in range(N)]
+    sl = [[] for n in range(N)]
+    for n in range(N):
+        for d, w in dl[n]:
+            sl[d].append((n, w))
+    mp, mn = [-1] * N, [-1] * N
+    for q in sch[1].values():
+        for i in range(1, len(q)):
+            mp[q[i][2]], mn[q[i - 1][2]] = q[i - 1][2], q[i][2]
+    banks = [[x[2] for x in sorted(h)] for h in sch[6]]
+    bp, bn = [()] * N, [-1] * N
+
+    def link():
+        for h in banks:
+            for i, n in enumerate(h):
+                bp[n] = tuple((m, 0.0 if eng[m] == "P" else SL) for m in head[h[i - 1]]) if i else ()
+                for m in head[n]:
+                    bn[m] = h[i + 1] if i + 1 < len(h) else -1
+    link()
+    order = sorted(range(N), key=lambda n: (sch[2][n], n))
+    pos, end, tail = [0] * N, [0.0] * N, [0.0] * N
+    for i, n in enumerate(order):
+        pos[n] = i
+
+    def ahead(p0, p1):
+        for n in order[p0:p1]:
+            m = mp[n]
+            t = end[m] if m >= 0 else 0.0
+            for d, w in dl[n]:
+                if end[d] + w > t:
+                    t = end[d] + w
+            for d, w in bp[n]:
+                if end[d] + w > t:
+                    t = end[d] + w
+            end[n] = t + cost[n]
+
+    def behind(p1):
+        for n in order[p1::-1]:
+            m = mn[n]
+            t = tail[m] if m >= 0 and tail[m] > lat[n] else lat[n]
+            for d, w in sl[n]:
+                if tail[d] + w > t:
+                    t = tail[d] + w
+            m = bn[n]
+            if m >= 0 and tail[m] + (0.0 if eng[n] == "P" else SL) > t:
+                t = tail[m] + (0.0 if eng[n] == "P" else SL)
+            tail[n] = t + cost[n]
+
+    def unlink(n):
+        if mp[n] >= 0:
+            mn[mp[n]] = mn[n]
+        if mn[n] >= 0:
+            mp[mn[n]] = mp[n]
+
+    def insert(n, x, y):
+        mp[n], mn[n] = x, y
+        if x >= 0:
+            mn[x] = n
+        if y >= 0:
+            mp[y] = n
+
+    def lift(u, v):
+        p0, p1 = pos[u], pos[v]
+        need, todo = {v}, [v]
+        while todo:
+            n = todo.pop()
+            for d in [x[0] for x in dl[n]] + [x[0] for x in bp[n]] + [mp[n]]:
+                if d >= 0 and pos[d] >= p0 and d not in need:
+                    if d == u:
+                        return False
+                    need.add(d)
+                    todo.append(d)
+        seg = order[p0:p1 + 1]
+        order[p0:p1 + 1] = [n for n in seg if n in need] + [n for n in seg if n not in need]
+        for i in range(p0, p1 + 1):
+            pos[order[i]] = i
+        return True
+
+    ahead(0, N)
+    behind(N - 1)
+    cur = max(end[n] + lat[n] for n in range(N))
+    keep = (cur, list(order), list(way), [list(h) for h in banks], list(end), list(cost))
+    crit = [n for n in range(N) if end[n] - cost[n] + tail[n] > cur - SLACK and eng[n]]
+    for it in range(moves):
+        v = crit[int(rs.randint(len(crit)))]
+        beg, x, undo = end[v] - cost[v], rs.rand(), None
+        p0 = p1 = pos[v]
+        if len(ways[v]) > 1 and x < 0.35:
+            e, c = ways[v][1 - way[v]]
+            i = p0 - 1
+            while i >= 0 and eng[order[i]] != e:
+                i -= 1
+            if i < 0:
+                continue
+            old = (mp[v], mn[v], eng[v], cost[v])
+            unlink(v)
+            insert(v, order[i], mn[order[i]])
+            eng[v], cost[v], way[v] = e, c, 1 - way[v]
+            undo = 0
+        elif bp[v] and max(end[d] + w for d, w in bp[v]) >= beg - 1.0 and x < 0.8:
+            b = [b for b in range(3) if v in banks[b]][0]
+            old = [list(h) for h in banks]
+            seg = None
+            i = banks[b].index(v)
+            if x < 0.5:
+                b2 = (b + 1 + int(rs.randint(2))) % 3
+                j = len([m for m in banks[b2] if pos[m] < p0])
+                banks[b][i:], banks[b2][j:] = banks[b2][j:], banks[b][i:]
+                if (j and max(pos[m] for m in head[banks[b2][j - 1]]) > p0) or (i < len(banks[b]) and max(pos[m] for m in head[banks[b][i - 1]]) > pos[banks[b][i]]):
+                    banks[:] = old
+                    continue
+                link()
+            else:
+                u = banks[b][i - 1]
+                banks[b][i - 1], banks[b][i] = v, u
+                link()
+                p0, p1 = pos[u], max(pos[m] for m in head[v])
+                seg = order[p0:p1 + 1]
+                if not all(lift(u, m) for m in head[v] if pos[m] > pos[u]):
+                    banks[:] = old
+                    link()
+                    order[p0:p1 + 1] = seg
+                    for k, m in enumerate(seg):
+                        pos[m] = p0 + k
+                    continue
+            undo = 1
+        else:
+            if x > 0.6 and mn[v] >= 0:
+                u, v = v, mn[v]
+                for k in range(int(FAR * rs.rand() ** 2)):
+                    v = mn[v] if mn[v] >= 0 else v
+                p0, p1 = pos[u], pos[v]
+                seg, old, mv = order[p0:p1 + 1], (mp[u], mn[u]), u
+                unlink(u)
+                insert(u, v, mn[v])
+            else:
+                u = mp[v]
+                if u < 0 or end[u] < beg - 1.0:
+                    continue
+                for k in range(int(FAR * rs.rand() ** 2)):
+                    u = mp[u] if mp[u] >= 0 else u
+                p0, p1 = pos[u], pos[v]
+                seg, old, mv = order[p0:p1 + 1], (mp[v], mn[v]), v
+                unlink(v)
+                insert(v, mp[u], u)
+            if not lift(u, v):
+                unlink(mv)
+                insert(mv, old[0], old[1])
+                continue
+            undo = 2
+        p2 = min(N, p1 + 60)
+        was = [end[n] for n in order[p0:p2]], order[p0:p2]
+        ahead(p0, p2)
+        lim = cur + COOL * (1.0 - it / moves) * -np.log(1.0 - rs.rand())
+        ok = max(end[n] - cost[n] + tail[n] for n in order[p1 + (p1 + 1 < p2):p2]) <= lim
+        if ok:
+            ahead(p2, N)
+            new = max(end[n] + lat[n] for n in order[-200:])
+            ok = new <= lim
+            if not ok:
+                was = None
+        if ok:
+            cur = new
+            behind(N - 1 if undo == 1 else p1)
+            crit = [n for n in range(N) if end[n] - cost[n] + tail[n] > cur - SLACK and eng[n]]
+            if cur < keep[0]:
+                keep = (cur, list(order), list(way), [list(h) for h in banks], list(end), list(cost))
+            continue
+        if undo == 0:
+            unlink(v)
+            insert(v, old[0], old[1])
+            eng[v], cost[v], way[v] = old[2], old[3], 1 - way[v]
+        else:
+            if undo == 1:
+                banks[:] = old
+                link()
+            else:
+                unlink(mv)
+                insert(mv, old[0], old[1])
+            if seg:
+                order[p0:p1 + 1] = seg
+                for k, m in enumerate(seg):
+                    pos[m] = p0 + k
+        if was:
+            for t, n in zip(*was):
+                end[n] = t
+        else:
+            ahead(p0, N)
+    cur, order, way, banks, end, cost = keep
+    beg = [end[n] - cost[n] for n in range(N)]
+    for i, n in enumerate(order):
+        beg[n] += 1e-6 * i
+    slots = {e: [(beg[n], end[n], n) for n in order if ways[n][way[n]][0] == e] for e in "VSPGY"}
+    return cur, slots, beg, beg, end, way, [[(beg[n], 0.0, n) for n in h] for h in banks]
 
 
 def plan():
     program()
     last_w, last_r = {}, {}
-    bank = lambda q: SCRATCH[q[0]][0] == "psum"
+    bank = lambda q: SCR[q[0]][0] == "psum"
     for o in OPS:
         raw, oth = set(), set()
         for q in o["r"]:
             raw.update(d for (c0, c1, d) in last_w.get(q[0], []) if bank(q) or (c0 < q[2] and q[1] < c1))
             if bank(q):
-                oth.update(d for (c0, c1, d) in last_r.get(q[0], []) if OPS[d]["eng"] != o["eng"])
+                oth.update(d for (c0, c1, d) in last_r.get(q[0], []) if OPS[d]["eng"] != o["eng"] or o["alt"] or OPS[d]["alt"])
         for q in o["w"]:
-            oth.update(d for (c0, c1, d) in last_w.get(q[0], []) + last_r.get(q[0], []) if bank(q) or (c0 < q[2] and q[1] < c1))
+            oth.update(d for (c0, c1, d) in last_w.get(q[0], []) + last_r.get(q[0], [])
+                       if (bank(q) or (c0 < q[2] and q[1] < c1)) and not (o["acc"] and OPS[d]["acc"]))
         for q in o["w"]:
-            keep = lambda t: not (bank(q) or (q[1] <= t[0] and t[1] <= q[2]))
+            keep = lambda t: o["acc"] or not (bank(q) or (q[1] <= t[0] and t[1] <= q[2]))
             last_w[q[0]] = [t for t in last_w.get(q[0], []) if keep(t)]
             last_r[q[0]] = [t for t in last_r.get(q[0], []) if keep(t)]
         for q in o["w"]:
@@ -728,89 +1044,173 @@ def plan():
             raw, oth = set(), set()
         o["deps"] = (raw | oth | set(x["n"] for x in o["after"])) - {o["n"]}
         o["know"] = {}
+        o["early"] = set()
         o["wait"] = set(d for d in o["deps"] if not (OPS[d]["eng"] == o["eng"] and o["eng"] in "PG"))
     N = len(OPS)
-    eng = [o["eng"] for o in OPS]
-    cost = [o["cost"] for o in OPS]
-    tail = [o["cost"] + o["lat"] for o in OPS]
-    dl = [[(d, tail[d] + SL if d in o["wait"] else cost[d]) for d in sorted(o["deps"])] for o in OPS]
-    pr = list(tail)
-    for n in range(N - 1, -1, -1):
-        pr[n] += OPS[n].get("prio", 0.0)
-        for d, w in dl[n]:
-            pr[d] = max(pr[d], pr[n] + w + 1.0)
-
+    use = {}
+    for o in OPS:
+        for q in set(q[0] for q in o["r"] + o["w"] if q[0][:2] == "D#"):
+            use.setdefault(q, []).append(o["n"])
+    head, inside = {}, set()
+    for q, l in use.items():
+        head[l[0]] = l
+        inside.update(l[1:])
+        first = OPS[l[0]]
+        for m in l[1:]:
+            for d in OPS[m]["deps"] - set(l) - first["deps"]:
+                first["deps"].add(d)
+                first["early"].add(d)
+    ways = [[(o["eng"], o["cost"])] + ([(o["alt"][0], o["alt"][2])] if o["alt"] else []) for o in OPS]
+    lat = [o["lat"] for o in OPS]
+    dl = [[(d, lat[d] + SL if d in o["wait"] else -o["cost"] if d in o["early"] else 0.0) for d in sorted(o["deps"])] for o in OPS]
     rl = [[] for o in OPS]
     for n in range(N):
         for d, w in dl[n]:
-            rl[d].append((n, cost[n] + w - cost[d]))
-    zero, lat = [0.0] * N, [tail[n] - cost[n] for n in range(N)]
+            rl[d].append((n, w))
+    topo, left = [n for n in range(N) if not dl[n]], [len(x) for x in dl]
+    for d in topo:
+        for n, w in rl[d]:
+            left[n] -= 1
+            if not left[n]:
+                topo.append(n)
+    topo.reverse()
+    pr = [o["cost"] + o["lat"] for o in OPS]
+    for n in topo:
+        pr[n] += OPS[n].get("prio", 0.0)
+        for d, w in dl[n]:
+            pr[d] = max(pr[d], pr[n] + w + OPS[d]["cost"] + 1.0)
+    zero = [0.0] * N
 
-    def turn(sch):
-        back = place([sch[2][n] + cost[n] + 1e-6 * n for n in range(N)], rl, lat, True)
-        p = [back[2][n] + cost[n] - 1e-6 * n for n in range(N)]
-        for n in range(N - 1, -1, -1):
+    def place(pr, bias, dl=dl, base=zero, fix=None):
+        slots = {e: [] for e in "VSPGY"}
+        beg, end, rdy, way = [0.0] * N, [0.0] * N, [0.0] * N, [0] * N
+        held = [[] for b in range(3)]
+
+        def put(n, t0):
+            for d, w in dl[n]:
+                if end[d] + w > t0:
+                    t0 = end[d] + w
+            rdy[n] = t0
+            best = None
+            for j in (range(len(ways[n])) if fix is None else (fix[n],)):
+                e, c = ways[n][j]
+                t, i = t0, 0
+                if e is not None:
+                    sl = slots[e]
+                    i = len(sl)
+                    while i > 0 and sl[i - 1][1] > t:
+                        i -= 1
+                    while i < len(sl) and sl[i][0] < t + c:
+                        t = max(t, sl[i][1])
+                        i += 1
+                f = t + c + (bias[n] if j else 0.0)
+                if best is None or f < best[0]:
+                    best = (f, j, e, c, t, i)
+            f, j, e, c, t, i = best
+            if e is not None:
+                slots[e].insert(i, (t, t + c, n))
+            beg[n], end[n], way[n] = t, t + c, j
+        for n in sorted(range(N), key=lambda n: (-pr[n], n)):
+            if fix is not None or n not in head:
+                if fix is not None or n not in inside:
+                    put(n, base[n])
+                continue
+            t0 = 0.0
+            while True:
+                for m in head[n]:
+                    put(m, t0 if m == n else 0.0)
+                t1, t2 = beg[n], max(end[m] for m in head[n]) + SL
+                nxt = [max([y for x, y, m in h if x < t2 and t1 < y] + [0.0]) for h in held]
+                if min(nxt) == 0.0:
+                    free = [b for b in range(3) if nxt[b] == 0.0]
+                    held[max(free, key=lambda b: max([y for x, y, m in held[b] if y <= t1] + [0.0]))].append((t1, t2, n))
+                    break
+                for m in head[n]:
+                    slots[ways[m][way[m]][0]].remove((beg[m], end[m], m))
+                t0 = min(nxt)
+        return max(end[n] + lat[n] for n in range(N)), slots, beg, rdy, end, way, held
+
+    def chain(sch):
+        return [(m, h[i + 1][2]) for h in map(sorted, sch[6]) for i in range(len(h) - 1) for m in head[h[i][2]]]
+
+    def mend(p, dl, order, step):
+        for n in order:
             for d, w in dl[n]:
                 if p[d] <= p[n]:
-                    p[d] = p[n] + 1e-3
-        return place(p), p
+                    p[d] = p[n] + step
+        return p
 
-    def place(pr, dl=dl, base=zero, back=False):
-        if back:
-            for n in range(N):
-                for d, w in dl[n]:
-                    if pr[d] <= pr[n]:
-                        pr[d] = pr[n] + 1e-3
-        slots = {e: [] for e in "VSPGY"}
-        beg, rdy = [0.0] * N, [0.0] * N
-        for n in sorted(range(N), key=lambda n: (-pr[n], n)):
-            t = max([beg[d] + w for d, w in dl[n]] + [base[n]])
-            rdy[n] = t
-            if eng[n] is not None:
-                sl = slots[eng[n]]
-                i = len(sl)
-                while i > 0 and sl[i - 1][1] > t:
-                    i -= 1
-                while i < len(sl) and sl[i][0] < t + cost[n]:
-                    t = max(t, sl[i][1])
-                    i += 1
-                sl.insert(i, (t, t + cost[n], n))
-            beg[n] = t
-        return max(beg[n] + tail[n] for n in range(N)), slots, beg, rdy
+    def turn(sch, bias):
+        r2 = [list(x) for x in rl]
+        for m, n in chain(sch):
+            r2[m].append((n, SL))
+        back = place(mend([sch[4][n] + 1e-6 * n for n in range(N)], r2, sorted(range(N), key=lambda n: (sch[2][n], n)), 1e-3), bias, r2, lat, sch[5])
+        p = mend([back[4][n] - 1e-6 * n for n in range(N)], dl, topo, 1e-3)
+        return place(p, bias), p
 
     rs = np.random.RandomState(SEED)
-    cur = best = place(pr)
+    bias = [-LEAN0] * N
+    kin = {}
+    for o in OPS:
+        kin.setdefault(o["kind"], []).append(o["n"])
+    free = [n for n in range(N) if len(ways[n]) > 1]
+    cur = best = place(pr, bias)
     for it in range(TRIES):
-        fin, slots, beg, rdy = cur
+        fin, slots, beg, rdy, end, way, hd = cur
+        after = {}
+        for m, n in chain(cur):
+            if n not in after or end[m] > end[after[n]]:
+                after[n] = m
         prev = {sl[i][2]: sl[i - 1][2] for sl in slots.values() for i in range(1, len(sl))}
-        n = max(range(N), key=lambda n: beg[n] + tail[n])
+        n = max(range(N), key=lambda n: end[n] + lat[n])
         held = []
         while beg[n] > 0:
-            if beg[n] > rdy[n] + 1.0:
+            if n in after and end[after[n]] + SL >= beg[n] - 1.0:
+                held.append((n, 200.0))
+                prev[n] = n = after[n]
+            elif beg[n] > rdy[n] + 1.0:
                 if pr[prev[n]] > pr[n]:
                     held.append((n, beg[n] - rdy[n]))
                 n = prev[n]
             else:
-                n = max(dl[n], key=lambda x: beg[x[0]] + x[1])[0]
-        if not held:
-            break
-        p2 = list(pr)
-        for j in range(int(rs.randint(1, 4))):
+                n = max(dl[n], key=lambda x: end[x[0]] + x[1])[0]
+        p2, b2 = list(pr), bias
+        for j in range(int(rs.randint(1, 4)) if held else 0):
             n, w = held[int(rs.randint(len(held)))]
-            p2[n] = max(p2[n] + w * float(rs.rand()), pr[prev[n]] + 1.0)
-        for n in range(N - 1, -1, -1):
-            for d, w in dl[n]:
-                if p2[d] <= p2[n]:
-                    p2[d] = p2[n] + 1.0
-        t2 = place(p2)
+            up = max(w * float(rs.rand()), pr[prev[n]] + 1.0 - p2[n])
+            for m in (kin[OPS[n]["kind"]] if it % 4 else [n]):
+                p2[m] += up
+        if rs.rand() < RAND:
+            x = 3000.0 * float(rs.randn())
+            for m in kin[OPS[int(rs.randint(N))]["kind"]]:
+                p2[m] += x
+        if it % 3 == 0:
+            b2 = list(bias)
+            n = free[int(rs.randint(len(free)))]
+            x = (1.0 if way[n] else -1.0) * LEAN * float(rs.rand())
+            for m in kin[OPS[n]["kind"]]:
+                b2[m] = x
+        t2 = place(mend(p2, dl, topo, 1.0), b2)
         if it % TURN == 0:
-            t2, p2 = turn(t2)
-        if t2[0] <= fin + 800.0 * (1.0 - it / TRIES) * float(rs.rand()):
-            cur, pr = t2, p2
+            t2, p2 = turn(t2, b2)
+        if t2[0] <= fin + HEAT * (1.0 - it / TRIES) * float(rs.rand()):
+            cur, pr, bias = t2, p2, b2
             if t2[0] < best[0]:
                 best = t2
+    for moves in (FIRST, MOVES):
+        best = polish(best, [[x for x in dl[n] if x[0] not in OPS[n]["early"]] for n in range(N)], ways, lat, head, rs, moves)
     for o in OPS:
         o["t"] = best[2][o["n"]]
+        o["deps"] -= o["early"]
+        if best[5][o["n"]]:
+            o["eng"], o["emit"], o["cost"] = o["alt"]
+    for b, h in enumerate(best[6]):
+        for x in h:
+            BANK[[q for q in use if use[q][0] == x[2]][0]] = "D%d" % b
+    for m, n in chain(best):
+        OPS[n]["deps"].add(m)
+        if OPS[m]["eng"] != "P":
+            OPS[n]["wait"].add(m)
     order = {e: [x[2] for x in best[1][e]] for e in best[1]}
     pos = {n: i for e in order for i, n in enumerate(order[e])}
     need = set()
@@ -912,15 +1312,21 @@ def rank_program(g, core, T, topo):
     off = [x for x in cores if topo.chip(x) != topo.chip(core)][0]
     es = topo.engines(core, off)
     h = len(es) // 2
-    c = {"ls1": [0], "ne": len(es)}
-    for nm, d in (("p", p), ("q", q)):
-        c[nm] = {"rid": topo.addr(d)[0], "pid": topo.addr(d)[1], "m8": bits(es), "m4a": bits(es[:h]), "m4b": bits(es[h:])}
-    sent = [0]
+    sent, out = [0], [0]
 
     def big(what, i):
-        ls, num = (T.sem.ls0, sent) if what == "X" else (T.sem.ls1, c["ls1"])
+        ls, num = (T.sem.ls0, sent) if what == "X" else (T.sem.ls1, out)
         num[0] += hand(what, i, ways[rank][what][i], 0, ls)
-    c["big"] = big
+
+    def one(dst, src, sem):
+        g.remote_dma(dst, src, T.sem[sem], T.sem.ls1, topo.addr(p)[1], topo.addr(p)[0], bits(es))
+        out[0] += len(es)
+
+    def two(d1, s1, m1, d2, s2, m2):
+        g.remote_dma_fused([RemoteDMATransfer(dst_ids=[DstId(rid=topo.addr(to)[0], pnc=topo.addr(to)[1])], dma_engine_mask=bits(m), remote_sem=T.sem[sem], src=x, dst=y)
+                            for to, m, sem, x, y in ((p, es[:h], m1, s1, d1), (q, es[h:], m2, s2, d2))], local_sem=T.sem.ls1)
+        out[0] += len(es)
+    c = {"big": big, "one": one, "two": two}
     vals = {"xarr": sum(len(step(topo, w, len(w) - 2)) for w in ways[(rank + SH) % n]["X"])}
     for i, w in enumerate(ways[(rank + SH) % n]["C"]):
         vals["ca%d" % i] = len(step(topo, w, len(w) - 2))
@@ -945,6 +1351,6 @@ def rank_program(g, core, T, topo):
     for e in "VSPG":
         if TOTAL[e]:
             g.wait_ge(T.sem["s" + e], TOTAL[e])
-    g.wait_ge(T.sem.ls1, c["ls1"][0])
+    g.wait_ge(T.sem.ls1, out[0])
     for s in ("ox", "ow", "on"):
         g.wait_ge(T.sem[s], 16)

@@ -8,6 +8,7 @@ VP = NUL + 16
 CEN = V // 2
 BIG = float(2 ** 20)
 DEAD = 2048.0
+LIFT = 4096.0
 OFF = 128 * DEAD
 THR = 135168.0
 PEN = 262144.0
@@ -15,22 +16,23 @@ K0 = 8.0 - 1.0 / 32
 M1 = 1.5 * 2 ** 23
 M2 = 1.5 * 2 ** 24
 M16 = 1.5 * 2 ** 27
-HV = [[12, 12], [8, 8]]
-HVL = [[8, 8], [8, 8]]
-EA = ["VV", "SS", "SS", "SS"]
-VQ = "VVSSVSSVSVVSSVSV"
+HV = [[3, 3], [3, 2]]
+HVL = [[2, 2], [2, 2]]
+EA = ["22", "SS", "SS", "SS"]
+VQ = (("D", (15, 14)), ("KA", (7, 6, 5, 4)), ("D", (13, 12)), ("D", (11, 10)), ("KB", (3, 2, 1, 0)), ("D", (9, 8)))
 STEPS = "rc0A1kBbe"
 XS = 4
 OS = 6
-SEED, TRIES = 3, 600
-FIRST = 110000
-MOVES = 70000
+SEED, TRIES = 3, 60
+FIRST = 1000000
+MOVES = 300000
 FAR = 12
+WIN, STAY = 200, 1500
 TURN, LEAN = 8, 1500.0
 LEAN0 = 900.0
 HEAT = 200.0
 RAND = 0.3
-COOL = 45.0
+COOL = 90.0
 SLACK = 60.0
 SIM = 64
 NCH = 4
@@ -38,26 +40,27 @@ CW = V // NCH
 
 SCRATCH = {}
 for _d, _l in (
-        ("bfloat16", (("X", 2 * VP), ("XO", V), ("CT", NUL), ("VV", 4112), ("XC", 4096), ("MM", 4096), ("ED", 4096), ("BB", 32), ("nB", 17 * 128), ("L2", 128),
+        ("bfloat16", (("X", 2 * VP), ("XO", V), ("VV", 4112), ("XC", 4096), ("MM", 4096), ("ED", 4096), ("BB", 32), ("nB", 5 * 128), ("L2", 128),
                       ("IL", 160), ("K16", 256), ("nIb", 128), ("PENI", 128), ("nPEN", 128), ("CI", 128), ("Bx", 128), ("NST", 768), ("NS8", 256), ("KN", 128),
-                      ("KI", 256), ("KH", 256), ("CC", 1024), ("DN", 256), ("xs", 512), ("EQ", 7 * 256), ("eq", 512), ("OH", 512), ("DM", 768), ("UM", 768),
+                      ("KI", 256), ("KH", 256), ("CC", 1024), ("xs", 512), ("EQ", 7 * 256), ("eq", 512), ("OH", 512), ("DM", 768), ("UM", 768),
                       ("G0", 256), ("G1", 512), ("OA", 256), ("NU", 256), ("en", 128), ("sb", 256), ("xm", 512), ("GU", 512), ("PQ", 144), ("de", 128),
-                      ("RR", 512), ("CR", 512), ("junk", 1536), ("mid", 1024), ("rmid", 1024), ("Lo", 256), ("ones", 128), ("wn", 32), ("m2", 256), ("Me", 256),
+                      ("TRI", 64), ("mid", 1024), ("rmid", 1024), ("ones", 128), ("wn", 32), ("Me", 256),
                       ("R1", 320))),
-        ("float16", (("Ih", 128), ("nIh", 128), ("I2", 256), ("B2", 96), ("CU", V), ("CQ", V), ("ZW", 512), ("RC", 160), ("DA", 512), ("DB", 512), ("DL", 1808),
-                     ("TL", 1808), ("Wn", 272), ("Wf", 256), ("Wb", 256), ("Cc", 256), ("Y", 256), ("YS", 512), ("DK", 512), ("UK", 512), ("XV", 256),
+        ("float16", (("Ih", 128), ("nIh", 128), ("I2", 256), ("B2", 16), ("CU", V), ("CQ", V), ("RT", 512), ("Wn", 272), ("RC", 160), ("DA", 512), ("DL", 1168),
+                     ("TL", 1168), ("Wf", 256), ("Wb", 256), ("Cc", 256), ("Y", 256), ("YS", 512), ("DK", 512), ("UK", 512), ("XV", 256),
                      ("es", 128), ("NV", 32), ("YE", 512), ("YA", 512))),
-        ("float32", (("Li", 256), ("RST", 256), ("RF", 256), ("RB", 256), ("KM", 16), ("col", 32), ("abf", 32), ("XF", VP), ("DF", 256), ("CP", V), ("cth", 512),
-                     ("I32", 128), ("pm", 512), ("pd", 272), ("pe", 512), ("sm", 1024), ("xa", 256), ("xb", 256), ("xc", 256), ("ra", 160), ("RS5", 160),
-                     ("ef", 32), ("Hi", 16), ("tq", 256), ("TS", 256), ("yo", 256), ("yc", 256))),
+        ("float32", (("RST", 256), ("RF", 256), ("RB", 256), ("col", 32), ("abf", 32), ("XF", 2 * VP), ("DF", 1280), ("CP", V), ("cth", 512),
+                     ("I32", 128), ("pm", 512), ("pd", 272), ("pe", 512), ("sm", 1024), ("xc", 256), ("ra", 160), ("RS5", 160),
+                     ("ef", 32), ("yo", 256), ("yc", 256))),
         ("int32", (("CA", V), ("wi", 256), ("ci", 256), ("ti", 256), ("pi", 8))),
         ("uint16", (("WO", 256), ("CO", 512), ("el", 16), ("fl", 16), ("ab", 32), ("eff", 128), ("rl", 128)))):
     for _n, _c in _l:
         SCRATCH[_n] = ("sbuf", [128, _c], _d)
-for _n, _s, _d in (("LL", [8, 128], "bfloat16"), ("TA", [16, 32], "float16"), ("TB", [16, 32], "float16"), ("WXo", [16, 24], "float32"), ("WXe", [16, 28], "float32")):
+for _n, _s, _d in (("LL", [8, 128], "float16"), ("DV", [2, 160], "float16"), ("Wz", [16, 32], "float16"), ("TA", [16, 32], "float16"), ("TB", [16, 32], "float16"), ("WXo", [16, 24], "float32"), ("WXe", [16, 28], "float32")):
     SCRATCH[_n] = ("sbuf", [128] + _s, _d)
-for _n in ("KA", "KB", "PE"):
-    SCRATCH[_n] = ("psum", [128, 512], "float32")
+SCRATCH["PE"] = ("psum", [128, 512], "float32")
+for _n in ("KA", "KB"):
+    SCRATCH[_n] = ("psum", [128, 4, 128], "float32")
 for _n in ("PT", "PW", "D0", "D1", "D2"):
     SCRATCH[_n] = ("psum", [128, 32, 16], "float32")
 
@@ -99,7 +102,7 @@ def regs(x):
         return regs(x[1]) + regs(x[2])
     if x[0] == "t":
         w, c = SCR[x[1]][1][2], rng(x[3])
-        return [(x[1], w * i + c[0], w * i + c[-1] + 1) for i in rng(x[2])]
+        return [(x[1], w * i + min(c), w * i + max(c) + 1) for i in rng(x[2])]
     return [(x[1], x[2], x[3])]
 
 
@@ -130,16 +133,18 @@ def mk(T, x):
     if x[0] == "r":
         return t[:, x[3] - 1:(x[2] - 1 if x[2] else None):-1]
     p = slice(None) if x[-1] is None else slice(x[-1][0], x[-1][1])
-    f = lambda y: y if isinstance(y, int) else slice(y[0], y[1]) if y[2] == 1 else slice(*y)
+    f = lambda y: y if isinstance(y, int) else slice(y[0], y[1]) if y[2] == 1 else slice(y[0], y[1] if y[1] >= 0 else None, y[2])
     if x[0] == "t":
         return t[p, f(x[2]), f(x[3])]
+    if x[1] in ("KA", "KB"):
+        return t[p, 0, f(x[2:5])]
     return t[p, f(x[2:5])]
 
 
 OPS, SEEN = [], {}
-CY = 0.9
-PEC = 0.53
-GA, SCA, VF, SF, PF, SL, RI, RL = 1.56, 3.8, 30.0, 50.0, 40.0, 120.0, 700.0, 2500.0
+CY = 0.97
+PEC = 0.57
+GA, SCA, VF, SF, PF, SL, RI, RL = 1.65, 4.2, 33.0, 54.0, 43.0, 120.0, 900.0, 2300.0
 
 
 def op(eng, emit, rd, wr, cost, tok=None, lat=0.0, track=True, after=(), acc=False):
@@ -181,7 +186,8 @@ def ts(out, in_, s1, o1, s2=None, o2=None):
 
 def tt(out, x, y, o):
     b = 1.0 if (ps(x) or ps(y) or x[0] == "i") else 2.0
-    return op("V", lambda g, T, c: g.vector.tensor_tensor(mk(T, out), mk(T, x), mk(T, y), o), [x, y], [out], _vc(out, [x], b))
+    return op("V", lambda g, T, c: g.vector.tensor_tensor(mk(T, out), mk(T, x), mk(T, y), o), [x, y] + ([out[2]] if out[0] == "i" else []),
+              [out[1] if out[0] == "i" else out], _vc(out, [x], b))
 
 
 def scan(out, d0, d1, init, o0, o1):
@@ -190,7 +196,8 @@ def scan(out, d0, d1, init, o0, o1):
 
 
 def red(out, in_, o):
-    return op("V", lambda g, T, c: g.vector.tensor_reduce(mk(T, out), mk(T, in_), AxisListType.X, o), [in_], [out], VF + max(64, cnt(in_)) * CY)
+    return op("V", lambda g, T, c: g.vector.tensor_reduce(mk(T, out), mk(T, in_), AxisListType.X, o, apply_absolute_value=True), [in_], [out],
+              VF + max(64, cnt(in_)) * CY)
 
 
 def ms(out, v):
@@ -220,7 +227,14 @@ def lin(out, in_, scale, bias=0.0):
 
 
 def gather(out, src):
+    if src[0] == "i" and src[1][1] == "XF":
+        return either(ts(out, src, -LIFT, A.add), act(out, src, F.Identity, -LIFT))
     return either(cp(out, src), act(out, src, F.Copy))
+
+
+def scatter(win, off, src):
+    x = ind(win, off)
+    return either(cp(x, src), op("S", lambda g, T, c: g.scalar.activation(mk(T, x), mk(T, src), F.Silu), [src, off], [win], 65 + SCA * CY * 256))
 
 
 def pe(ml, acc=False):
@@ -242,6 +256,10 @@ def iota(out, pat, base, cm):
     else:
         e = lambda g, T, c: g.iota(mk(T, out), pat, base, cm, allow_small_or_imprecise_dtypes=True)
     return op("G", e, [], [out], 130 + 2 * CY * cnt(out))
+
+
+def gcp(out, in_):
+    return op("G", lambda g, T, c: g.affine_select(mk(T, out), mk(T, in_), [[0, cnt(out)]], A.is_ge, 0.0, 0, 0), [in_], [out], 170 + 2 * CY * cnt(out))
 
 
 def load(q, out, src, sem, lat):
@@ -274,14 +292,15 @@ def sb(i):
 
 I_ = a("IL", 16, 144)
 B1 = a("Bx", 0, 128, 16)
-B32, Bm16, B16 = [a("BB", 8 * i, 8 * i + 8) for i in range(3)]
-(KC, MG0, MG1, SC, MLO, MHI, M12, AC, AD, MV, N16, PP, K32, P64, MK) = range(15)
+B32, Bm16, B16, Bm8 = [a("BB", 8 * i, 8 * i + 8) for i in range(4)]
+(KC, AC, AD, PP, P8, MK) = range(6)
 (BND, BND2, TH16, TH2, NQ, NJ, E1, FL, S_, QQ, W0, W1, W2, W3, X0, X1, X2, X3, KZ, KO, KX, Z1, T1_, T2_, US, RED, FH, NW, PN, VB, VT, U1, U2, U3, C2, TH) = range(36)
+TINY = 2.0 ** -23
 (CK, POS, PI, NEG, H1, H2, ED_, PF_, NP_, NP2, WEF, WFH) = range(12)
 NL, PC, PTH, KK = a("en", 7, 128, 8), sm(C2), sm(TH), ("KA", "KB")
-OWN, PAR = a("XF", 0, V), a("X", VP, VP + V)
-OWND, PARD = a("XF", 0, NUL), a("X", VP, VP + NUL)
-OWNN, PARN = a("XF", 0, VP), a("X", VP, 2 * VP)
+OWN, PAR, PAR0 = a("XF", 0, V), a("XF", VP, VP + V), a("X", VP, VP + V)
+OWND, PARD = a("XF", 0, NUL), a("XF", VP, VP + NUL)
+OWNN, PARN, PARN0 = a("XF", 0, VP), a("XF", VP, 2 * VP), a("X", VP, 2 * VP)
 WP, WB = t3("PW", (0, 16)), t3("PW", (16, 32))
 WN = a("Wn", 0, 256)
 ZERO, CNUL = a("CC", 0, 16), a("NV", 0, 16)
@@ -301,15 +320,13 @@ def flip(bk, src, r0=0, hs=(0, 2)):
     pe([(t3(bk, (r0 + 8 * h, r0 + 8 * h + 8)), blk(src, h, 128), a("Ih"), True, True) for h in range(*hs)])
 
 
-def tolist(c0, n, nb=8):
-    scan(a("TL", c0, c0 + n), a("DA" if nb == 8 else "DB", 0, n), a("DL", c0, c0 + n), 0.0, A.mult, A.add)
+def tolist(c0, n):
+    scan(a("TL", c0, c0 + n), a("DA", 0, n), a("DL", c0, c0 + n), 0.0, A.mult, A.add)
     bk = dbank()
-    o = lambda j: t3(bk, j * nb // 16, (j * nb % 16, j * nb % 16 + nb))
-    w = lambda j, z: a("B2", 8 * z, 8 * z + 8) if nb == 8 else a("B2", 32 + 16 * z + 4 * j, 36 + 16 * z + 4 * j)
-    ml = [m for j in range(n // 128) for m in ((o(j), a("TL", c0 + 128 * j, c0 + 128 * j + 128), w(j, 0), nb == 8, False),
-                                               (o(j), a("TL", c0 + 128 * j + 1, c0 + 128 * j + 129), w(j, 1), False, False),
-                                               (o(j), a("DL", c0 + 128 * j + 1, c0 + 128 * j + 129), w(j, 0), False, nb == 8 or j == 3))]
-    pe(ml if nb == 8 else [(t3(bk, 0), a("Ih"), a("B2", 64, 80), True, False)] + ml)
+    o = lambda j: t3(bk, j // 2, (j % 2 * 8, j % 2 * 8 + 8))
+    pe([m for j in range(n // 128) for m in ((o(j), a("TL", c0 + 128 * j, c0 + 128 * j + 128), a("B2", 0, 8), True, False),
+                                             (o(j), a("TL", c0 + 128 * j + 1, c0 + 128 * j + 129), a("B2", 8, 16), False, False),
+                                             (o(j), a("DL", c0 + 128 * j + 1, c0 + 128 * j + 129), a("B2", 0, 8), False, True))])
     return bk
 
 
@@ -317,25 +334,23 @@ def consts():
     iota(a("pi", 0, 1), [[0, 1]], 0, 1)
     iota(a("IL"), [[1, 160]], -16, -1)
     iota(a("K16"), [[0, 16], [1, 16]], 0, 0)
-    iota(a("Li"), [[1, 256]], 0, 0)
     iota(a("L2"), [[1, 8], [0, 16]], 0, -1)
-    iota(a("junk", 0, 512), [[0, 16], [1, 32]], 0, 0)
     iota(a("NS8"), [[0, 32], [1, 8]], 0, 0)
     iota(a("RS5"), [[0, 32], [1, 5]], 0, 0)
     iota(a("KN"), [[0, 16], [2, 8]], 1, 0)
     ts(a("L2"), a("L2"), 0.0, A.is_equal)
     ts(a("IL"), a("IL"), 0.0, A.is_equal)
     cp(col(PP), a("pi", 0, 1))
-    for j, (c, m) in enumerate(((KC, 15), (P64, 63), (MG1, 16))):
+    for j, (c, m) in enumerate(((KC, 15), (P8, 7))):
         ts(a("pi", j + 1, j + 2), a("pi", 0, 1), m, A.bitwise_and)
         cp(col(c), a("pi", j + 1, j + 2))
-    ts(col(MG1), col(MG1), 1.0 / 16, A.mult)
-    ts(col(K32), col(PP), 64.0, A.is_ge, 16.0, A.mult)
-    tt(col(K32), col(K32), col(KC), A.add)
-    ts(col(MG0), col(MG1), -1.0, A.mult, 1.0, A.add)
-    ts(col(MLO), col(KC), 8.0, A.is_lt)
-    ts(col(M12), col(KC), 12.0, A.is_equal)
-    ts(col(MHI), col(KC), 12.0, A.is_lt, col(MLO), A.subtract)
+    ts(a("col", MK, MK + 8), a("K16", 0, 8), col(P8), A.is_equal)
+    ts(a("TRI"), a("K16", 0, 64), col(KC), A.is_ge, 32768.0, A.mult)
+    act(sm(VT), a("K16", 0, 16), F.Identity, col(KC), 16.0)
+    act(sm(VB), sm(VT), F.Identity, V * TINY, TINY)
+    ms(t3("DV"), 0.0)
+    for k in (0, 2, 4):
+        ms(t3("DV", None, (16 * k + 8, 16 * k + 16)), -1.0)
     act(a("nIb"), I_, F.Identity, 0.0, -1.0)
     act(a("PENI"), I_, F.Identity, 0.0, PEN)
     cp(a("Ih"), I_)
@@ -345,50 +360,26 @@ def consts():
     act(a("I32"), I_, F.Copy)
     pe([(a("KA", 0, 128), a("L2", p=(0, 8)), a("L2", p=(0, 8)), True, True)])
     act(a("Bx"), a("KA", 0, 128), F.Copy)
-    for x, v in ((B32, 32.0), (Bm16, -16.0), (B16, 16.0)):
+    for x, v in ((B32, 32.0), (Bm16, -16.0), (B16, 16.0), (Bm8, -8.0)):
         act(x, B1, F.Identity, 0.0, v)
     cp(a("B2", 0, 8), B1)
     ts(a("B2", 8, 16), B1, -1.0, A.mult)
-    tt(a("B2", 16, 20), a("Bx", 0, 64, 16), a("Bx", 64, 128, 16), A.add)
-    ts(a("B2", 20, 24), a("K16", 0, 4), 16.0, A.mult)
-    for q in range(4):
-        ts(a("B2", 24, 28), a("B2", 20, 24), float(V + 16 + 64 * q), A.add)
-        tt(a("B2", 32 + 4 * q, 36 + 4 * q), a("B2", 24, 28), a("B2", 16, 20), A.mult)
-    ts(a("B2", 48, 64), a("B2", 32, 48), -1.0, A.mult)
     for nv in sorted(set(x for y in HV + HVL for x in y) - {0}):
-        ts(a("Me", 0, 128), a("K16", 0, 128), float(nv), A.is_lt, -16.0, A.mult)
-        tt(blk("nB", nv, 128), a("Me", 0, 128), a("Bx"), A.mult)
+        lin(blk("nB", nv, 128), a("Bx"), -16.0)
+        for c in range(nv, 4):
+            ms(a("nB", 128 * nv + c, 128 * nv + 128, 4), 0.0)
     for z in range(2):
         ts(blk("DA", z), a("K16"), col(KC), A.is_le)
     ms(a("DA", 0, 512, 16), 0.0)
-    ts(a("DB"), a("junk", 0, 512), col(K32), A.is_le)
-    ms(a("DB", 0, 512, 32), 0.0)
-    ts(col(MV), col(KC), 12.0, A.is_lt, BIG, A.mult)
-    for z in range(2):
-        tt(col(MK + z), col(MG0 + z), col(MV), A.mult)
-        ts(col(MK + 2 + z), col(MG0 + z), col(M12), A.mult, 256.0, A.mult)
-    ts(col(N16), col(M12), -16.0, A.mult)
-    ts(a("KM"), a("K16", 0, 16), col(KC), A.is_equal)
-    act(blk("CC", 0), a("K16"), F.Identity, 0.0, 0.0)
-    ts(a("B2", 64, 80), ZERO, col(KC), A.add, -16.0, A.add)
+    act(a("CC", 0, 16), a("K16", 0, 16), F.Identity, 0.0, 0.0)
     for h in range(2):
         ts(a("NV", 16 + 8 * h, 24 + 8 * h), a("CC", 0, 8), col(PP), A.add, float(CEN + 128 * h), A.add)
-    for x, v in ((a("ZW"), 0.0), (a("DL"), 0.0), (a("TL", 0, 1808, 128), 0.0), (a("RC"), 0.0), (a("R1"), 1.0)):
+    for x, v in ((a("Wn", 256, 272), 0.0), (t3("Wz"), 0.0), (a("DL"), 0.0), (a("TL", 0, 1168, 128), 0.0), (a("RC"), 0.0), (a("R1"), 1.0)):
         ms(x, v)
     for z in range(2):
         cp(a("RC", 80 * z + 4, 80 * z + 80, 5), a("NV", 16, 32))
     for c0 in (1, 4, 160, 164):
         ms(a("R1", c0, c0 // 160 * 160 + 160, 5), 0.0)
-    for q in range(4):
-        act(col(AD), col(P64), F.Identity, 4096.0 * (64 * q - 12 * 256), 4096.0)
-        act(sm(VB, 4, 4 * q), a("K16", 0, 4), F.Identity, col(AD), 0.0)
-    act(sm(VT), sm(VB), F.Identity, 0.0, -1.0)
-    for b in range(16):
-        if VQ[b] == "S" and (b == 0 or VQ[b - 1] == "V"):
-            n = len(VQ[b:]) - len(VQ[b:].lstrip("S"))
-            lin(sm(VT, n, b), sm(VB, n, b), 0.0)
-    for z in range(2):
-        act(blk("CR", z), a("Li"), F.Identity, 0.0, col(N16))
     act(a("RS5"), a("RS5"), F.Relu, 16 * BIG, -16 * BIG)
     act(a("NS8"), a("NS8"), F.Sign)
     act(a("nPEN"), I_, F.Identity, 0.0, -PEN)
@@ -400,29 +391,15 @@ def consts():
     for k in (14, 15):
         act(a("KI", k, 256, 16), a("K16", 0, 16), F.Identity, PEN, 0.0)
     act(a("KH"), a("K16"), F.Identity, 0.0, 1.0 / 16)
-    for x, v in ((a("XF", V, NUL), 0.0), (a("X", VP + V, VP + NUL), 0.0), (a("XF", NUL, VP), DEAD), (a("X", VP + NUL, 2 * VP), -DEAD), (sm(U1), 0.5), (sm(U2), 0.0),
-                 (a("Wn", 256, 272), 0.0), (CNUL, float(NUL - CEN)), (a("DK"), 1.0), (t3("TA"), 0.0), (t3("TB"), 0.0), (a("pd", 0, 8), 0.0), (a("pd", 264, 272), 0.0)):
+    for x, v in ((a("XF", V, NUL), LIFT), (a("X", VP + V, VP + NUL), 0.0), (a("XF", NUL, VP), LIFT + DEAD), (a("X", VP + NUL, 2 * VP), 2 * DEAD),
+                 (a("XF", VP + V, VP + NUL), LIFT), (a("XF", VP + NUL, 2 * VP), LIFT + 2 * DEAD),
+                 (CNUL, float(NUL - CEN)), (a("DK"), 1.0), (t3("TA"), 0.0), (t3("TB"), 0.0), (a("pd", 0, 8), 0.0), (a("pd", 264, 272), 0.0)):
         ms(x, v)
-    for x, v in ((a("xc"), DEAD), (a("DN"), -DEAD), (a("ones"), 1.0), (a("RF"), 0.0), (a("RB"), 0.0),
+    for x, v in ((blk("DF", 0), LIFT + DEAD), (blk("DF", 1), LIFT + 2 * DEAD), (a("ones"), 1.0), (a("RF"), 0.0), (a("RB"), 0.0),
                  (blk("DM", 0), 0.0), (blk("DM", 1), 0.0), (blk("DM", 2), 4096.0), (blk("G0", 0), 1.0), (blk("G1", 0), 0.0), (blk("G1", 1), -1.0), (blk("CC", 3), -0.5),
                  (a("G0", 15, 256, 16), 0.0), (a("G1", 271, 512, 16), -40.0), (a("RF", 14, 256, 16), BIG), (sb(CK), -K0)):
         either(ms(x, v), act(x, a("K16", 0, cnt(x)), F.Identity, v, 0.0))["r"] = regs(a("K16"))
-    act(a("DF"), a("xc"), F.Silu)["cost"] += 1300
-    act(a("CT", V, NUL), a("K16"), F.Identity, 0.0, 0.0)
-    scan(sm(U3, 8), sm(U1, 8), sm(U2, 8), 1.0, A.mult, A.add)
-    cp(sm(U3, 4, 8), sm(U3, 4))
-    tt(sm(Z1, 12), sm(U3, 12), a("KM", 0, 12), A.mult)
-    red(col(SC), sm(Z1, 12), A.add)
-    ts(a("tq"), a("Li"), 0.5, A.add, col(SC), A.mult)
-    ts(a("xa"), a("tq"), M1, A.add, M1, A.subtract)
-    act(a("xb"), a("xa"), F.Identity, 0.0, -1.0)
-    pe([(a("KB", 0, 256), a("I32"), a("tq"), True, False), (a("KB", 0, 256), a("I32"), a("xb"), False, True)])
-    act(a("m2"), a("KB", 0, 256), F.Sign)
-    act(a("Lo"), a("m2"), F.Identity, 0.0, col(MLO))
-    act(a("Hi"), a("m2", 0, 16), F.Identity, 0.0, col(MHI))
-    for c in range(V // 256):
-        x = a("Hi", c, c + 1)
-        either(ts(blk("CT", c), a("Lo"), x, A.add), act(blk("CT", c), a("Lo"), F.Identity, x))["prio"] = 4000.0
+    act(a("DF", 0, 16), a("DF", 0, 16), F.Silu)["cost"] += 1300
 
 
 def cands(h, tab, lst, hs):
@@ -432,23 +409,24 @@ def cands(h, tab, lst, hs):
     flip("PT", "Cc", 16 * h, hs)
 
 
-def paths():
-    act(a("de"), t3("PW", (0, 16), (0, 16, 2)), F.Identity, 1700.0 * 64, -64.0)
+def paths(r):
+    ts(a("de"), a("Wn", 0, 256, 2), -64.0, A.mult, 1700.0 * 64, A.add)
     scan(a("es"), a("de"), a("Wn", 0, 256, 2), 0.0, A.max, A.min)
     cp(a("DL", 0, 256, 16), a("es", 7, 128, 8))
     ts(a("el"), t3(tolist(0, 256), 0), float(CEN), A.add)
     scan(a("en"), a("de"), a("KN"), 0.0, A.max, A.min)
-    bk = dbank()
-    for z in range(2):
+    if r < RO - 1:
+        bk = dbank()
         for h in range(2):
-            cp(a("ZW", 128 * (2 * z + h) + h, 128 * (2 * z + h) + 128, 2), a("Wn", 128 * h + z, 128 * h + 128, 2))
-    pe([(t3(bk, (8 * z, 8 * z + 8)), blk("ZW", 2 * z + h, 128), a("Ih"), h == 0, h == 1) for z in range(2) for h in range(2)])
-    for z in range(2):
-        ts(blk("WO", z, 128), t3(bk, (8 * z, 8 * z + 8)), float(CEN), A.add)
+            o, x = t3("Wz", (8 * h, 8 * h + 8), (16 * h, 16 * h + 16)), blk("Wn", h, 128)
+            either(cp(o, x), gcp(o, x)) if r else cp(o, x)
+        pe([(t3(bk, (8 * z, 8 * z + 8)), t3("Wz", (8 * h, 8 * h + 8), (z, 32, 2)), a("Ih"), h == 0, h == 1) for z in range(2) for h in range(2)])
+        ts(a("WO"), t3(bk, (0, 16)), float(CEN), A.add)
     for nm, z, n in (("WXo", 1, 6), ("WXe", 0, 7)):
         act(t3(nm, None, (0, n)), t3("PW", (0, 16), (z, z + 2 * n, 2)), F.Copy)
-        act(t3(nm, None, (n, 2 * n)), t3(nm, None, (0, n)), F.Copy)
-        act(t3(nm, None, (2 * n, 4 * n)), t3(nm, None, (0, 2 * n)), F.Copy)
+        for m in (n, 2 * n):
+            o, x = t3(nm, None, (m, 2 * m)), t3(nm, None, (0, m))
+            either(act(o, x, F.Copy), gcp(o, x) if r else cp(o, x))
     cands(0, "CA", "el", (0, 2))
 
 
@@ -464,22 +442,21 @@ def fit(h, hs):
 def hop(h, H, win, nv):
     for j in range(4 * H, 4 * H + 4):
         gather(blk("XC", j, 512), ind(win, blk("CO", 8 * h + j, 32)))
-    xs, xc, mm = blk("xs", 2 * h + H, 128), lambda i: a("XC", 2048 * H + i, 2048 * H + 2048, 16), lambda i: blk("MM", 16 * H + i, 128)
-    key = lambda i: a(KK[H], i, 128, 16)
+    xs, xc = blk("xs", 2 * h + H, 128), lambda i, st=16: a("XC", 2048 * H + i, 2048 * H + 2048, st)
+    mm, key = lambda c, j=0, st=1: a("MM", 2048 * H + 512 * c + j, 2048 * H + 512 * c + 512, st), lambda i: a(KK[H], i, 128, 16)
+    four = lambda bk, w, first: [(t3(bk, None, (j, 16, 4)), w, xs, first and j == 0, j == 3) for j in range(4)]
     if nv:
-        pe([(a(KK[H], 0, 128), xs, blk("nB", nv, 128), False, False)] + [(key(i), xc(i), Bm16, False, False) for i in range(nv)], True)
-        for i0 in range(0, nv, XS):
-            xe = t3(dbank(), (0, 8))
-            pe([(xe, I_, xs, True, True)])
-            for i in range(i0, min(nv, i0 + XS)):
-                tt(mm(i), xc(i), xe, A.max)
-            pe([(key(i), mm(i), B32, False, False) for i in range(i0, min(nv, i0 + XS))], True)
-    for i0 in range(nv, 16, 4):
-        bk, js = dbank(), range(i0, min(16, i0 + 4))
-        o = lambda i: t3(bk, (8 * (i - i0), 8 * (i - i0) + 8))
-        pe([m for i in js for m in ((o(i), I_, xc(i), True, False), (o(i), a("nIb"), xs, False, True))])
-        act(blk("MM", 16 * H + i0, 128, 0, 128 * len(js)), t3(bk, (0, 8 * len(js))), F.Abs, 0.0, 0.5)
-        pe([(key(i), mm(i), B32, False, False) for i in js], True)
+        pe([(a(KK[H], 0, 128), xs, blk("nB", nv, 128), False, False)] + [(key(i), xc(i), Bm16, False, False) for i in range(16) if i % 4 < nv], True)
+        xe = dbank()
+        pe(four(xe, I_, True))
+        for c in range(nv):
+            tt(mm(c), xc(c, 4), t3(xe), A.max)
+    for c in range(4):
+        if c >= nv:
+            bk = dbank()
+            pe([(t3(bk), I_, xc(c, 4), True, False)] + four(bk, a("nIb"), False))
+            act(mm(c), t3(bk), F.Abs, 0.0, 0.5)
+        pe([(key(c + 4 * j), mm(c, j, 4), B32, False, False) for j in range(4)], True)
     pe([(a(KK[H], 0, 16), I_, ZERO, False, True)])
     key, pm, eq, ne, y = a(KK[H], 0, 128), blk("pm", 2 * h + H, 128), blk("eq", H, 128), blk("eq", 2 + H, 128), blk("Y", H, 128)
     scan(pm, a("RST", 0, 128), key, 0.0, A.add, A.min)
@@ -489,17 +466,17 @@ def hop(h, H, win, nv):
     scan(blk("YS", 2 * h + H, 128), ne, y, 0.0, A.mult, A.add)
 
 
-def row(h, k, nm="VV"):
-    return a(nm, 2048 * (k & 1) + 2 * (k // 2) + h, 2048 * (k & 1) + 2048, 16)
+def row(h, k, nm="VV", n=2048):
+    return a(nm, 2048 * (k & 1) + k // 2 + 8 * h, 2048 * (k & 1) + n, 16)
 
 
 def rows(r):
     for j in range(8):
-        gather(blk("VV", j, 512), ind(OWNN if j < 4 else PARN, blk("WO", j, 32)))
+        gather(blk("VV", j, 512), ind(OWNN if j < 4 else PARN if r else PARN0, blk("WO", j, 32)))
     if r > 0:
         pe([(a("PE", 0, 256), I_, a("K16"), True, False)]
            + [(a("PE", 128 * h + k, 128 * h + 128, 16), row(h, k), Bm16, False, False) for h in range(2) for k in range(0, 16, 2)])
-        pe([(a("PE", 128 * h + k, 128 * h + 128, 16), row(h, k), B16, False, h == 1 and k == 15) for h in range(2) for k in range(1, 16, 2)])
+        pe([(a("PE", 128 * h + k, 128 * h + 128, 16), row(h, k), Bm8, False, h == 1 and k == 15) for h in range(2) for k in range(1, 16, 2)])
         scan(a("pd", 8, 264), a("RST"), a("PE", 0, 256), 0.0, A.add, A.min)
 
 
@@ -550,9 +527,6 @@ def cut():
     act(sm(PN), sb(POS), F.Identity, ST + 4096.0, 4096.0)
     tt(sm(NW), sm(NW), sm(PN), A.add)
     tt(a("Wf", 0, 256, 16), a("Wf", 0, 256, 16), sm(NW), A.min)
-    w15 = t3("PW", (16, 32), 15)
-    pe([(WB, a("Ih"), a("Wb"), True, False), (WB, a("nIh"), a("Wf"), False, False), (w15, a("nIh"), a("Wb", 15, 256, 16), False, False),
-        (w15, a("Ih"), a("Wf", 15, 256, 16), False, True)])
 
 
 def edges(r, t):
@@ -570,13 +544,19 @@ def edges(r, t):
             act(blk("ED", 16 * t + j0, 128, 0, 128 * len(js)), t3(bk, (0, 8 * len(js))), F.Abs)
             pe([(key(h, k), blk("ED", 16 * t + j0 + j, 128), B16, False, False) for j, (h, k) in js], True)
     else:
+        nc = int(EA[r][0])
         for z in range(2):
-            pe([(key(h, k), row(h, k + z), Bm16, False, False) for h, k in hk], True)
-        for c in range(4 * (t == 0 or EA[r][0] == "S")):
-            bk = dbank()
-            pe([(t3(bk), I_, blk("VV", 4 + c, 512), True, True)])
-            for u in ((0, 1) if EA[r] == "VV" else (t,)):
-                tt(blk("ED", 4 * u + c, 512), blk("VV", c, 512, 2 * u, 512), t3(bk), A.max)
+            pe([(key(h, k)[:5] + ((0, 32 * nc),), row(h, k + z, "VV", 512 * nc), Bm16, False, False) for h, k in hk], True)
+        for c in range(4):
+            if c >= nc:
+                bk = dbank()
+                pe([(t3(bk), I_, blk("VV", 4 + c, 512), True, False), (t3(bk), a("nIb"), blk("VV", c, 512, t, 512), False, True)])
+                act(blk("ED", 4 * t + c, 512), t3(bk), F.Abs, 0.0, 0.5)
+            elif t == 0:
+                bk = dbank()
+                pe([(t3(bk), I_, blk("VV", 4 + c, 512), True, True)])
+                for u in range(2):
+                    tt(blk("ED", 4 * u + c, 512), blk("VV", c, 512, u, 512), t3(bk), A.max)
         pe([(key(h, k), row(h, k, "ED"), B32, False, False) for h, k in hk], True)
 
 
@@ -620,6 +600,44 @@ def ends(r):
     pe([(a("PE", 256, 416), a("Ih"), a("RC"), True, False)] + [m + (False, r == 0 and i == len(ml) - 1) for i, m in enumerate(ml)])
 
 
+def equal():
+    dv, ra, rb = lambda k: t3("DV", None, (16 * k + 8, 16 * k + 16)), a("ra", 4, 80, 5), a("ra", 84, 160, 5)
+    ts(dv(6), ra, 1.0 / 2048, A.mult)
+    ts(dv(8), ra, 1.0 / 2048, A.mult)
+    cp(dv(7), rb)
+    tt(sm(VT), ra, rb, A.mult)
+    ts(dv(1), sm(VT), 1.0 / 2048, A.mult)
+    act(sm(RED), sm(VT), F.Identity, 0.0, 1.0 / 2048)
+    tt(dv(3), sm(RED), dv(1), A.subtract)
+    bk = dbank()
+    pe([(t3(bk, (8 * j, 8 * j + 8)), t3("DV", h, (c0, c0 + 128)), a("Ih"), j > 0 or h == 0, j > 0 or h == 1)
+        for j, h, c0 in ((0, 0, 8), (0, 1, 0), (1, 0, 24), (2, 0, 16), (3, 1, 16))])
+    cp(a("RT"), t3(bk))
+    for gm in range(8):
+        ts(t3("LL", None, (16 * gm, 16 * gm + 16)), a("RT", 0, 128), col(MK + gm), A.mult)
+    c1 = 0
+    for i, (q, bs) in enumerate(VQ):
+        ns = [16 * b + 16 for b in bs]
+        if q == "D":
+            bk = dbank()
+            part = [t3(bk, (0, bs[0] + 1)), t3(bk, (bs[0] + 1, bs[0] + bs[1] + 2))]
+            tri = t3(bk, (bs[0], bs[0] + bs[1] + 2, bs[1] + 1))
+        else:
+            part = [t3(q, j, (128 - n, 128)) for j, n in enumerate(ns)]
+            tri = t3(q, None, (112, 128))
+        pe([(part[j], t3("LL", b % 8), blk("RT", 1 + b // 8, 128, 0, ns[j]), j == 0, False) for j, b in enumerate(bs)]
+           + [(tri, I_, a("TRI", 0, cnt(tri)), False, True)])
+        if q == "D":
+            act(a("MM", c1, c1 + sum(ns)), t3(bk, (0, sum(ns) // 16)), F.Abs)
+        for j, b in enumerate(bs):
+            n = ns[j]
+            if q == "D":
+                scan(a("ED", 128 * b + 128 - n // 2, 128 * b + 128), a("MM", c1, c1 + n // 2), a("MM", c1 + n // 2, c1 + n), BIG, A.min, A.min)
+                c1 += n
+            else:
+                red(a("ED", 128 * b + 127, 128 * b + 128), part[j], A.min)
+
+
 def program():
     for i in range(NCH):
         load("Y", blk("X", i, CW), (lambda i: lambda T: T.pts[:, CW * i:CW * i + CW])(i), "lx%d" % i, 2200 + 400 * i)
@@ -633,13 +651,14 @@ def program():
     left = op(None, None, [a("X", 0, V)], [], 0, tok=("ls0", None), lat=5000, after=ss)
     for i in range(NCH):
         load("Y", blk("CA", i, CW), (lambda i: lambda T: T.cand[:, CW * i:CW * i + CW])(i), "lk%d" % i, 3000 + 1500 * i)["after"].append(left)
-    op(None, None, [], [PAR], 0, tok=("xarr", None), lat=8000, after=ss)
+    op(None, None, [], [PAR0], 0, tok=("xarr", None), lat=8000, after=ss)
     for i in range(NCH):
         ts(blk("CU", i, CW), blk("CA", i, CW), float(-CEN), A.add)
-        sc = op("G", (lambda i: lambda g, T, c: c["big"]("C", i))(i), [blk("CU", i, CW), PAR], [], RI, track=False, after=ss)
+        sc = op("G", (lambda i: lambda g, T, c: c["big"]("C", i))(i), [blk("CU", i, CW), PAR0], [], RI, track=False, after=ss)
         op(None, None, [], [blk("CQ", i, CW)], 0, tok=("ca%d" % i, None), lat=13000 + 1000 * i, after=[sc])
     for i in range(2 * NCH):
-        gather(blk("XF", i, CW // 2), blk("X", i, CW // 2))
+        lin(blk("XF", i, CW // 2), blk("X", i, CW // 2), 1.0, LIFT)
+        lin(blk("XF", i, CW // 2, VP), blk("X", i, CW // 2, VP), 1.0, LIFT)
     consts()
     for j in range(2 * NCH):
         bk = t3(dbank(), (0, CW // 32))
@@ -659,7 +678,7 @@ def program():
     tt(a("Wf"), WP, blk("UM", 2), A.max)
     ts(WN, a("Wf"), float(NUL - CEN), A.min)
     pe([(WP, a("Ih"), WN, True, True)])
-    paths()
+    paths(0)
     rows(0)
     edges(0, 0)
     edges(0, 1)
@@ -671,47 +690,28 @@ def program():
         cp(a("DL", 512, 1024, 16), a("ra", 4, 160, 5))
         bk = t3(tolist(512, 512), (0, 2))
         ts(a("ab"), bk, float(CEN), A.add)
-        lin(a("abf"), bk, 1.0, float(CEN))
+        lin(a("abf"), bk, TINY, CEN * TINY)
         if r > 0:
-            paths()
-        for z in range(2):
-            tt(blk("RR", z), ind(a("CT"), blk("ab", z, 16)), blk("CR", z), A.add)
-            for gm in range(2):
-                o, x = t3("LL", (4 * z, 4 * z + 4), (64 * gm, 64 * gm + 64)), blk("RR", z)
-                either(ts(o, x, col(MK + gm), A.mult, col(MK + 2 + gm), A.add), act(o, x, F.Identity, col(MK + 2 + gm), col(MK + gm)))
+            paths(r)
+        equal()
         mid, rmid = blk("mid", r), blk("rmid", r)
         for z in range(2):
-            gather(blk("xm", z), ind((OWND, PARD)[z], blk("ab", z, 16)))
+            gather(blk("xm", z), ind((OWND, PARD if r else PARN0)[z], blk("ab", z, 16)))
         bk = t3(dbank(), (0, 16))
         group(bk, [(I_, blk("xm", 0)), (I_, blk("xm", 1)), (I_, blk("CC", 3))])
         act(a("xc"), bk, F.Identity, M2)
         act(mid, a("xc"), F.Identity, -0.5 * M2, 0.5)
+        lin(blk("DF", 2), a("xc"), 0.5, LIFT - 0.5 * M2)
 
         def e(g, T, c, r=r, mid=mid, rmid=rmid):
             c["one"](mk(T, rmid), mk(T, mid), "am%d" % r)
         s = op("G", e, [mid], [], RI, track=False)
         op(None, None, [], [rmid], 0, tok=("am%d" % r, None), lat=RL + 2000, after=[s])
-        nv = ns = 0
-        for b in range(15, -1, -1):
-            n, pp = 64 * (b // 4 + 1), (32 * (b % 4), 32 * (b % 4) + 32)
-            if VQ[b] == "V":
-                nv += 1
-                bk = ("PE", "KA", "KB")[nv % 3]
-                part = lambda c0, c1: a(bk, c0, c1)
-            else:
-                ns += 1
-                bk = dbank()
-                part = lambda c0, c1: t3(bk, (c0 // 16, c1 // 16))
-            pe([(part(n * z, n * z + n), t3("LL", 4 * z + b // 4, p=pp), a("RR", 256 * z, 256 * z + n, p=pp), True, True) for z in range(2)])
-            if VQ[b] == "V":
-                red(sm(RED, 1, b), part(0, 2 * n), A.max)
-            else:
-                act(blk("junk", ns % 3, 512, 0, 2 * n), part(0, 2 * n), F.Relu, sm(VB, 1, b), 1.0, sm(RED, 1, b))
-        tt(a("DL", 1280, 1792, 32), sm(RED), sm(VT), A.is_gt)
-        bk = t3(tolist(1280, 512, 4), 0)
+        lin(blk("DF", 3), rmid, 1.0, LIFT)
+        tt(sm(RED), sm(VB), a("ED", 127, 2048, 128), A.subtract)
         for z in range(2):
-            tt(blk("ef", z, 16), bk, blk("abf", z, 16), A.max)
-        cp(blk("eff", r, 32), a("ef"))
+            tt(blk("ef", z, 16), sm(RED), blk("abf", z, 16), A.max)
+        ts(blk("eff", r, 32), a("ef"), 1.0 / TINY, A.mult)
         ea, eb, ra, rk = blk("eff", 2 * r, 16), blk("eff", 2 * r + 1, 16), blk("rl", 2 * r, 16), blk("rl", 2 * r + 1, 16)
 
         def e(g, T, c, r=r, ea=ea, eb=eb, ra=ra, rk=rk):
@@ -720,7 +720,7 @@ def program():
         op(None, None, [], [ra], 0, tok=("aa%d" % r, None), lat=RL, after=[s])
         op(None, None, [], [rk], 0, tok=("ak%d" % r, None), lat=RL, after=[s])
         if not last:
-            act(a("wn", 0, 16), a("ef", 0, 16), F.Sign, V - 0.5, -1.0)
+            act(a("wn", 0, 16), a("ef", 0, 16), F.Sign, V - 0.5, -1.0 / TINY)
             o = slot()
             pe([(o, a("ones"), a("wn", 0, 16), True, True)])
             act(sm(U2), o, F.Identity, (1024 - 15.5) / 16, 0.5, col(AC))
@@ -729,14 +729,12 @@ def program():
             act(col(AC), col(AC), F.Identity, col(AD), 128.0)
             act(sm(BND, 32), sm(TH16, 32), F.Identity, col(AC))
         fit(0, (0, 2))
-        cp(ind(OWND, ea), mid)
-        cp(ind(PARD, ra), rmid)
-        cp(ind(PARD, eb), a("DN"))
-        x = ind(OWND, rk)
-        either(cp(x, a("DF")), op("S", lambda g, T, c, x=x: g.scalar.activation(mk(T, x), mk(T, a("DF")), F.Silu), [a("DF"), rk], [OWND],
-                                  65 + SCA * CY * 256))
+        for w, o, x in ((OWND, ea, blk("DF", 2)), (PARD, eb, blk("DF", 1)), (OWND, rk, blk("DF", 0))):
+            scatter(w, o, x)
+        lin(blk("DF", 4), ind(PARD, ra), 2.0, -LIFT - 2 * DEAD)
+        tt(ind(PARD, ra), blk("DF", 3), blk("DF", 4), A.max)
         hv = HVL if last else HV
-        ts(blk("xs", 0), ind(OWN, a("el")), 255.0, A.min)
+        ts(blk("xs", 0), ind(OWN, a("el")), -LIFT, A.add, 255.0, A.min)
         if not last:
             bk = dbank()
             pe([(t3(bk, 0, (8 * H, 8 * H + 8)), blk("xs", H, 128), Bm16, True, True) for H in range(2)])
@@ -748,8 +746,7 @@ def program():
             cp(a("DL", c0, c0 + 128, 16), a("YS", 128 * H + 15, 128 * H + 128, 16))
             ts(fl, t3(tolist(c0, 128), 0, (0, 8)), float(CEN), A.add)
             cands(1, "CP", "fl", (H, H + 1))
-            x = blk("xs", 2 + H, 128)
-            either(ts(x, ind(PAR, fl), 0.0, A.max), act(x, ind(PAR, fl), F.Relu))
+            gather(blk("xs", 2 + H, 128), ind(PAR, fl))
         k1, k2 = a("pm", 15, 256, 16), a("pm", 271, 512, 16)
         act(sb(H1), k1, F.Relu, -16.0 * THR, 16.0)
         act(sb(H2), NL, F.Relu, -13.0 * BIG, BIG)
@@ -769,8 +766,8 @@ def program():
             lin(PTH, o, 1.0, THR)
 
         def second(H):
-            if H == 0:
-                fit(1, (0, 2))
+            if last or H == 0:
+                fit(1, (H, H + 1) if last else (0, 2))
             hop(1, H, OWN, hv[1][H])
         if last:
             act(a("G1", 270, 512, 16), NL, F.Identity, 13.5, -1.0)
@@ -778,8 +775,8 @@ def program():
             tt(a("Wf"), WP, a("Me"), A.mult)
             for i in range(2 * NCH):
                 if i < OS:
-                    act(blk("X", i, CW // 2), blk("XF", i, CW // 2), F.Copy)
-                ts(blk("XO", i, CW // 2), blk("X" if i < OS else "XF", i, CW // 2), 255.0, A.min)
+                    act(blk("X", i, CW // 2), blk("XF", i, CW // 2), F.Identity, -LIFT)
+                ts(blk("XO", i, CW // 2), blk("X" if i < OS else "XF", i, CW // 2), -LIFT * (i >= OS), A.add, 255.0, A.min)
             store(lambda T: T.yx[:, :], lambda T: T.XO[:, :], a("XO"), "ox", 9000)
         steps = {"r": lambda: rows(r + 1), "c": cut, "k": keys, "0": lambda: edges(r + 1, 0), "1": lambda: edges(r + 1, 1), "e": lambda: ends(r + 1),
                  "b": bounds, "A": lambda: second(0), "B": lambda: second(1)}
@@ -795,9 +792,10 @@ def program():
             pe([(pick(z, c), a(w), x, False, False) for z in range(2) for c, w, x in
                 ((0, "PENI", ng), (1, "nPEN", ng), (2, "PENI", ng), (0, "PENI", sb(WFH)), (2, "PENI", sb(WFH)), (3, "nPEN", sb(WFH)))])
             pe([(pick(0, 3), a("Ih"), a("YS", 271, 512, 16), False, True)])
+            pe([(WP, a("Ih"), a("Wf"), True, False), (WB, a("Ih"), a("Wb"), False, False), (t3("PW", (0, 16), 15), a("nPEN"), a("G1", 15, 256, 16), False, False)]
+               + [(t3("PW", (16 + 8 * h, 24 + 8 * h)), a("PENI"), a("ones"), False, False) for h in range(2)])
             scan(rev("GU", 0, 256), rev("G0", 0, 256), rev("G1", 0, 256), 0.0, A.mult, A.add)
-            tt(a("TS"), WB, blk("GU", 0), A.mult)
-            pe([(WP, a("Ih"), a("Wf"), True, False), (WP, a("I32"), a("TS"), False, True)])
+            pe([(WP, a("PENI"), blk("GU", 0), False, False), (WB, a("nPEN"), blk("GU", 0), False, True)])
         scan(rev("GU", 256, 512), rev("G0", 0, 256), rev("G1", 256, 512), 0.0, A.mult, A.add)
         ts(a("OA"), blk("GU", 1), M2, A.add, M2, A.is_equal)
         if last:
@@ -805,16 +803,16 @@ def program():
         else:
             lin(a("NU"), a("OA"), -3968.0, float(NUL - CEN))
             tt(a("XV"), t3(vb, (0, 16)), a("NU"), A.max)
-            tt(WN, WP, a("XV"), A.min)
+            tt(a("Wf"), WP, a("XV"), A.min)
+            tt(WN, WB, a("Wf"), A.min)
             pe([(WP, a("Ih"), WN, True, True)])
     act(sm(U1), ng, F.Identity, 2.0, -2.0)
     tt(a("wn", 16, 32), sm(U1), NL, A.add)
-    pe([(a("KA", 128 * h, 128 * h + 128, p=p8), a("wn", 16 + 8 * h, 24 + 8 * h), I_, True, True) for h in range(2)])
-    act(a("yc", p=p8), a("KA", 0, 256, p=p8), F.Copy)
-    bk = dbank()
-    pe([(t3(bk, (8 * h, 8 * h + 8)), blk(x, h, 128), w, i == 0, i == 3) for h in range(2)
-        for i, (x, w) in enumerate((("Wf", a("Ih")), ("Me", a("CI")), ("XV", a("Ih")), ("OA", a("CI"))))])
-    gather(a("yo"), t3(bk, (0, 16)))
+    pe([(t3("KA", h, None, p8), a("wn", 16 + 8 * h, 24 + 8 * h), I_, True, True) for h in range(2)])
+    act(a("yc", p=p8), t3("KA", (0, 2), None, p8), F.Copy)
+    for i, (x, w) in enumerate((("Wf", a("Ih")), ("Me", a("CI")), ("OA", a("CI")), ("XV", a("Ih")))):
+        pe([(blk("PE", h, 128), blk(x, h, 128), w, i + h == 0, i + h == 4) for h in range(2)])
+    gather(a("yo"), a("PE", 0, 256))
     store(lambda T: T.yw[:, :], lambda T: T.yo[:, :], a("yo"), "ow", 2500)
     store(lambda T: T.yn[:, :], lambda T: T.yc[0:8, :], a("yc"), "on", 2500)
 
@@ -858,8 +856,8 @@ def polish(sch, dl, ways, lat, head, rs, moves):
                     t = end[d] + w
             end[n] = t + cost[n]
 
-    def behind(p1):
-        for n in order[p1::-1]:
+    def behind(p1, p0=0):
+        for n in reversed(order[p0:p1 + 1]):
             m = mn[n]
             t = tail[m] if m >= 0 and tail[m] > lat[n] else lat[n]
             for d, w in sl[n]:
@@ -904,8 +902,21 @@ def polish(sch, dl, ways, lat, head, rs, moves):
     behind(N - 1)
     cur = max(end[n] + lat[n] for n in range(N))
     keep = (cur, list(order), list(way), [list(h) for h in banks], list(end), list(cost))
-    crit = [n for n in range(N) if end[n] - cost[n] + tail[n] > cur - SLACK and eng[n]]
-    for it in range(moves):
+    wb = N
+    for it in range(moves + 1):
+        if it % STAY == 0 or it == moves:
+            ahead(0, N)
+            behind(N - 1)
+            cur = max(end[n] + lat[n] for n in range(N))
+            if cur < keep[0]:
+                keep = (cur, list(order), list(way), [list(h) for h in banks], list(end), list(cost))
+            if it == moves:
+                break
+            wa = max(0, wb - WIN // 2) if wb < N else 0
+            wb = min(N, wa + WIN)
+            crit = [n for n in order[wa:wb] if end[n] - cost[n] + tail[n] > cur - SLACK and eng[n]]
+        if not crit:
+            continue
         v = crit[int(rs.randint(len(crit)))]
         beg, x, undo = end[v] - cost[v], rs.rand(), None
         p0 = p1 = pos[v]
@@ -977,18 +988,17 @@ def polish(sch, dl, ways, lat, head, rs, moves):
         ahead(p0, p2)
         lim = cur + COOL * (1.0 - it / moves) * -np.log(1.0 - rs.rand())
         ok = max(end[n] - cost[n] + tail[n] for n in order[p1 + (p1 + 1 < p2):p2]) <= lim
-        if ok:
-            ahead(p2, N)
-            new = max(end[n] + lat[n] for n in order[-200:])
-            ok = new <= lim
+        p3 = max(p2, wb)
+        if ok and p3 > p2:
+            ahead(p2, p3)
+            ok = max(end[n] - cost[n] + tail[n] for n in order[p2:p3]) <= lim
             if not ok:
                 was = None
         if ok:
-            cur = new
-            behind(N - 1 if undo == 1 else p1)
-            crit = [n for n in range(N) if end[n] - cost[n] + tail[n] > cur - SLACK and eng[n]]
-            if cur < keep[0]:
-                keep = (cur, list(order), list(way), [list(h) for h in banks], list(end), list(cost))
+            behind(p3 - 1 if undo == 1 else p1, min(p0, wa))
+            len_ = [end[n] - cost[n] + tail[n] for n in order[wa:wb]]
+            cur = max(len_)
+            crit = [n for n, x in zip(order[wa:wb], len_) if x > cur - SLACK and eng[n]]
             continue
         if undo == 0:
             unlink(v)
@@ -1009,7 +1019,7 @@ def polish(sch, dl, ways, lat, head, rs, moves):
             for t, n in zip(*was):
                 end[n] = t
         else:
-            ahead(p0, N)
+            ahead(p0, p3)
     cur, order, way, banks, end, cost = keep
     beg = [end[n] - cost[n] for n in range(N)]
     for i, n in enumerate(order):

@@ -16,23 +16,25 @@ K0 = 8.0 - 1.0 / 32
 M1 = 1.5 * 2 ** 23
 M2 = 1.5 * 2 ** 24
 M16 = 1.5 * 2 ** 27
-HV = [[3, 3], [3, 2]]
-HVL = [[2, 2], [2, 2]]
+HV = [[3, 3], [3, 3]]
+HVL = [[2, 2], [3, 3]]
 EA = ["22", "SS", "SS", "SS"]
 VQ = (("D", (15, 14)), ("KA", (7, 6, 5, 4)), ("D", (13, 12)), ("D", (11, 10)), ("KB", (3, 2, 1, 0)), ("D", (9, 8)))
 STEPS = "rc0A1kBbe"
 XS = 4
 OS = 6
-SEED, TRIES = 3, 60
-FIRST = 1000000
-MOVES = 300000
+SEED, TRIES = 8, 30
+FIRST = 800000
+MOVES = 250000
+STARTS = 1
+KIND, DEAR, SLOW = ((1.0, 1.0), (0.9, 1.24), (0.84, 1.3), (0.8, 1.4)), 0.75, 0.1
 FAR = 12
 WIN, STAY = 200, 1500
 TURN, LEAN = 8, 1500.0
 LEAN0 = 900.0
 HEAT = 200.0
 RAND = 0.3
-COOL = 90.0
+COOL = 150.0
 SLACK = 60.0
 SIM = 64
 NCH = 4
@@ -43,11 +45,11 @@ for _d, _l in (
         ("bfloat16", (("X", 2 * VP), ("XO", V), ("VV", 4112), ("XC", 4096), ("MM", 4096), ("ED", 4096), ("BB", 32), ("nB", 5 * 128), ("L2", 128),
                       ("IL", 160), ("K16", 256), ("nIb", 128), ("PENI", 128), ("nPEN", 128), ("CI", 128), ("Bx", 128), ("NST", 768), ("NS8", 256), ("KN", 128),
                       ("KI", 256), ("KH", 256), ("CC", 1024), ("xs", 512), ("EQ", 7 * 256), ("eq", 512), ("OH", 512), ("DM", 768), ("UM", 768),
-                      ("G0", 256), ("G1", 512), ("OA", 256), ("NU", 256), ("en", 128), ("sb", 256), ("xm", 512), ("GU", 512), ("PQ", 144), ("de", 128),
+                      ("G0", 256), ("G1", 512), ("OA", 256), ("NU", 256), ("en", 128), ("sb", 256), ("xm", 512), ("GU", 512), ("PQ", 512), ("IS", 256), ("de", 128),
                       ("TRI", 64), ("mid", 1024), ("rmid", 1024), ("ones", 128), ("wn", 32), ("Me", 256),
                       ("R1", 320))),
         ("float16", (("Ih", 128), ("nIh", 128), ("I2", 256), ("B2", 16), ("CU", V), ("CQ", V), ("RT", 512), ("Wn", 272), ("RC", 160), ("DA", 512), ("DL", 1168),
-                     ("TL", 1168), ("Wf", 256), ("Wb", 256), ("Cc", 256), ("Y", 256), ("YS", 512), ("DK", 512), ("UK", 512), ("XV", 256),
+                     ("TL", 1168), ("Wf", 256), ("Cc", 256), ("Y", 256), ("YS", 512), ("DK", 512), ("UK", 512), ("XV", 256),
                      ("es", 128), ("NV", 32), ("YE", 512), ("YA", 512))),
         ("float32", (("RST", 256), ("RF", 256), ("RB", 256), ("col", 32), ("abf", 32), ("XF", 2 * VP), ("DF", 1280), ("CP", V), ("cth", 512),
                      ("I32", 128), ("pm", 512), ("pd", 272), ("pe", 512), ("sm", 1024), ("xc", 256), ("ra", 160), ("RS5", 160),
@@ -141,7 +143,7 @@ def mk(T, x):
     return t[p, f(x[2:5])]
 
 
-OPS, SEEN = [], {}
+OPS, SEEN, STOP, LAST, LATE, POST = [], {}, set(), [], [], []
 CY = 0.97
 PEC = 0.57
 GA, SCA, VF, SF, PF, SL, RI, RL = 1.65, 4.2, 33.0, 54.0, 43.0, 120.0, 900.0, 2300.0
@@ -154,6 +156,7 @@ def op(eng, emit, rd, wr, cost, tok=None, lat=0.0, track=True, after=(), acc=Fal
     k = (eng, ("D",) + tuple(sorted(set(q[0] for q in r))) if w and w[0][0][:2] == "D#" else w[0][:1 if w[0][0] in ("X", "XF", "mid", "eff", "rl", "rmid") else 2] if w else ())
     SEEN[k] = SEEN.get(k, 0) + 1
     o["kind"] = k + (SEEN[k],)
+    o["sort"] = 0 if tok or not w else 3 if w[0][2] - w[0][1] == NUL else 2 if any(isop(x) and x[0] == "i" for x in rd) else 1
     OPS.append(o)
     return o
 
@@ -238,12 +241,19 @@ def scatter(win, off, src):
 
 
 def pe(ml, acc=False):
+    n = len(OPS)
+
     def e(g, T, c):
-        for m in ml:
-            r = g.tensor.matmul(mk(T, m[0]), mk(T, m[1]), mk(T, m[2]), m[3], m[4])
+        for i, m in enumerate(ml):
+            end = (n, m[0][1]) in STOP and all(x[0][1] != m[0][1] for x in ml[i + 1:])
+            r = g.tensor.matmul(mk(T, m[0]), mk(T, m[1]), mk(T, m[2]), m[3], m[4] or end)
         return r
     co = PF + sum(max(min(64, cnt(m[1])), cnt(m[2])) * (4 if dty(m[1]) == "float32" else 1) * PEC for m in ml)
     return op("P", e, [x for m in ml for x in m[1:3]], [m[0] for m in ml], co, acc=acc)
+
+
+def close(bank):
+    op("P", None, [], [a(bank, 0, 16)], 0.0)["close"] = bank
 
 
 def group(out, terms):
@@ -296,7 +306,7 @@ B32, Bm16, B16, Bm8 = [a("BB", 8 * i, 8 * i + 8) for i in range(4)]
 (KC, AC, AD, PP, P8, MK) = range(6)
 (BND, BND2, TH16, TH2, NQ, NJ, E1, FL, S_, QQ, W0, W1, W2, W3, X0, X1, X2, X3, KZ, KO, KX, Z1, T1_, T2_, US, RED, FH, NW, PN, VB, VT, U1, U2, U3, C2, TH) = range(36)
 TINY = 2.0 ** -23
-(CK, POS, PI, NEG, H1, H2, ED_, PF_, NP_, NP2, WEF, WFH) = range(12)
+(CK, POS, PI, NEG, H1, H2, ED_, PF_, NP_, NP2, WEF, WFH, WR) = range(13)
 NL, PC, PTH, KK = a("en", 7, 128, 8), sm(C2), sm(TH), ("KA", "KB")
 OWN, PAR, PAR0 = a("XF", 0, V), a("XF", VP, VP + V), a("X", VP, VP + V)
 OWND, PARD = a("XF", 0, NUL), a("XF", VP, VP + NUL)
@@ -384,6 +394,8 @@ def consts():
     act(a("NS8"), a("NS8"), F.Sign)
     act(a("nPEN"), I_, F.Identity, 0.0, -PEN)
     act(a("CI"), I_, F.Identity, 0.0, float(CEN))
+    for z, v in enumerate((ST * 32 / OFF, float(-V))):
+        lin(blk("IS", z, 128), I_, v)
     act(a("RST"), a("K16"), F.Relu, 16 * BIG, -16 * BIG)
     for i in range(3):
         act(blk("NST", i), a("K16"), F.Sign)
@@ -419,15 +431,16 @@ def paths(r):
         bk = dbank()
         for h in range(2):
             o, x = t3("Wz", (8 * h, 8 * h + 8), (16 * h, 16 * h + 16)), blk("Wn", h, 128)
-            either(cp(o, x), gcp(o, x)) if r else cp(o, x)
+            POST.append(gcp(o, x) if r else cp(o, x))
         pe([(t3(bk, (8 * z, 8 * z + 8)), t3("Wz", (8 * h, 8 * h + 8), (z, 32, 2)), a("Ih"), h == 0, h == 1) for z in range(2) for h in range(2)])
         ts(a("WO"), t3(bk, (0, 16)), float(CEN), A.add)
     for nm, z, n in (("WXo", 1, 6), ("WXe", 0, 7)):
         act(t3(nm, None, (0, n)), t3("PW", (0, 16), (z, z + 2 * n, 2)), F.Copy)
         for m in (n, 2 * n):
             o, x = t3(nm, None, (m, 2 * m)), t3(nm, None, (0, m))
-            either(act(o, x, F.Copy), gcp(o, x) if r else cp(o, x))
-    cands(0, "CA", "el", (0, 2))
+            either(act(o, x, F.Copy), cp(o, x))
+    if r:
+        cands(0, "CA", "el", (0, 2))
 
 
 def fit(h, hs):
@@ -441,7 +454,9 @@ def fit(h, hs):
 
 def hop(h, H, win, nv):
     for j in range(4 * H, 4 * H + 4):
-        gather(blk("XC", j, 512), ind(win, blk("CO", 8 * h + j, 32)))
+        o = gather(blk("XC", j, 512), ind(win, blk("CO", 8 * h + j, 32)))
+        if (h, H) == (0, 1):
+            LATE.append(o)
     xs, xc = blk("xs", 2 * h + H, 128), lambda i, st=16: a("XC", 2048 * H + i, 2048 * H + 2048, st)
     mm, key = lambda c, j=0, st=1: a("MM", 2048 * H + 512 * c + j, 2048 * H + 512 * c + 512, st), lambda i: a(KK[H], i, 128, 16)
     four = lambda bk, w, first: [(t3(bk, None, (j, 16, 4)), w, xs, first and j == 0, j == 3) for j in range(4)]
@@ -457,7 +472,7 @@ def hop(h, H, win, nv):
             pe([(t3(bk), I_, xc(c, 4), True, False)] + four(bk, a("nIb"), False))
             act(mm(c), t3(bk), F.Abs, 0.0, 0.5)
         pe([(key(c + 4 * j), mm(c, j, 4), B32, False, False) for j in range(4)], True)
-    pe([(a(KK[H], 0, 16), I_, ZERO, False, True)])
+    close(KK[H])
     key, pm, eq, ne, y = a(KK[H], 0, 128), blk("pm", 2 * h + H, 128), blk("eq", H, 128), blk("eq", 2 + H, 128), blk("Y", H, 128)
     scan(pm, a("RST", 0, 128), key, 0.0, A.add, A.min)
     tt(eq, key, pm, A.is_equal)
@@ -472,12 +487,18 @@ def row(h, k, nm="VV", n=2048):
 
 def rows(r):
     for j in range(8):
-        gather(blk("VV", j, 512), ind(OWNN if j < 4 else PARN if r else PARN0, blk("WO", j, 32)))
+        o = gather(blk("VV", j, 512), ind(OWNN if j < 4 else PARN if r else PARN0, blk("WO", j, 32)))
+        for x in LATE[-4:]:
+            x["after"].append(o)
     if r > 0:
         pe([(a("PE", 0, 256), I_, a("K16"), True, False)]
            + [(a("PE", 128 * h + k, 128 * h + 128, 16), row(h, k), Bm16, False, False) for h in range(2) for k in range(0, 16, 2)])
         pe([(a("PE", 128 * h + k, 128 * h + 128, 16), row(h, k), Bm8, False, h == 1 and k == 15) for h in range(2) for k in range(1, 16, 2)])
         scan(a("pd", 8, 264), a("RST"), a("PE", 0, 256), 0.0, A.add, A.min)
+
+
+def sa(d):
+    return [(a("Ih"), a("Wn", d, d + 256)), (blk("I2", 0, 128), t3("TA", None, (d + 2, d + 18))), (blk("I2", 1, 128), t3("TA", None, (d, d + 16)))]
 
 
 def cut():
@@ -486,7 +507,8 @@ def cut():
     act(a("RB", 0, 256, 2), a("pd", 5, 261, 2), F.Relu, 4 * OFF, 4.0)
     act(a("RB", 2, 256, 16), a("K16", 0, 16), F.Identity, BIG, 0.0)
     act(sb(PF_), a("pd", 10, 264, 16), F.Relu, -4 * OFF, -4.0)
-    act(a("PQ", 0, 129), a("pd", 8, 266, 2), F.Identity, -OFF / 32, -1.0 / 32)
+    for z in range(2):
+        act(a("PQ", z, 256, 2), a("pd", 8 + 2 * z, 264 + 2 * z, 2), F.Relu, -OFF / 32, -1.0 / 32)
     act(sm(NQ), NL, F.Identity, -0.5 - 2 * OFF, 0.5)
     act(sm(NJ), NL, F.Identity, -2 * OFF)
     tt(sm(QQ), jj, sm(NQ), A.subtract)
@@ -513,20 +535,12 @@ def cut():
     tt(a("DM", 0, 256, 16), sm(FH), a("DM", 256, 512, 16), A.subtract)
     act(a("DM", 512, 768, 16), sm(FL), F.Identity, -55296.0, 8192.0)
     scan(a("UM"), a("NST"), a("DM"), 0.0, A.mult, A.add)
-    sa = lambda d: [(a("Ih"), a("Wn", d, d + 256)), (blk("I2", 0, 128), t3("TA", None, (d + 2, d + 18))), (blk("I2", 1, 128), t3("TA", None, (d, d + 16)))]
     tt(t3("TA", None, (0, 16)), WP, blk("UM", 0), A.mult)
     group(WB, sa(0))
     tt(t3("TB", None, (0, 16)), WB, blk("UM", 1), A.mult)
-    group(WB, sa(2) + [(a("Ih"), t3("TB", None, (6, 22))), (a("nIh"), t3("TB", None, (2, 18)))])
-    tt(a("Wb"), WB, blk("UM", 2), A.max)
-    for z in range(2):
-        tt(a("Wf", z, 256, 2), t3("PW", (0, 16), (z, 16, 2)), a("PQ", z, z + 128), A.max)
-    ec = a("es", 7, 128, 8)
-    ts(sm(NW), ec, float(V - ST - CEN), A.is_ge, float(-V), A.mult)
-    tt(sm(NW), sm(NW), ec, A.add)
-    act(sm(PN), sb(POS), F.Identity, ST + 4096.0, 4096.0)
-    tt(sm(NW), sm(NW), sm(PN), A.add)
-    tt(a("Wf", 0, 256, 16), a("Wf", 0, 256, 16), sm(NW), A.min)
+    either(ts(blk("PQ", 1), blk("UM", 2), 0.0, A.max), act(blk("PQ", 1), blk("UM", 2), F.Relu))
+    tt(sm(NW), a("Wn", 0, 256, 16), a("PQ", 0, 256, 16), A.add)
+    ts(sb(WR), sm(NW), OFF / 32 + V - ST - CEN, A.is_ge)
 
 
 def edges(r, t):
@@ -548,16 +562,17 @@ def edges(r, t):
         for z in range(2):
             pe([(key(h, k)[:5] + ((0, 32 * nc),), row(h, k + z, "VV", 512 * nc), Bm16, False, False) for h, k in hk], True)
         for c in range(4):
+            odd = blk("VV", 4 + c, 512, -t, 512)
             if c >= nc:
-                bk = dbank()
-                pe([(t3(bk), I_, blk("VV", 4 + c, 512), True, False), (t3(bk), a("nIb"), blk("VV", c, 512, t, 512), False, True)])
+                bk = dbank() if (c, t) != (3, 1) else "PT"
+                pe([(t3(bk), a("nIb"), blk("VV", c, 512), True, False)])
+                pe([(t3(bk), I_, odd, False, True)])
                 act(blk("ED", 4 * t + c, 512), t3(bk), F.Abs, 0.0, 0.5)
-            elif t == 0:
-                bk = dbank()
-                pe([(t3(bk), I_, blk("VV", 4 + c, 512), True, True)])
-                for u in range(2):
-                    tt(blk("ED", 4 * u + c, 512), blk("VV", c, 512, u, 512), t3(bk), A.max)
-        pe([(key(h, k), row(h, k, "ED"), B32, False, False) for h, k in hk], True)
+            else:
+                if t == 0:
+                    pe([(t3(KK[c]), I_, blk("VV", c, 512), True, True)])
+                tt(blk("ED", 4 * t + c, 512), odd, t3(KK[c]), A.max)
+        pe([(key(h, k), row(h, k + 2 * t, "ED"), B32, False, False) for h, k in hk], True)
 
 
 def pick(z, c):
@@ -565,7 +580,7 @@ def pick(z, c):
 
 
 def ends(r):
-    pe([(a("PE", 0, 16), I_, ZERO, False, True)])
+    close("PE")
     if r == 0:
         scan(a("pe", 0, 256), a("RST"), a("PE", 0, 256), 0.0, A.add, A.min)
         ks, nv = a("pe", 15, 256, 16), 1
@@ -623,8 +638,9 @@ def equal():
             part = [t3(bk, (0, bs[0] + 1)), t3(bk, (bs[0] + 1, bs[0] + bs[1] + 2))]
             tri = t3(bk, (bs[0], bs[0] + bs[1] + 2, bs[1] + 1))
         else:
-            part = [t3(q, j, (128 - n, 128)) for j, n in enumerate(ns)]
-            tri = t3(q, None, (112, 128))
+            w = SCR[q][1][2]
+            part = [t3(q, j, (w - n, w)) for j, n in enumerate(ns)]
+            tri = t3(q, (0, len(bs)), (w - 16, w))
         pe([(part[j], t3("LL", b % 8), blk("RT", 1 + b // 8, 128, 0, ns[j]), j == 0, False) for j, b in enumerate(bs)]
            + [(tri, I_, a("TRI", 0, cnt(tri)), False, True)])
         if q == "D":
@@ -635,7 +651,7 @@ def equal():
                 scan(a("ED", 128 * b + 128 - n // 2, 128 * b + 128), a("MM", c1, c1 + n // 2), a("MM", c1 + n // 2, c1 + n), BIG, A.min, A.min)
                 c1 += n
             else:
-                red(a("ED", 128 * b + 127, 128 * b + 128), part[j], A.min)
+                red(a("ED", 128 * b + 127, 128 * b + 128), part[j], A.min)["after"] += LAST
 
 
 def program():
@@ -653,8 +669,9 @@ def program():
         load("Y", blk("CA", i, CW), (lambda i: lambda T: T.cand[:, CW * i:CW * i + CW])(i), "lk%d" % i, 3000 + 1500 * i)["after"].append(left)
     op(None, None, [], [PAR0], 0, tok=("xarr", None), lat=8000, after=ss)
     for i in range(NCH):
-        ts(blk("CU", i, CW), blk("CA", i, CW), float(-CEN), A.add)
-        sc = op("G", (lambda i: lambda g, T, c: c["big"]("C", i))(i), [blk("CU", i, CW), PAR0], [], RI, track=False, after=ss)
+        for j in (2 * i, 2 * i + 1):
+            ts(blk("CU", j, CW // 2), blk("CA", j, CW // 2), float(-CEN), A.add)
+        sc = op("G", (lambda i: lambda g, T, c: c["big"]("C", i))(i), [blk("CU", i, CW), PAR0], [], RI, track=False, after=ss + ([sc] if i else []))
         op(None, None, [], [blk("CQ", i, CW)], 0, tok=("ca%d" % i, None), lat=13000 + 1000 * i, after=[sc])
     for i in range(2 * NCH):
         lin(blk("XF", i, CW // 2), blk("X", i, CW // 2), 1.0, LIFT)
@@ -682,6 +699,7 @@ def program():
     rows(0)
     edges(0, 0)
     edges(0, 1)
+    cands(0, "CA", "el", (0, 2))
     ends(0)
     for r in range(RO):
         last = r == RO - 1
@@ -717,6 +735,8 @@ def program():
         def e(g, T, c, r=r, ea=ea, eb=eb, ra=ra, rk=rk):
             c["two"](mk(T, ra), mk(T, ea), "aa%d" % r, mk(T, rk), mk(T, eb), "ak%d" % r)
         s = op("G", e, [ea, eb], [], RI, track=False)
+        for x in POST[-2:] if 0 < r < RO - 1 else ():
+            x["after"].append(s)
         op(None, None, [], [ra], 0, tok=("aa%d" % r, None), lat=RL, after=[s])
         op(None, None, [], [rk], 0, tok=("ak%d" % r, None), lat=RL, after=[s])
         if not last:
@@ -792,8 +812,11 @@ def program():
             pe([(pick(z, c), a(w), x, False, False) for z in range(2) for c, w, x in
                 ((0, "PENI", ng), (1, "nPEN", ng), (2, "PENI", ng), (0, "PENI", sb(WFH)), (2, "PENI", sb(WFH)), (3, "nPEN", sb(WFH)))])
             pe([(pick(0, 3), a("Ih"), a("YS", 271, 512, 16), False, True)])
-            pe([(WP, a("Ih"), a("Wf"), True, False), (WB, a("Ih"), a("Wb"), False, False), (t3("PW", (0, 16), 15), a("nPEN"), a("G1", 15, 256, 16), False, False)]
-               + [(t3("PW", (16 + 8 * h, 24 + 8 * h)), a("PENI"), a("ones"), False, False) for h in range(2)])
+            w0, q0 = t3("PW", (0, 16), 0), a("PQ", 0, 256, 16)
+            pe([(WB, w, x, i == 0, False) for i, (w, x) in enumerate(sa(2) + [(a("Ih"), t3("TB", None, (6, 22))), (a("nIh"), t3("TB", None, (2, 18)))])])
+            pe([m + (False, False) for m in [(WP, a("Ih"), WN), (WP, I_, blk("PQ", 0)), (w0, a("nIb"), q0), (w0, blk("IS", 0, 128), q0), (w0, blk("IS", 1, 128), sb(WR)),
+                                             (t3("PW", (0, 16), 15), a("nPEN"), a("G1", 15, 256, 16)), (WB, a("PENI"), blk("PQ", 1))]
+                + [(t3("PW", (16 + 8 * h, 24 + 8 * h)), a("PENI"), a("ones")) for h in range(2)]])
             scan(rev("GU", 0, 256), rev("G0", 0, 256), rev("G1", 0, 256), 0.0, A.mult, A.add)
             pe([(WP, a("PENI"), blk("GU", 0), False, False), (WB, a("nPEN"), blk("GU", 0), False, True)])
         scan(rev("GU", 256, 512), rev("G0", 0, 256), rev("G1", 256, 512), 0.0, A.mult, A.add)
@@ -804,7 +827,7 @@ def program():
             lin(a("NU"), a("OA"), -3968.0, float(NUL - CEN))
             tt(a("XV"), t3(vb, (0, 16)), a("NU"), A.max)
             tt(a("Wf"), WP, a("XV"), A.min)
-            tt(WN, WB, a("Wf"), A.min)
+            LAST[:] = [tt(WN, WB, a("Wf"), A.min)]
             pe([(WP, a("Ih"), WN, True, True)])
     act(sm(U1), ng, F.Identity, 2.0, -2.0)
     tt(a("wn", 16, 32), sm(U1), NL, A.add)
@@ -820,7 +843,21 @@ def program():
 def polish(sch, dl, ways, lat, head, rs, moves):
     N = len(dl)
     way = list(sch[5])
-    eng, cost = [ways[n][way[n]][0] for n in range(N)], [ways[n][way[n]][1] for n in range(N)]
+    lo, hi = [[KIND[o["sort"]][i] for o in OPS] for i in range(2)]
+    eng, cost, cos2 = [ways[n][way[n]][0] for n in range(N)], [ways[n][way[n]][1] * lo[n] for n in range(N)], [ways[n][way[n]][1] * hi[n] for n in range(N)]
+    cos2 = [c if e else SLOW * x for e, c, x in zip(eng, cos2, lat)]
+    en2, tai2 = [0.0] * N, [0.0] * N
+
+    def span(l):
+        return max(end[n] - cost[n] + tail[n] for n in l) + DEAR * max(en2[n] - cos2[n] + tai2[n] for n in l)
+
+    def tight(l):
+        out = []
+        for e, c, t in ((end, cost, tail), (en2, cos2, tai2)):
+            x = [e[n] - c[n] + t[n] for n in l]
+            top = max(x)
+            out += [top, [n for n, y in zip(l, x) if y > top - SLACK and eng[n]]]
+        return out[0] + DEAR * out[2], (out[1], out[3])
     sl = [[] for n in range(N)]
     for n in range(N):
         for d, w in dl[n]:
@@ -847,26 +884,34 @@ def polish(sch, dl, ways, lat, head, rs, moves):
     def ahead(p0, p1):
         for n in order[p0:p1]:
             m = mp[n]
-            t = end[m] if m >= 0 else 0.0
+            t, u = (end[m], en2[m]) if m >= 0 else (0.0, 0.0)
             for d, w in dl[n]:
                 if end[d] + w > t:
                     t = end[d] + w
+                if en2[d] + w > u:
+                    u = en2[d] + w
             for d, w in bp[n]:
                 if end[d] + w > t:
                     t = end[d] + w
-            end[n] = t + cost[n]
+                if en2[d] + w > u:
+                    u = en2[d] + w
+            end[n], en2[n] = t + cost[n], u + cos2[n]
 
     def behind(p1, p0=0):
         for n in reversed(order[p0:p1 + 1]):
             m = mn[n]
             t = tail[m] if m >= 0 and tail[m] > lat[n] else lat[n]
+            u = tai2[m] if m >= 0 and tai2[m] > lat[n] else lat[n]
             for d, w in sl[n]:
                 if tail[d] + w > t:
                     t = tail[d] + w
+                if tai2[d] + w > u:
+                    u = tai2[d] + w
             m = bn[n]
-            if m >= 0 and tail[m] + (0.0 if eng[n] == "P" else SL) > t:
-                t = tail[m] + (0.0 if eng[n] == "P" else SL)
-            tail[n] = t + cost[n]
+            if m >= 0:
+                w = 0.0 if eng[n] == "P" else SL
+                t, u = max(t, tail[m] + w), max(u, tai2[m] + w)
+            tail[n], tai2[n] = t + cost[n], u + cos2[n]
 
     def unlink(n):
         if mp[n] >= 0:
@@ -900,25 +945,26 @@ def polish(sch, dl, ways, lat, head, rs, moves):
 
     ahead(0, N)
     behind(N - 1)
-    cur = max(end[n] + lat[n] for n in range(N))
+    cur = span(order)
     keep = (cur, list(order), list(way), [list(h) for h in banks], list(end), list(cost))
     wb = N
     for it in range(moves + 1):
         if it % STAY == 0 or it == moves:
             ahead(0, N)
             behind(N - 1)
-            cur = max(end[n] + lat[n] for n in range(N))
+            cur = span(order)
             if cur < keep[0]:
                 keep = (cur, list(order), list(way), [list(h) for h in banks], list(end), list(cost))
             if it == moves:
                 break
             wa = max(0, wb - WIN // 2) if wb < N else 0
             wb = min(N, wa + WIN)
-            crit = [n for n in order[wa:wb] if end[n] - cost[n] + tail[n] > cur - SLACK and eng[n]]
-        if not crit:
+            cur, crit = tight(order[wa:wb])
+        if not crit[it & 1]:
             continue
-        v = crit[int(rs.randint(len(crit)))]
-        beg, x, undo = end[v] - cost[v], rs.rand(), None
+        v = crit[it & 1][int(rs.randint(len(crit[it & 1])))]
+        fin = (end, en2)[it & 1]
+        beg, x, undo = fin[v] - (cost, cos2)[it & 1][v], rs.rand(), None
         p0 = p1 = pos[v]
         if len(ways[v]) > 1 and x < 0.35:
             e, c = ways[v][1 - way[v]]
@@ -927,12 +973,12 @@ def polish(sch, dl, ways, lat, head, rs, moves):
                 i -= 1
             if i < 0:
                 continue
-            old = (mp[v], mn[v], eng[v], cost[v])
+            old = (mp[v], mn[v], eng[v], cost[v], cos2[v])
             unlink(v)
             insert(v, order[i], mn[order[i]])
-            eng[v], cost[v], way[v] = e, c, 1 - way[v]
+            eng[v], cost[v], cos2[v], way[v] = e, c * lo[v], c * hi[v], 1 - way[v]
             undo = 0
-        elif bp[v] and max(end[d] + w for d, w in bp[v]) >= beg - 1.0 and x < 0.8:
+        elif bp[v] and max(fin[d] + w for d, w in bp[v]) >= beg - 1.0 and x < 0.8:
             b = [b for b in range(3) if v in banks[b]][0]
             old = [list(h) for h in banks]
             seg = None
@@ -970,7 +1016,7 @@ def polish(sch, dl, ways, lat, head, rs, moves):
                 insert(u, v, mn[v])
             else:
                 u = mp[v]
-                if u < 0 or end[u] < beg - 1.0:
+                if u < 0 or fin[u] < beg - 1.0:
                     continue
                 for k in range(int(FAR * rs.rand() ** 2)):
                     u = mp[u] if mp[u] >= 0 else u
@@ -984,26 +1030,24 @@ def polish(sch, dl, ways, lat, head, rs, moves):
                 continue
             undo = 2
         p2 = min(N, p1 + 60)
-        was = [end[n] for n in order[p0:p2]], order[p0:p2]
+        was = [end[n] for n in order[p0:p2]], [en2[n] for n in order[p0:p2]], order[p0:p2]
         ahead(p0, p2)
         lim = cur + COOL * (1.0 - it / moves) * -np.log(1.0 - rs.rand())
-        ok = max(end[n] - cost[n] + tail[n] for n in order[p1 + (p1 + 1 < p2):p2]) <= lim
+        ok = span(order[p1 + (p1 + 1 < p2):p2]) <= lim
         p3 = max(p2, wb)
         if ok and p3 > p2:
             ahead(p2, p3)
-            ok = max(end[n] - cost[n] + tail[n] for n in order[p2:p3]) <= lim
+            ok = span(order[p2:p3]) <= lim
             if not ok:
                 was = None
         if ok:
             behind(p3 - 1 if undo == 1 else p1, min(p0, wa))
-            len_ = [end[n] - cost[n] + tail[n] for n in order[wa:wb]]
-            cur = max(len_)
-            crit = [n for n, x in zip(order[wa:wb], len_) if x > cur - SLACK and eng[n]]
+            cur, crit = tight(order[wa:wb])
             continue
         if undo == 0:
             unlink(v)
             insert(v, old[0], old[1])
-            eng[v], cost[v], way[v] = old[2], old[3], 1 - way[v]
+            eng[v], cost[v], cos2[v], way[v] = old[2], old[3], old[4], 1 - way[v]
         else:
             if undo == 1:
                 banks[:] = old
@@ -1016,8 +1060,8 @@ def polish(sch, dl, ways, lat, head, rs, moves):
                 for k, m in enumerate(seg):
                     pos[m] = p0 + k
         if was:
-            for t, n in zip(*was):
-                end[n] = t
+            for t, u, n in zip(*was):
+                end[n], en2[n] = t, u
         else:
             ahead(p0, p3)
     cur, order, way, banks, end, cost = keep
@@ -1207,8 +1251,9 @@ def plan():
             cur, pr, bias = t2, p2, b2
             if t2[0] < best[0]:
                 best = t2
-    for moves in (FIRST, MOVES):
-        best = polish(best, [[x for x in dl[n] if x[0] not in OPS[n]["early"]] for n in range(N)], ways, lat, head, rs, moves)
+    plain = [[x for x in dl[n] if x[0] not in OPS[n]["early"]] for n in range(N)]
+    best = min((polish(best, plain, ways, lat, head, rs, FIRST) for it in range(STARTS)), key=lambda x: x[0])
+    best = polish(best, plain, ways, lat, head, rs, MOVES)
     for o in OPS:
         o["t"] = best[2][o["n"]]
         o["deps"] -= o["early"]
@@ -1241,10 +1286,14 @@ def plan():
     total = {}
     for e in order:
         total[e] = 0
-        for n in order[e]:
+        for i, n in enumerate(order[e]):
+            real = [m for m in order[e][:i + 1] if OPS[m]["emit"]][-1] if "close" in OPS[n] else n
+            if real != n:
+                STOP.add(([m for m in order[e][:i] if any(q[0] == OPS[n]["close"] for q in OPS[m]["w"])][-1], OPS[n]["close"]))
             if n in need:
                 total[e] += 1
                 OPS[n]["inc"] = total[e]
+                OPS[real]["add"] = OPS[real].get("add", 0) + 1
     return order, total, best[0]
 
 
@@ -1263,7 +1312,7 @@ def routes(topo, cores):
         x = [x for x in range(SIM) if x not in used and ok(x)][0]
         used.add(x)
         return x
-    turn = {}
+    turn, spare = {}, {}
     for r in range(n):
         s, d = cores[r], cores[(r - SH) % n]
         if topo.chip(s) == topo.chip(d):
@@ -1280,14 +1329,22 @@ def routes(topo, cores):
         w3 = [s, o, take(lambda x: mate(x) and topo.die(x) == topo.die(o)), d]
         w1 = [s, take(lambda x: here(x) and not topo.may_write(x, probe)), d]
         turn[topo.chip(s)] = 1 - turn.get(topo.chip(s), 0)
-        ways.append({"X": [w3, w1, w1 if turn[topo.chip(s)] else [s, d], [s, d]], "C": [w3, w1, w3, w1]})
+        t = turn[topo.chip(s)]
+        ways.append({"X": [w3, w1, w1 if t else [s, d], [s, d]], "C": [w3, w1, w3, w1]})
+        if not t:
+            spare[topo.chip(s)] = (w3[1:-1], w1[1:-1])
+    for w in ways:
+        s, d = w["C"][0][0], w["C"][0][-1]
+        if w["C"][0] == w["C"][1] and topo.chip(s) != topo.chip(d):
+            w["C"] = w["C"][:2] + [[s] + x + [d] for x in spare[topo.chip(s)]]
+            w["slot"] = {("C", 2): 1, ("C", 3): 0}
     return ways
 
 
-def step(topo, w, j):
+def step(topo, w, j, far=None):
     es = topo.engines(w[j], w[j + 1])
-    if j + 2 < len(w) and topo.chip(w[j]) == topo.chip(w[j + 1]):
-        es = [x for x in es if x not in topo.engines(w[j], w[-1])]
+    if (j + 2 < len(w) or far is not None) and topo.chip(w[j]) == topo.chip(w[j + 1]):
+        es = [x for x in es if x not in topo.engines(w[j], w[-1] if far is None else far)]
     return es
 
 
@@ -1296,12 +1353,14 @@ def rank_program(g, core, T, topo):
     n = len(cores)
     rank = T.rank_of(core)
     ways = routes(topo, cores)
+    far = lambda w: [x for x in cores if topo.chip(x) != topo.chip(w[0])][0] if len(w) == 2 else None
 
-    def hand(what, i, w, j, ls):
-        cs = slice(CW * i, CW * i + CW)
-        src, es, d = (T.X if what == "X" else T.CU)[:, cs], step(topo, w, j), w[j + 1]
+    def hand(what, r, i, j, ls):
+        w, k, t = ways[r][what][i], ways[r].get("slot", {}).get((what, i), i), T.X if what == "X" else T.CU
+        cs, ks = slice(CW * i, CW * i + CW), slice(CW * k, CW * k + CW)
+        src, es, d = t[:, ks if j else cs], step(topo, w, j, far(w) if what == "C" else None), w[j + 1]
         if j + 2 < len(w):
-            dst, sem = src, T.sem[("hx%d" if what == "X" else "hc%d") % i]
+            dst, sem = t[:, ks], T.sem[("hx%d" if what == "X" else "hc%d") % k]
         else:
             dst, sem = (T.X[:, VP + CW * i:VP + CW * i + CW], T.sem.xarr) if what == "X" else (T.CQ[:, cs], T.sem["ca%d" % i])
         g.remote_dma(dst, src, sem, ls, topo.addr(d)[1], topo.addr(d)[0], bits(es))
@@ -1313,8 +1372,8 @@ def rank_program(g, core, T, topo):
                 for i, w in enumerate(ways[r][what]):
                     if core in w:
                         j = w.index(core)
-                        g.wait_ge(T.sem[("hx%d" if what == "X" else "hc%d") % i], len(step(topo, w, j - 1)))
-                        out += hand(what, i, w, j, T.sem.ls0)
+                        g.wait_ge(T.sem[("hx%d" if what == "X" else "hc%d") % ways[r].get("slot", {}).get((what, i), i)], len(step(topo, w, j - 1)))
+                        out += hand(what, r, i, j, T.sem.ls0)
         if out:
             g.wait_ge(T.sem.ls0, out)
         return
@@ -1326,7 +1385,7 @@ def rank_program(g, core, T, topo):
 
     def big(what, i):
         ls, num = (T.sem.ls0, sent) if what == "X" else (T.sem.ls1, out)
-        num[0] += hand(what, i, ways[rank][what][i], 0, ls)
+        num[0] += hand(what, rank, i, 0, ls)
 
     def one(dst, src, sem):
         g.remote_dma(dst, src, T.sem[sem], T.sem.ls1, topo.addr(p)[1], topo.addr(p)[0], bits(es))
@@ -1339,7 +1398,7 @@ def rank_program(g, core, T, topo):
     c = {"big": big, "one": one, "two": two}
     vals = {"xarr": sum(len(step(topo, w, len(w) - 2)) for w in ways[(rank + SH) % n]["X"])}
     for i, w in enumerate(ways[(rank + SH) % n]["C"]):
-        vals["ca%d" % i] = len(step(topo, w, len(w) - 2))
+        vals["ca%d" % i] = len(step(topo, w, len(w) - 2, far(w)))
     for r in range(RO):
         vals["am%d" % r], vals["aa%d" % r], vals["ak%d" % r] = len(es), h, len(es) - h
     qs = {"V": g.vector, "S": g.scalar, "P": g.tensor, "G": g, "Y": g.sync}
@@ -1355,9 +1414,9 @@ def rank_program(g, core, T, topo):
                     qs[e].wait_ge(T.sem[s], vals[s] if v is None else v)
             for d in o["cw"]:
                 qs[e].wait_ge(T.sem["s" + OPS[d]["eng"]], OPS[d]["inc"])
-            r = o["emit"](g, T, c)
-            if "inc" in o:
-                r.then_inc(T.sem["s" + e], 1)
+            r = o["emit"](g, T, c) if o["emit"] else None
+            if "add" in o:
+                r.then_inc(T.sem["s" + e], o["add"])
     for e in "VSPG":
         if TOTAL[e]:
             g.wait_ge(T.sem["s" + e], TOTAL[e])

import numpy as np
from concourse.bass import DstId, RemoteDMATransfer
from concourse.mybir import AluOpType as A, AxisListType, ActivationFunctionType as F

V, L, RO, SH, ST = 3328, 256, 4, 3, 61
NUL = V + L
VP = NUL + 16
CEN = V // 2
BIG = float(2 ** 20)
DEAD = 2048.0
LIFT = 4096.0
OFF = 128 * DEAD
THR = 135168.0
PEN = 262144.0
K0 = 8.0 - 1.0 / 32
M1 = 1.5 * 2 ** 23
M2 = 1.5 * 2 ** 24
M16 = 1.5 * 2 ** 27
HV = [[3, 3], [3, 3]]
HVL = [[2, 2], [3, 3]]
EA = ["22", "SS", "SS", "SS"]
VQ = (("D", (15, 14)), ("KA", (7, 6, 5, 4)), ("D", (13, 12)), ("D", (11, 10)), ("KB", (3, 2, 1, 0)), ("D", (9, 8)))
STEPS = "rc0A1kBbe"
XS = 4
OS = 6
SEED, TRIES = 8, 30
FIRST = 800000
MOVES = 250000
STARTS = 1
KIND, DEAR, SLOW = ((1.0, 1.0), (0.9, 1.24), (0.84, 1.3), (0.8, 1.4)), 0.75, 0.1
FAR = 12
WIN, STAY = 200, 1500
TURN, LEAN = 8, 1500.0
LEAN0 = 900.0
HEAT = 200.0
RAND = 0.3
COOL = 150.0
SLACK = 60.0
SIM = 64
NCH = 4
CW = V // NCH

SCRATCH = {}
for _d, _l in (
        ("bfloat16", (("X", 2 * VP), ("XO", V), ("VV", 4112), ("XC", 4096), ("MM", 4096), ("ED", 4096), ("BB", 32), ("nB", 5 * 128), ("L2", 128),
                      ("IL", 160), ("K16", 256), ("nIb", 128), ("PENI", 128), ("nPEN", 128), ("CI", 128), ("Bx", 128), ("NST", 768), ("NS8", 256), ("KN", 128),
                      ("KI", 256), ("KH", 256), ("CC", 1024), ("xs", 512), ("EQ", 7 * 256), ("eq", 512), ("OH", 512), ("DM", 768), ("UM", 768),
                      ("G0", 256), ("G1", 512), ("OA", 256), ("NU", 256), ("en", 128), ("sb", 256), ("xm", 512), ("GU", 512), ("PQ", 512), ("IS", 256), ("de", 128),
                      ("TRI", 64), ("mid", 1024), ("rmid", 1024), ("ones", 128), ("wn", 32), ("Me", 256),
                      ("R1", 320))),
        ("float16", (("Ih", 128), ("nIh", 128), ("I2", 256), ("B2", 16), ("CU", V), ("CQ", V), ("RT", 512), ("Wn", 272), ("RC", 160), ("DA", 512), ("DL", 1168),
                     ("TL", 1168), ("Wf", 256), ("Cc", 256), ("Y", 256), ("YS", 512), ("DK", 512), ("UK", 512), ("XV", 256),
                     ("es", 128), ("NV", 32), ("YE", 512), ("YA", 512))),
        ("float32", (("RST", 256), ("RF", 256), ("RB", 256), ("col", 32), ("abf", 32), ("XF", 2 * VP), ("DF", 1280), ("CP", V), ("cth", 512),
                     ("I32", 128), ("pm", 512), ("pd", 272), ("pe", 512), ("sm", 1024), ("xc", 256), ("ra", 160), ("RS5", 160),
                     ("ef", 32), ("yo", 256), ("yc", 256))),
        ("int32", (("CA", V), ("wi", 256), ("ci", 256), ("ti", 256), ("pi", 8))),
        ("uint16", (("WO", 256), ("CO", 512), ("el", 16), ("fl", 16), ("ab", 32), ("eff", 128), ("rl", 128)))):
    for _n, _c in _l:
        SCRATCH[_n] = ("sbuf", [128, _c], _d)
for _n, _s, _d in (("LL", [8, 128], "float16"), ("DV", [2, 160], "float16"), ("Wz", [16, 32], "float16"), ("TA", [16, 32], "float16"), ("TB", [16, 32], "float16"), ("WXo", [16, 24], "float32"), ("WXe", [16, 28], "float32")):
    SCRATCH[_n] = ("sbuf", [128] + _s, _d)
SCRATCH["PE"] = ("psum", [128, 512], "float32")
for _n in ("KA", "KB"):
    SCRATCH[_n] = ("psum", [128, 4, 128], "float32")
for _n in ("PT", "PW", "D0", "D1", "D2"):
    SCRATCH[_n] = ("psum", [128, 32, 16], "float32")

SEMAPHORES = (["sV", "sS", "sP", "sG", "ls0", "ls1", "xarr", "lw", "lc", "lt", "ox", "ow", "on"]
              + ["%s%d" % (s, i) for s in ("lx", "hx", "hc", "lk", "ca") for i in range(NCH)]
              + ["%s%d" % (s, r) for s in ("am", "aa", "ak") for r in range(RO)])
TWO = ("bfloat16", "float16", "uint16")
SCR, BANK = dict(SCRATCH), {}


def a(name, c0=0, c1=None, st=1, p=None):
    return ("a", name, c0, SCR[name][1][1] if c1 is None else c1, st, p)


def rev(name, c0, c1):
    return ("r", name, c0, c1)


def t3(name, r=None, c=None, p=None):
    s = SCR[name][1]
    f = lambda x, n: (0, n, 1) if x is None else x if isinstance(x, int) else (x[0], x[1], x[2] if len(x) > 2 else 1)
    return ("t", name, f(r, s[1]), f(c, s[2]), p)


def ind(w, o):
    return ("i", w, o)


def isop(x):
    return isinstance(x, tuple)


def rng(x):
    return [x] if isinstance(x, int) else range(*x)


def regs(x):
    if x[0] == "i":
        return regs(x[1]) + regs(x[2])
    if x[0] == "t":
        w, c = SCR[x[1]][1][2], rng(x[3])
        return [(x[1], w * i + min(c), w * i + max(c) + 1) for i in rng(x[2])]
    return [(x[1], x[2], x[3])]


def cnt(x):
    if x[0] == "i":
        return 16 * cnt(x[2])
    if x[0] == "t":
        return len(rng(x[2])) * len(rng(x[3]))
    if x[0] == "r":
        return x[3] - x[2]
    return len(range(x[2], x[3], x[4]))


def dty(x):
    return SCR[x[1][1] if x[0] == "i" else x[1]][2]


def ps(x):
    return x[0] != "i" and SCR[x[1]][0] == "psum"


def mk(T, x):
    if not isop(x):
        return x
    if x[0] == "i":
        return mk(T, x[1]).indirect(mk(T, x[2]))
    t = T[BANK.get(x[1], x[1])]
    if x[0] == "r":
        return t[:, x[3] - 1:(x[2] - 1 if x[2] else None):-1]
    p = slice(None) if x[-1] is None else slice(x[-1][0], x[-1][1])
    f = lambda y: y if isinstance(y, int) else slice(y[0], y[1]) if y[2] == 1 else slice(y[0], y[1] if y[1] >= 0 else None, y[2])
    if x[0] == "t":
        return t[p, f(x[2]), f(x[3])]
    if x[1] in ("KA", "KB"):
        return t[p, 0, f(x[2:5])]
    return t[p, f(x[2:5])]


OPS, SEEN, STOP, LAST, LATE, POST = [], {}, set(), [], [], []
CY = 0.97
PEC = 0.57
GA, SCA, VF, SF, PF, SL, RI, RL = 1.65, 4.2, 33.0, 54.0, 43.0, 120.0, 900.0, 2300.0


def op(eng, emit, rd, wr, cost, tok=None, lat=0.0, track=True, after=(), acc=False):
    r = [q for x in rd if isop(x) for q in regs(x)]
    w = [q for x in wr for q in regs(x)]
    o = {"eng": eng, "emit": emit, "r": r, "w": w, "cost": cost, "tok": tok, "lat": lat, "track": track, "after": list(after), "n": len(OPS), "acc": acc, "alt": None}
    k = (eng, ("D",) + tuple(sorted(set(q[0] for q in r))) if w and w[0][0][:2] == "D#" else w[0][:1 if w[0][0] in ("X", "XF", "mid", "eff", "rl", "rmid") else 2] if w else ())
    SEEN[k] = SEEN.get(k, 0) + 1
    o["kind"] = k + (SEEN[k],)
    o["sort"] = 0 if tok or not w else 3 if w[0][2] - w[0][1] == NUL else 2 if any(isop(x) and x[0] == "i" for x in rd) else 1
    OPS.append(o)
    return o


def _vc(out, ins, base):
    n = cnt(out)
    if out[0] == "i":
        return 50 + SCA * CY * n
    if ins[0][0] == "i":
        return 50 + GA * CY * n
    return VF + max(64, n * base) * CY


def _half(*xs):
    return 0.5 if all(dty(x) in TWO for x in xs) else 1.0


def cp(out, in_):
    return op("V", lambda g, T, c: g.vector.tensor_copy(mk(T, out), mk(T, in_)), [in_] + ([out[2]] if out[0] == "i" else []),
              [out[1] if out[0] == "i" else out], _vc(out, [in_], _half(out, in_)))


def ts(out, in_, s1, o1, s2=None, o2=None):
    if o2 is None:
        e = lambda g, T, c: g.vector.tensor_scalar(mk(T, out), mk(T, in_), mk(T, s1), None, o1)
    else:
        e = lambda g, T, c: g.vector.tensor_scalar(mk(T, out), mk(T, in_), mk(T, s1), mk(T, s2), o1, o2)
    return op("V", e, [in_, s1, s2], [out], _vc(out, [in_], _half(out, in_)))


def tt(out, x, y, o):
    b = 1.0 if (ps(x) or ps(y) or x[0] == "i") else 2.0
    return op("V", lambda g, T, c: g.vector.tensor_tensor(mk(T, out), mk(T, x), mk(T, y), o), [x, y] + ([out[2]] if out[0] == "i" else []),
              [out[1] if out[0] == "i" else out], _vc(out, [x], b))


def scan(out, d0, d1, init, o0, o1):
    return op("V", lambda g, T, c: g.vector.tensor_tensor_scan(mk(T, out), mk(T, d0), mk(T, d1), init, o0, o1), [d0, d1], [out],
              _vc(out, [d0], _half(out, d0, d1)))


def red(out, in_, o):
    return op("V", lambda g, T, c: g.vector.tensor_reduce(mk(T, out), mk(T, in_), AxisListType.X, o, apply_absolute_value=True), [in_], [out],
              VF + max(64, cnt(in_)) * CY)


def ms(out, v):
    return op("V", lambda g, T, c: g.vector.memset(mk(T, out), v), [], [out], VF + max(64, cnt(out) * _half(out)) * CY)


def act(out, in_, f, bias=0.0, scale=1.0, acc=None):
    n = cnt(in_)
    co = 65 + GA * CY * n if in_[0] == "i" else SF + max(64, n) * CY
    if acc is None:
        e = lambda g, T, c: g.scalar.activation(mk(T, out), mk(T, in_), f, mk(T, bias), mk(T, scale))
    else:
        e = lambda g, T, c: g.scalar.activation(mk(T, out), mk(T, in_), f, mk(T, bias), mk(T, scale), accum_out=mk(T, acc))
        co += 20
    return op("S", e, [in_, bias, scale], [out] + ([acc] if acc else []), co)


def either(v, s):
    x = OPS.pop()
    SEEN[x["kind"][:2]] -= 1
    v["alt"] = (x["eng"], x["emit"], x["cost"])
    return v


def lin(out, in_, scale, bias=0.0):
    return either(ts(out, in_, scale, A.mult, bias, A.add), act(out, in_, F.Identity, bias, scale))


def gather(out, src):
    if src[0] == "i" and src[1][1] == "XF":
        return either(ts(out, src, -LIFT, A.add), act(out, src, F.Identity, -LIFT))
    return either(cp(out, src), act(out, src, F.Copy))


def scatter(win, off, src):
    x = ind(win, off)
    return either(cp(x, src), op("S", lambda g, T, c: g.scalar.activation(mk(T, x), mk(T, src), F.Silu), [src, off], [win], 65 + SCA * CY * 256))


def pe(ml, acc=False):
    n = len(OPS)

    def e(g, T, c):
        for i, m in enumerate(ml):
            end = (n, m[0][1]) in STOP and all(x[0][1] != m[0][1] for x in ml[i + 1:])
            r = g.tensor.matmul(mk(T, m[0]), mk(T, m[1]), mk(T, m[2]), m[3], m[4] or end)
        return r
    co = PF + sum(max(min(64, cnt(m[1])), cnt(m[2])) * (4 if dty(m[1]) == "float32" else 1) * PEC for m in ml)
    return op("P", e, [x for m in ml for x in m[1:3]], [m[0] for m in ml], co, acc=acc)


def close(bank):
    op("P", None, [], [a(bank, 0, 16)], 0.0)["close"] = bank


def group(out, terms):
    pe([(out, w, x, i == 0, i == len(terms) - 1) for i, (w, x) in enumerate(terms)])


def iota(out, pat, base, cm):
    if dty(out) == "int32":
        e = lambda g, T, c: g.iota(mk(T, out), pat, base, cm)
    else:
        e = lambda g, T, c: g.iota(mk(T, out), pat, base, cm, allow_small_or_imprecise_dtypes=True)
    return op("G", e, [], [out], 130 + 2 * CY * cnt(out))


def gcp(out, in_):
    return op("G", lambda g, T, c: g.affine_select(mk(T, out), mk(T, in_), [[0, cnt(out)]], A.is_ge, 0.0, 0, 0), [in_], [out], 170 + 2 * CY * cnt(out))


def load(q, out, src, sem, lat):
    def e(g, T, c):
        (g.sync if q == "Y" else g.scalar).dma_start(mk(T, out), src(T)).then_inc(T.sem[sem], 16)
    return op(q, e, [], [out], 100, tok=(sem, 16), lat=lat)


def store(dst, src, reg, sem, lat):
    def e(g, T, c):
        g.sync.dma_start(dst(T), src(T)).then_inc(T.sem[sem], 16)
    return op("Y", e, [reg], [], 100, tok=(sem, 16), lat=lat)


def sm(i, n=16, o=0):
    return a("sm", 16 * i + o, 16 * i + o + n)


def col(i):
    return a("col", i, i + 1)


def blk(name, i, w=256, o=0, n=None):
    return a(name, w * i + o, w * i + o + (w if n is None else n))


def sb(i):
    return blk("sb", i, 16)


I_ = a("IL", 16, 144)
B1 = a("Bx", 0, 128, 16)
B32, Bm16, B16, Bm8 = [a("BB", 8 * i, 8 * i + 8) for i in range(4)]
(KC, AC, AD, PP, P8, MK) = range(6)
(BND, BND2, TH16, TH2, NQ, NJ, E1, FL, S_, QQ, W0, W1, W2, W3, X0, X1, X2, X3, KZ, KO, KX, Z1, T1_, T2_, US, RED, FH, NW, PN, VB, VT, U1, U2, U3, C2, TH) = range(36)
TINY = 2.0 ** -23
(CK, POS, PI, NEG, H1, H2, ED_, PF_, NP_, NP2, WEF, WFH, WR) = range(13)
NL, PC, PTH, KK = a("en", 7, 128, 8), sm(C2), sm(TH), ("KA", "KB")
OWN, PAR, PAR0 = a("XF", 0, V), a("XF", VP, VP + V), a("X", VP, VP + V)
OWND, PARD = a("XF", 0, NUL), a("XF", VP, VP + NUL)
OWNN, PARN, PARN0 = a("XF", 0, VP), a("XF", VP, 2 * VP), a("X", VP, 2 * VP)
WP, WB = t3("PW", (0, 16)), t3("PW", (16, 32))
WN = a("Wn", 0, 256)
ZERO, CNUL = a("CC", 0, 16), a("NV", 0, 16)


def dbank():
    n = "D#%d" % len(SCR)
    SCR[n] = SCR["D0"]
    return n


def slot():
    return t3(dbank(), 0)


def flip(bk, src, r0=0, hs=(0, 2)):
    pe([(t3(bk, (r0 + 8 * h, r0 + 8 * h + 8)), blk(src, h, 128), a("Ih"), True, True) for h in range(*hs)])


def tolist(c0, n):
    scan(a("TL", c0, c0 + n), a("DA", 0, n), a("DL", c0, c0 + n), 0.0, A.mult, A.add)
    bk = dbank()
    o = lambda j: t3(bk, j // 2, (j % 2 * 8, j % 2 * 8 + 8))
    pe([m for j in range(n // 128) for m in ((o(j), a("TL", c0 + 128 * j, c0 + 128 * j + 128), a("B2", 0, 8), True, False),
                                             (o(j), a("TL", c0 + 128 * j + 1, c0 + 128 * j + 129), a("B2", 8, 16), False, False),
                                             (o(j), a("DL", c0 + 128 * j + 1, c0 + 128 * j + 129), a("B2", 0, 8), False, True))])
    return bk


def consts():
    iota(a("pi", 0, 1), [[0, 1]], 0, 1)
    iota(a("IL"), [[1, 160]], -16, -1)
    iota(a("K16"), [[0, 16], [1, 16]], 0, 0)
    iota(a("L2"), [[1, 8], [0, 16]], 0, -1)
    iota(a("NS8"), [[0, 32], [1, 8]], 0, 0)
    iota(a("RS5"), [[0, 32], [1, 5]], 0, 0)
    iota(a("KN"), [[0, 16], [2, 8]], 1, 0)
    ts(a("L2"), a("L2"), 0.0, A.is_equal)
    ts(a("IL"), a("IL"), 0.0, A.is_equal)
    cp(col(PP), a("pi", 0, 1))
    for j, (c, m) in enumerate(((KC, 15), (P8, 7))):
        ts(a("pi", j + 1, j + 2), a("pi", 0, 1), m, A.bitwise_and)
        cp(col(c), a("pi", j + 1, j + 2))
    ts(a("col", MK, MK + 8), a("K16", 0, 8), col(P8), A.is_equal)
    ts(a("TRI"), a("K16", 0, 64), col(KC), A.is_ge, 32768.0, A.mult)
    act(sm(VT), a("K16", 0, 16), F.Identity, col(KC), 16.0)
    act(sm(VB), sm(VT), F.Identity, V * TINY, TINY)
    ms(t3("DV"), 0.0)
    for k in (0, 2, 4):
        ms(t3("DV", None, (16 * k + 8, 16 * k + 16)), -1.0)
    act(a("nIb"), I_, F.Identity, 0.0, -1.0)
    act(a("PENI"), I_, F.Identity, 0.0, PEN)
    cp(a("Ih"), I_)
    ts(a("nIh"), I_, -1.0, A.mult)
    ts(blk("I2", 0, 128), I_, 2.0, A.mult)
    ts(blk("I2", 1, 128), I_, -2.0, A.mult)
    act(a("I32"), I_, F.Copy)
    pe([(a("KA", 0, 128), a("L2", p=(0, 8)), a("L2", p=(0, 8)), True, True)])
    act(a("Bx"), a("KA", 0, 128), F.Copy)
    for x, v in ((B32, 32.0), (Bm16, -16.0), (B16, 16.0), (Bm8, -8.0)):
        act(x, B1, F.Identity, 0.0, v)
    cp(a("B2", 0, 8), B1)
    ts(a("B2", 8, 16), B1, -1.0, A.mult)
    for nv in sorted(set(x for y in HV + HVL for x in y) - {0}):
        lin(blk("nB", nv, 128), a("Bx"), -16.0)
        for c in range(nv, 4):
            ms(a("nB", 128 * nv + c, 128 * nv + 128, 4), 0.0)
    for z in range(2):
        ts(blk("DA", z), a("K16"), col(KC), A.is_le)
    ms(a("DA", 0, 512, 16), 0.0)
    act(a("CC", 0, 16), a("K16", 0, 16), F.Identity, 0.0, 0.0)
    for h in range(2):
        ts(a("NV", 16 + 8 * h, 24 + 8 * h), a("CC", 0, 8), col(PP), A.add, float(CEN + 128 * h), A.add)
    for x, v in ((a("Wn", 256, 272), 0.0), (t3("Wz"), 0.0), (a("DL"), 0.0), (a("TL", 0, 1168, 128), 0.0), (a("RC"), 0.0), (a("R1"), 1.0)):
        ms(x, v)
    for z in range(2):
        cp(a("RC", 80 * z + 4, 80 * z + 80, 5), a("NV", 16, 32))
    for c0 in (1, 4, 160, 164):
        ms(a("R1", c0, c0 // 160 * 160 + 160, 5), 0.0)
    act(a("RS5"), a("RS5"), F.Relu, 16 * BIG, -16 * BIG)
    act(a("NS8"), a("NS8"), F.Sign)
    act(a("nPEN"), I_, F.Identity, 0.0, -PEN)
    act(a("CI"), I_, F.Identity, 0.0, float(CEN))
    for z, v in enumerate((ST * 32 / OFF, float(-V))):
        lin(blk("IS", z, 128), I_, v)
    act(a("RST"), a("K16"), F.Relu, 16 * BIG, -16 * BIG)
    for i in range(3):
        act(blk("NST", i), a("K16"), F.Sign)
    act(a("KI"), a("K16"), F.Identity, -K0)
    for k in (14, 15):
        act(a("KI", k, 256, 16), a("K16", 0, 16), F.Identity, PEN, 0.0)
    act(a("KH"), a("K16"), F.Identity, 0.0, 1.0 / 16)
    for x, v in ((a("XF", V, NUL), LIFT), (a("X", VP + V, VP + NUL), 0.0), (a("XF", NUL, VP), LIFT + DEAD), (a("X", VP + NUL, 2 * VP), 2 * DEAD),
                 (a("XF", VP + V, VP + NUL), LIFT), (a("XF", VP + NUL, 2 * VP), LIFT + 2 * DEAD),
                 (CNUL, float(NUL - CEN)), (a("DK"), 1.0), (t3("TA"), 0.0), (t3("TB"), 0.0), (a("pd", 0, 8), 0.0), (a("pd", 264, 272), 0.0)):
        ms(x, v)
    for x, v in ((blk("DF", 0), LIFT + DEAD), (blk("DF", 1), LIFT + 2 * DEAD), (a("ones"), 1.0), (a("RF"), 0.0), (a("RB"), 0.0),
                 (blk("DM", 0), 0.0), (blk("DM", 1), 0.0), (blk("DM", 2), 4096.0), (blk("G0", 0), 1.0), (blk("G1", 0), 0.0), (blk("G1", 1), -1.0), (blk("CC", 3), -0.5),
                 (a("G0", 15, 256, 16), 0.0), (a("G1", 271, 512, 16), -40.0), (a("RF", 14, 256, 16), BIG), (sb(CK), -K0)):
        either(ms(x, v), act(x, a("K16", 0, cnt(x)), F.Identity, v, 0.0))["r"] = regs(a("K16"))
    act(a("DF", 0, 16), a("DF", 0, 16), F.Silu)["cost"] += 1300


def cands(h, tab, lst, hs):
    co = a("CO", 256 * h + 128 * hs[0], 256 * h + 128 * hs[1])
    ts(co, ind(a(tab), a(lst, 8 * hs[0], 8 * hs[1])), float(CEN * h), A.add)
    ts(a("Cc", 128 * hs[0], 128 * hs[1]), co, float(-CEN), A.add)
    flip("PT", "Cc", 16 * h, hs)


def paths(r):
    ts(a("de"), a("Wn", 0, 256, 2), -64.0, A.mult, 1700.0 * 64, A.add)
    scan(a("es"), a("de"), a("Wn", 0, 256, 2), 0.0, A.max, A.min)
    cp(a("DL", 0, 256, 16), a("es", 7, 128, 8))
    ts(a("el"), t3(tolist(0, 256), 0), float(CEN), A.add)
    scan(a("en"), a("de"), a("KN"), 0.0, A.max, A.min)
    if r < RO - 1:
        bk = dbank()
        for h in range(2):
            o, x = t3("Wz", (8 * h, 8 * h + 8), (16 * h, 16 * h + 16)), blk("Wn", h, 128)
            POST.append(gcp(o, x) if r else cp(o, x))
        pe([(t3(bk, (8 * z, 8 * z + 8)), t3("Wz", (8 * h, 8 * h + 8), (z, 32, 2)), a("Ih"), h == 0, h == 1) for z in range(2) for h in range(2)])
        ts(a("WO"), t3(bk, (0, 16)), float(CEN), A.add)
    for nm, z, n in (("WXo", 1, 6), ("WXe", 0, 7)):
        act(t3(nm, None, (0, n)), t3("PW", (0, 16), (z, z + 2 * n, 2)), F.Copy)
        for m in (n, 2 * n):
            o, x = t3(nm, None, (m, 2 * m)), t3(nm, None, (0, m))
            either(act(o, x, F.Copy), cp(o, x))
    if r:
        cands(0, "CA", "el", (0, 2))


def fit(h, hs):
    for H in range(*hs):
        pe([(a(KK[H], 0, 128), I_, a("KH", 0, 128), True, False)])
    for s in range(6 + h):
        tt(a("EQ", 256 * s + 128 * hs[0], 256 * s + 128 * hs[1]), t3("PT", (16 * h + 8 * hs[0], 16 * h + 8 * hs[1])),
           t3(("WXo", "WXe")[h], (8 * hs[0], 8 * hs[1]), (s, s + 16)), A.is_equal)
        pe([(a(KK[H], 0, 128), a("PENI"), blk("EQ", 2 * s + H, 128), False, False) for H in range(*hs)], True)


def hop(h, H, win, nv):
    for j in range(4 * H, 4 * H + 4):
        o = gather(blk("XC", j, 512), ind(win, blk("CO", 8 * h + j, 32)))
        if (h, H) == (0, 1):
            LATE.append(o)
    xs, xc = blk("xs", 2 * h + H, 128), lambda i, st=16: a("XC", 2048 * H + i, 2048 * H + 2048, st)
    mm, key = lambda c, j=0, st=1: a("MM", 2048 * H + 512 * c + j, 2048 * H + 512 * c + 512, st), lambda i: a(KK[H], i, 128, 16)
    four = lambda bk, w, first: [(t3(bk, None, (j, 16, 4)), w, xs, first and j == 0, j == 3) for j in range(4)]
    if nv:
        pe([(a(KK[H], 0, 128), xs, blk("nB", nv, 128), False, False)] + [(key(i), xc(i), Bm16, False, False) for i in range(16) if i % 4 < nv], True)
        xe = dbank()
        pe(four(xe, I_, True))
        for c in range(nv):
            tt(mm(c), xc(c, 4), t3(xe), A.max)
    for c in range(4):
        if c >= nv:
            bk = dbank()
            pe([(t3(bk), I_, xc(c, 4), True, False)] + four(bk, a("nIb"), False))
            act(mm(c), t3(bk), F.Abs, 0.0, 0.5)
        pe([(key(c + 4 * j), mm(c, j, 4), B32, False, False) for j in range(4)], True)
    close(KK[H])
    key, pm, eq, ne, y = a(KK[H], 0, 128), blk("pm", 2 * h + H, 128), blk("eq", H, 128), blk("eq", 2 + H, 128), blk("Y", H, 128)
    scan(pm, a("RST", 0, 128), key, 0.0, A.add, A.min)
    tt(eq, key, pm, A.is_equal)
    lin(ne, eq, -1.0, 1.0)
    tt(y, t3("PT", (16 * h + 8 * H, 16 * h + 8 * H + 8)), eq, A.mult)
    scan(blk("YS", 2 * h + H, 128), ne, y, 0.0, A.mult, A.add)


def row(h, k, nm="VV", n=2048):
    return a(nm, 2048 * (k & 1) + k // 2 + 8 * h, 2048 * (k & 1) + n, 16)


def rows(r):
    for j in range(8):
        o = gather(blk("VV", j, 512), ind(OWNN if j < 4 else PARN if r else PARN0, blk("WO", j, 32)))
        for x in LATE[-4:]:
            x["after"].append(o)
    if r > 0:
        pe([(a("PE", 0, 256), I_, a("K16"), True, False)]
           + [(a("PE", 128 * h + k, 128 * h + 128, 16), row(h, k), Bm16, False, False) for h in range(2) for k in range(0, 16, 2)])
        pe([(a("PE", 128 * h + k, 128 * h + 128, 16), row(h, k), Bm8, False, h == 1 and k == 15) for h in range(2) for k in range(1, 16, 2)])
        scan(a("pd", 8, 264), a("RST"), a("PE", 0, 256), 0.0, A.add, A.min)


def sa(d):
    return [(a("Ih"), a("Wn", d, d + 256)), (blk("I2", 0, 128), t3("TA", None, (d + 2, d + 18))), (blk("I2", 1, 128), t3("TA", None, (d, d + 16)))]


def cut():
    jj, ub = a("pd", 23, 264, 16), a("G1", 14, 256, 16)
    act(a("RF", 1, 256, 2), a("pd", 12, 268, 2), F.Relu, -4 * OFF, -4.0)
    act(a("RB", 0, 256, 2), a("pd", 5, 261, 2), F.Relu, 4 * OFF, 4.0)
    act(a("RB", 2, 256, 16), a("K16", 0, 16), F.Identity, BIG, 0.0)
    act(sb(PF_), a("pd", 10, 264, 16), F.Relu, -4 * OFF, -4.0)
    for z in range(2):
        act(a("PQ", z, 256, 2), a("pd", 8 + 2 * z, 264 + 2 * z, 2), F.Relu, -OFF / 32, -1.0 / 32)
    act(sm(NQ), NL, F.Identity, -0.5 - 2 * OFF, 0.5)
    act(sm(NJ), NL, F.Identity, -2 * OFF)
    tt(sm(QQ), jj, sm(NQ), A.subtract)
    act(sm(W0), sm(QQ), F.Relu, 0.0, -BIG)
    act(sm(W1), sm(QQ), F.Relu, BIG, BIG)
    act(sm(W2), sm(QQ), F.Relu, BIG, -BIG)
    act(sm(W3), sm(QQ), F.Relu, 0.0, BIG)
    ts(ub, sm(QQ), 0.5, A.is_lt)
    ts(a("G1", 15, 256, 16), sm(QQ), 0.0, A.is_equal, -1.0, A.mult)
    act(sm(E1), jj, F.Identity, OFF - 0.25, 0.5)
    ts(sm(FL), sm(E1), M1, A.add, M1, A.subtract)
    act(sm(S_), sm(FL), F.Identity, 2.0, 2.0)
    tt(sm(US), ub, sm(S_), A.mult)
    tt(sb(POS), NL, sm(US), A.subtract)
    tt(sm(U1), sm(NJ), jj, A.subtract)
    tt(sm(U1), sm(U1), sm(QQ), A.min)
    act(sb(PI), sm(U1), F.Relu, 0.0, BIG)
    act(sb(NEG), sb(POS), F.Relu, 0.0, -BIG)
    pg = slot()
    group(pg, [(I_, sb(x)) for x in (CK, POS, PI)])
    act(a("G1", 270, 512, 16), pg, F.Identity, 13.5 - K0, -1.0)
    act(sm(FH), sm(FL), F.Identity, 0.0, 0.5)
    ts(a("DM", 256, 512, 16), sm(FL), 2.0, A.is_ge)
    tt(a("DM", 0, 256, 16), sm(FH), a("DM", 256, 512, 16), A.subtract)
    act(a("DM", 512, 768, 16), sm(FL), F.Identity, -55296.0, 8192.0)
    scan(a("UM"), a("NST"), a("DM"), 0.0, A.mult, A.add)
    tt(t3("TA", None, (0, 16)), WP, blk("UM", 0), A.mult)
    group(WB, sa(0))
    tt(t3("TB", None, (0, 16)), WB, blk("UM", 1), A.mult)
    either(ts(blk("PQ", 1), blk("UM", 2), 0.0, A.max), act(blk("PQ", 1), blk("UM", 2), F.Relu))
    tt(sm(NW), a("Wn", 0, 256, 16), a("PQ", 0, 256, 16), A.add)
    ts(sb(WR), sm(NW), OFF / 32 + V - ST - CEN, A.is_ge)


def edges(r, t):
    if t == 0:
        pe([(a("PE", 0, 256), I_, a("KI"), True, False)])
        if r > 0:
            pe([(a("PE", z, 256, 16), I_, sb(PF_), False, False) for z in range(2)], True)
    key = lambda h, k: a("PE", 128 * h + k, 128 * h + 128, 16)
    hk = [(h, k) for h in range(2) for k in range(t, 14, 2)]
    if EA[r][t] == "S":
        for j0 in range(0, 14, 4):
            bk, js = dbank(), list(enumerate(hk[j0:j0 + 4]))
            o = lambda j: t3(bk, (8 * j, 8 * j + 8))
            pe([m for j, (h, k) in js for m in ((o(j), I_, row(h, k), True, False), (o(j), a("nIb"), row(h, k + 1), False, True))])
            act(blk("ED", 16 * t + j0, 128, 0, 128 * len(js)), t3(bk, (0, 8 * len(js))), F.Abs)
            pe([(key(h, k), blk("ED", 16 * t + j0 + j, 128), B16, False, False) for j, (h, k) in js], True)
    else:
        nc = int(EA[r][0])
        for z in range(2):
            pe([(key(h, k)[:5] + ((0, 32 * nc),), row(h, k + z, "VV", 512 * nc), Bm16, False, False) for h, k in hk], True)
        for c in range(4):
            odd = blk("VV", 4 + c, 512, -t, 512)
            if c >= nc:
                bk = dbank() if (c, t) != (3, 1) else "PT"
                pe([(t3(bk), a("nIb"), blk("VV", c, 512), True, False)])
                pe([(t3(bk), I_, odd, False, True)])
                act(blk("ED", 4 * t + c, 512), t3(bk), F.Abs, 0.0, 0.5)
            else:
                if t == 0:
                    pe([(t3(KK[c]), I_, blk("VV", c, 512), True, True)])
                tt(blk("ED", 4 * t + c, 512), odd, t3(KK[c]), A.max)
        pe([(key(h, k), row(h, k + 2 * t, "ED"), B32, False, False) for h, k in hk], True)


def pick(z, c):
    return a("PE", 256 + 80 * z + c, 336 + 80 * z, 5)


def ends(r):
    close("PE")
    if r == 0:
        scan(a("pe", 0, 256), a("RST"), a("PE", 0, 256), 0.0, A.add, A.min)
        ks, nv = a("pe", 15, 256, 16), 1
    else:
        scan(rev("pe", 0, 256), rev("RF", 0, 256), rev("PE", 0, 256), 0.0, A.add, A.min)
        scan(a("pe", 241, 497), a("RB"), a("PE", 0, 256), 0.0, A.add, A.min)
        for z in range(2):
            tt(sm(X0 + 2 * z, 32), a("pe", 0, 512, 16), sm(W0 + 2 * z, 32), A.add)
            tt(sm(KZ + z), sm(X0 + 2 * z), sm(X1 + 2 * z), A.min)
        tt(sm(KX), sm(KO), sm(BND), A.min)
        tt(sb(WEF), sm(U3), sm(KX), A.is_lt)
        tt(sm(KX), sm(KX), sm(U3), A.min)
        ks, nv = sm(KZ, 32), 2
    ts(sm(T1_, 16 * nv), ks, M16, A.add, M16, A.subtract)
    tt(a("DK", 0, 256 * nv, 16), sm(T1_, 16 * nv), ks, A.subtract)
    tt(a("sb", 16 * NP_, 16 * (NP_ + nv)), ks, sm(BND, 16 * nv), A.is_ge)
    scan(a("UK", 0, 256 * nv), a("NST", 0, 256 * nv), a("DK", 0, 256 * nv), 0.0, A.mult, A.add)
    ts(a("OH", 0, 256 * nv), a("UK", 0, 256 * nv), M2, A.add, M2 + 8, A.is_equal)
    for v in range(nv):
        tt(blk("YE", v), WP, blk("OH", v), A.mult)
    for z in range(2):
        scan(blk("YA", z, 256, 0, 128 * nv), a("NS8", 0, 128 * nv), a("YE", z, 256 * nv, 2), 0.0, A.mult, A.add)
    ya = lambda z, v: a("YA", 256 * z + 128 * v + 7, 256 * z + 128 * v + 128, 8)
    ml = [(a("PE", 256, 416), a("PENI"), blk("R1", int(r > 0), 160))]
    for z in range(2):
        ml += [(pick(z, 1), a("Ih"), ya(z, 0)), (pick(z, 1), a("PENI"), sb(NP_))]
        if r:
            ml += [(pick(z, 0), a("Ih"), ya(z, 1)), (pick(z, 0), a("PENI"), sb(NP2)), (pick(z, 0), a("PENI"), sb(WEF)), (pick(z, 2), a("nPEN"), sb(WEF)),
                   (pick(z, 2), a("Ih"), a("YS", 15, 256, 16) if z else a("es", 7, 128, 8))]
    if r:
        ml += [(pick(1, 3), a("Ih"), a("YS", 15, 256, 16))]
    pe([(a("PE", 256, 416), a("Ih"), a("RC"), True, False)] + [m + (False, r == 0 and i == len(ml) - 1) for i, m in enumerate(ml)])


def equal():
    dv, ra, rb = lambda k: t3("DV", None, (16 * k + 8, 16 * k + 16)), a("ra", 4, 80, 5), a("ra", 84, 160, 5)
    ts(dv(6), ra, 1.0 / 2048, A.mult)
    ts(dv(8), ra, 1.0 / 2048, A.mult)
    cp(dv(7), rb)
    tt(sm(VT), ra, rb, A.mult)
    ts(dv(1), sm(VT), 1.0 / 2048, A.mult)
    act(sm(RED), sm(VT), F.Identity, 0.0, 1.0 / 2048)
    tt(dv(3), sm(RED), dv(1), A.subtract)
    bk = dbank()
    pe([(t3(bk, (8 * j, 8 * j + 8)), t3("DV", h, (c0, c0 + 128)), a("Ih"), j > 0 or h == 0, j > 0 or h == 1)
        for j, h, c0 in ((0, 0, 8), (0, 1, 0), (1, 0, 24), (2, 0, 16), (3, 1, 16))])
    cp(a("RT"), t3(bk))
    for gm in range(8):
        ts(t3("LL", None, (16 * gm, 16 * gm + 16)), a("RT", 0, 128), col(MK + gm), A.mult)
    c1 = 0
    for i, (q, bs) in enumerate(VQ):
        ns = [16 * b + 16 for b in bs]
        if q == "D":
            bk = dbank()
            part = [t3(bk, (0, bs[0] + 1)), t3(bk, (bs[0] + 1, bs[0] + bs[1] + 2))]
            tri = t3(bk, (bs[0], bs[0] + bs[1] + 2, bs[1] + 1))
        else:
            w = SCR[q][1][2]
            part = [t3(q, j, (w - n, w)) for j, n in enumerate(ns)]
            tri = t3(q, (0, len(bs)), (w - 16, w))
        pe([(part[j], t3("LL", b % 8), blk("RT", 1 + b // 8, 128, 0, ns[j]), j == 0, False) for j, b in enumerate(bs)]
           + [(tri, I_, a("TRI", 0, cnt(tri)), False, True)])
        if q == "D":
            act(a("MM", c1, c1 + sum(ns)), t3(bk, (0, sum(ns) // 16)), F.Abs)
        for j, b in enumerate(bs):
            n = ns[j]
            if q == "D":
                scan(a("ED", 128 * b + 128 - n // 2, 128 * b + 128), a("MM", c1, c1 + n // 2), a("MM", c1 + n // 2, c1 + n), BIG, A.min, A.min)
                c1 += n
            else:
                red(a("ED", 128 * b + 127, 128 * b + 128), part[j], A.min)["after"] += LAST


def program():
    for i in range(NCH):
        load("Y", blk("X", i, CW), (lambda i: lambda T: T.pts[:, CW * i:CW * i + CW])(i), "lx%d" % i, 2200 + 400 * i)
    load("S", a("wi"), lambda T: T.way[:, :], "lw", 2200)
    load("S", a("ci", p=(0, 8)), lambda T: T.cnt[:, :], "lc", 2200)
    load("S", a("ti", p=(0, 8)), lambda T: T.th[:, :], "lt", 2200)
    ss = []
    for i in range(NCH):
        ss.append(op("G", (lambda i: lambda g, T, c: c["big"]("X", i))(i), [blk("X", i, CW)], [], 1500 if i == 0 else RI, track=False))
        ss[-1]["prio"] = 1e9
    left = op(None, None, [a("X", 0, V)], [], 0, tok=("ls0", None), lat=5000, after=ss)
    for i in range(NCH):
        load("Y", blk("CA", i, CW), (lambda i: lambda T: T.cand[:, CW * i:CW * i + CW])(i), "lk%d" % i, 3000 + 1500 * i)["after"].append(left)
    op(None, None, [], [PAR0], 0, tok=("xarr", None), lat=8000, after=ss)
    for i in range(NCH):
        for j in (2 * i, 2 * i + 1):
            ts(blk("CU", j, CW // 2), blk("CA", j, CW // 2), float(-CEN), A.add)
        sc = op("G", (lambda i: lambda g, T, c: c["big"]("C", i))(i), [blk("CU", i, CW), PAR0], [], RI, track=False, after=ss + ([sc] if i else []))
        op(None, None, [], [blk("CQ", i, CW)], 0, tok=("ca%d" % i, None), lat=13000 + 1000 * i, after=[sc])
    for i in range(2 * NCH):
        lin(blk("XF", i, CW // 2), blk("X", i, CW // 2), 1.0, LIFT)
        lin(blk("XF", i, CW // 2, VP), blk("X", i, CW // 2, VP), 1.0, LIFT)
    consts()
    for j in range(2 * NCH):
        bk = t3(dbank(), (0, CW // 32))
        pe([(bk, a("Ih"), blk("CQ", j, CW // 2), True, True)])
        gather(blk("CP", j, CW // 2), bk)
    p8 = (0, 8)
    ts(a("Cc"), a("wi"), float(-CEN), A.add)
    flip("PW", "Cc")
    cp(a("cth", 0, 256, p=p8), a("ci", p=p8))
    ts(a("cth", 256, 512, p=p8), a("ti", p=p8), 16.0, A.mult, -8.0, A.add)
    pe([(blk("KA", j, 8), a("cth", 128 * j, 128 * j + 128, p=p8), a("I32", 0, 8, p=p8), True, True) for j in range(4)])
    act(a("DM", 512, 768, 16), a("KA", 0, 16), F.Identity, 2048.0, -4096.0)
    for z in range(2):
        act(sm(BND + z), a("KA", 16, 32), F.Copy)
        act(sm(TH16 + z), a("KA", 16, 32), F.Identity, 128 * 15.5)
    scan(blk("UM", 2), blk("NST", 0), blk("DM", 2), 0.0, A.mult, A.add)
    tt(a("Wf"), WP, blk("UM", 2), A.max)
    ts(WN, a("Wf"), float(NUL - CEN), A.min)
    pe([(WP, a("Ih"), WN, True, True)])
    paths(0)
    rows(0)
    edges(0, 0)
    edges(0, 1)
    cands(0, "CA", "el", (0, 2))
    ends(0)
    for r in range(RO):
        last = r == RO - 1
        SEEN.clear()
        scan(a("ra"), a("RS5"), a("PE", 256, 416), 0.0, A.add, A.min)
        cp(a("DL", 512, 1024, 16), a("ra", 4, 160, 5))
        bk = t3(tolist(512, 512), (0, 2))
        ts(a("ab"), bk, float(CEN), A.add)
        lin(a("abf"), bk, TINY, CEN * TINY)
        if r > 0:
            paths(r)
        equal()
        mid, rmid = blk("mid", r), blk("rmid", r)
        for z in range(2):
            gather(blk("xm", z), ind((OWND, PARD if r else PARN0)[z], blk("ab", z, 16)))
        bk = t3(dbank(), (0, 16))
        group(bk, [(I_, blk("xm", 0)), (I_, blk("xm", 1)), (I_, blk("CC", 3))])
        act(a("xc"), bk, F.Identity, M2)
        act(mid, a("xc"), F.Identity, -0.5 * M2, 0.5)
        lin(blk("DF", 2), a("xc"), 0.5, LIFT - 0.5 * M2)

        def e(g, T, c, r=r, mid=mid, rmid=rmid):
            c["one"](mk(T, rmid), mk(T, mid), "am%d" % r)
        s = op("G", e, [mid], [], RI, track=False)
        op(None, None, [], [rmid], 0, tok=("am%d" % r, None), lat=RL + 2000, after=[s])
        lin(blk("DF", 3), rmid, 1.0, LIFT)
        tt(sm(RED), sm(VB), a("ED", 127, 2048, 128), A.subtract)
        for z in range(2):
            tt(blk("ef", z, 16), sm(RED), blk("abf", z, 16), A.max)
        ts(blk("eff", r, 32), a("ef"), 1.0 / TINY, A.mult)
        ea, eb, ra, rk = blk("eff", 2 * r, 16), blk("eff", 2 * r + 1, 16), blk("rl", 2 * r, 16), blk("rl", 2 * r + 1, 16)

        def e(g, T, c, r=r, ea=ea, eb=eb, ra=ra, rk=rk):
            c["two"](mk(T, ra), mk(T, ea), "aa%d" % r, mk(T, rk), mk(T, eb), "ak%d" % r)
        s = op("G", e, [ea, eb], [], RI, track=False)
        for x in POST[-2:] if 0 < r < RO - 1 else ():
            x["after"].append(s)
        op(None, None, [], [ra], 0, tok=("aa%d" % r, None), lat=RL, after=[s])
        op(None, None, [], [rk], 0, tok=("ak%d" % r, None), lat=RL, after=[s])
        if not last:
            act(a("wn", 0, 16), a("ef", 0, 16), F.Sign, V - 0.5, -1.0 / TINY)
            o = slot()
            pe([(o, a("ones"), a("wn", 0, 16), True, True)])
            act(sm(U2), o, F.Identity, (1024 - 15.5) / 16, 0.5, col(AC))
            act(col(AD), col(AC), F.Identity, M1, 1.0 / 32)
            act(col(AD), col(AD), F.Identity, 4096 * M1, -4096.0)
            act(col(AC), col(AC), F.Identity, col(AD), 128.0)
            act(sm(BND, 32), sm(TH16, 32), F.Identity, col(AC))
        fit(0, (0, 2))
        for w, o, x in ((OWND, ea, blk("DF", 2)), (PARD, eb, blk("DF", 1)), (OWND, rk, blk("DF", 0))):
            scatter(w, o, x)
        lin(blk("DF", 4), ind(PARD, ra), 2.0, -LIFT - 2 * DEAD)
        tt(ind(PARD, ra), blk("DF", 3), blk("DF", 4), A.max)
        hv = HVL if last else HV
        ts(blk("xs", 0), ind(OWN, a("el")), -LIFT, A.add, 255.0, A.min)
        if not last:
            bk = dbank()
            pe([(t3(bk, 0, (8 * H, 8 * H + 8)), blk("xs", H, 128), Bm16, True, True) for H in range(2)])
            act(sb(ED_), t3(bk, 0), F.Relu, -65200.0 * 4096, -4096.0)
        for H in range(2):
            hop(0, H, PAR, hv[0][H])
            fl = a("fl", 8 * H, 8 * H + 8)
            c0 = 256 + 768 * H
            cp(a("DL", c0, c0 + 128, 16), a("YS", 128 * H + 15, 128 * H + 128, 16))
            ts(fl, t3(tolist(c0, 128), 0, (0, 8)), float(CEN), A.add)
            cands(1, "CP", "fl", (H, H + 1))
            gather(blk("xs", 2 + H, 128), ind(PAR, fl))
        k1, k2 = a("pm", 15, 256, 16), a("pm", 271, 512, 16)
        act(sb(H1), k1, F.Relu, -16.0 * THR, 16.0)
        act(sb(H2), NL, F.Relu, -13.0 * BIG, BIG)

        def keys():
            o = slot()
            group(o, [(I_, NL), (a("nIb"), a("ones", 0, 16))] + [(I_, sb(x)) for x in (CK, PI, ED_)])
            tt(sm(U3), o, k1, A.add)

        def bounds():
            if not last:
                o = slot()
                group(o, [(I_, NL)] + [(I_, sb(x)) for x in (CK, PI, NEG, H1, H2)])
                lin(PC, o, 1.0)
            o = slot()
            group(o, [(a("nIb"), sb(H1)), (a("nIb"), sb(H2))])
            lin(PTH, o, 1.0, THR)

        def second(H):
            if last or H == 0:
                fit(1, (H, H + 1) if last else (0, 2))
            hop(1, H, OWN, hv[1][H])
        if last:
            act(a("G1", 270, 512, 16), NL, F.Identity, 13.5, -1.0)
            ts(a("Me"), WN, float(V - CEN), A.is_lt)
            tt(a("Wf"), WP, a("Me"), A.mult)
            for i in range(2 * NCH):
                if i < OS:
                    act(blk("X", i, CW // 2), blk("XF", i, CW // 2), F.Identity, -LIFT)
                ts(blk("XO", i, CW // 2), blk("X" if i < OS else "XF", i, CW // 2), -LIFT * (i >= OS), A.add, 255.0, A.min)
            store(lambda T: T.yx[:, :], lambda T: T.XO[:, :], a("XO"), "ox", 9000)
        steps = {"r": lambda: rows(r + 1), "c": cut, "k": keys, "0": lambda: edges(r + 1, 0), "1": lambda: edges(r + 1, 1), "e": lambda: ends(r + 1),
                 "b": bounds, "A": lambda: second(0), "B": lambda: second(1)}
        for x in ("AbB" if last else STEPS):
            steps[x]()
        ng = a("G0", 14, 256, 16)
        vb = dbank()
        pe([(t3(vb, (0, 16), k), a("Ih"), CNUL if k == 15 else a("YS", 271 - 256 * (k & 1), 512 - 256 * (k & 1), 16), True, True) for k in range(16)])
        tt(ng, k2, PTH, A.is_gt)
        if not last:
            tt(sm(Z1), k2, PC, A.add)
            tt(sb(WFH), sm(Z1), sm(KX), A.is_lt)
            pe([(pick(z, c), a(w), x, False, False) for z in range(2) for c, w, x in
                ((0, "PENI", ng), (1, "nPEN", ng), (2, "PENI", ng), (0, "PENI", sb(WFH)), (2, "PENI", sb(WFH)), (3, "nPEN", sb(WFH)))])
            pe([(pick(0, 3), a("Ih"), a("YS", 271, 512, 16), False, True)])
            w0, q0 = t3("PW", (0, 16), 0), a("PQ", 0, 256, 16)
            pe([(WB, w, x, i == 0, False) for i, (w, x) in enumerate(sa(2) + [(a("Ih"), t3("TB", None, (6, 22))), (a("nIh"), t3("TB", None, (2, 18)))])])
            pe([m + (False, False) for m in [(WP, a("Ih"), WN), (WP, I_, blk("PQ", 0)), (w0, a("nIb"), q0), (w0, blk("IS", 0, 128), q0), (w0, blk("IS", 1, 128), sb(WR)),
                                             (t3("PW", (0, 16), 15), a("nPEN"), a("G1", 15, 256, 16)), (WB, a("PENI"), blk("PQ", 1))]
                + [(t3("PW", (16 + 8 * h, 24 + 8 * h)), a("PENI"), a("ones")) for h in range(2)]])
            scan(rev("GU", 0, 256), rev("G0", 0, 256), rev("G1", 0, 256), 0.0, A.mult, A.add)
            pe([(WP, a("PENI"), blk("GU", 0), False, False), (WB, a("nPEN"), blk("GU", 0), False, True)])
        scan(rev("GU", 256, 512), rev("G0", 0, 256), rev("G1", 256, 512), 0.0, A.mult, A.add)
        ts(a("OA"), blk("GU", 1), M2, A.add, M2, A.is_equal)
        if last:
            tt(a("XV"), t3(vb, (0, 16)), a("OA"), A.mult)
        else:
            lin(a("NU"), a("OA"), -3968.0, float(NUL - CEN))
            tt(a("XV"), t3(vb, (0, 16)), a("NU"), A.max)
            tt(a("Wf"), WP, a("XV"), A.min)
            LAST[:] = [tt(WN, WB, a("Wf"), A.min)]
            pe([(WP, a("Ih"), WN, True, True)])
    act(sm(U1), ng, F.Identity, 2.0, -2.0)
    tt(a("wn", 16, 32), sm(U1), NL, A.add)
    pe([(t3("KA", h, None, p8), a("wn", 16 + 8 * h, 24 + 8 * h), I_, True, True) for h in range(2)])
    act(a("yc", p=p8), t3("KA", (0, 2), None, p8), F.Copy)
    for i, (x, w) in enumerate((("Wf", a("Ih")), ("Me", a("CI")), ("OA", a("CI")), ("XV", a("Ih")))):
        pe([(blk("PE", h, 128), blk(x, h, 128), w, i + h == 0, i + h == 4) for h in range(2)])
    gather(a("yo"), a("PE", 0, 256))
    store(lambda T: T.yw[:, :], lambda T: T.yo[:, :], a("yo"), "ow", 2500)
    store(lambda T: T.yn[:, :], lambda T: T.yc[0:8, :], a("yc"), "on", 2500)


def polish(sch, dl, ways, lat, head, rs, moves):
    N = len(dl)
    way = list(sch[5])
    lo, hi = [[KIND[o["sort"]][i] for o in OPS] for i in range(2)]
    eng, cost, cos2 = [ways[n][way[n]][0] for n in range(N)], [ways[n][way[n]][1] * lo[n] for n in range(N)], [ways[n][way[n]][1] * hi[n] for n in range(N)]
    cos2 = [c if e else SLOW * x for e, c, x in zip(eng, cos2, lat)]
    en2, tai2 = [0.0] * N, [0.0] * N

    def span(l):
        return max(end[n] - cost[n] + tail[n] for n in l) + DEAR * max(en2[n] - cos2[n] + tai2[n] for n in l)

    def tight(l):
        out = []
        for e, c, t in ((end, cost, tail), (en2, cos2, tai2)):
            x = [e[n] - c[n] + t[n] for n in l]
            top = max(x)
            out += [top, [n for n, y in zip(l, x) if y > top - SLACK and eng[n]]]
        return out[0] + DEAR * out[2], (out[1], out[3])
    sl = [[] for n in range(N)]
    for n in range(N):
        for d, w in dl[n]:
            sl[d].append((n, w))
    mp, mn = [-1] * N, [-1] * N
    for q in sch[1].values():
        for i in range(1, len(q)):
            mp[q[i][2]], mn[q[i - 1][2]] = q[i - 1][2], q[i][2]
    banks = [[x[2] for x in sorted(h)] for h in sch[6]]
    bp, bn = [()] * N, [-1] * N

    def link():
        for h in banks:
            for i, n in enumerate(h):
                bp[n] = tuple((m, 0.0 if eng[m] == "P" else SL) for m in head[h[i - 1]]) if i else ()
                for m in head[n]:
                    bn[m] = h[i + 1] if i + 1 < len(h) else -1
    link()
    order = sorted(range(N), key=lambda n: (sch[2][n], n))
    pos, end, tail = [0] * N, [0.0] * N, [0.0] * N
    for i, n in enumerate(order):
        pos[n] = i

    def ahead(p0, p1):
        for n in order[p0:p1]:
            m = mp[n]
            t, u = (end[m], en2[m]) if m >= 0 else (0.0, 0.0)
            for d, w in dl[n]:
                if end[d] + w > t:
                    t = end[d] + w
                if en2[d] + w > u:
                    u = en2[d] + w
            for d, w in bp[n]:
                if end[d] + w > t:
                    t = end[d] + w
                if en2[d] + w > u:
                    u = en2[d] + w
            end[n], en2[n] = t + cost[n], u + cos2[n]

    def behind(p1, p0=0):
        for n in reversed(order[p0:p1 + 1]):
            m = mn[n]
            t = tail[m] if m >= 0 and tail[m] > lat[n] else lat[n]
            u = tai2[m] if m >= 0 and tai2[m] > lat[n] else lat[n]
            for d, w in sl[n]:
                if tail[d] + w > t:
                    t = tail[d] + w
                if tai2[d] + w > u:
                    u = tai2[d] + w
            m = bn[n]
            if m >= 0:
                w = 0.0 if eng[n] == "P" else SL
                t, u = max(t, tail[m] + w), max(u, tai2[m] + w)
            tail[n], tai2[n] = t + cost[n], u + cos2[n]

    def unlink(n):
        if mp[n] >= 0:
            mn[mp[n]] = mn[n]
        if mn[n] >= 0:
            mp[mn[n]] = mp[n]

    def insert(n, x, y):
        mp[n], mn[n] = x, y
        if x >= 0:
            mn[x] = n
        if y >= 0:
            mp[y] = n

    def lift(u, v):
        p0, p1 = pos[u], pos[v]
        need, todo = {v}, [v]
        while todo:
            n = todo.pop()
            for d in [x[0] for x in dl[n]] + [x[0] for x in bp[n]] + [mp[n]]:
                if d >= 0 and pos[d] >= p0 and d not in need:
                    if d == u:
                        return False
                    need.add(d)
                    todo.append(d)
        seg = order[p0:p1 + 1]
        order[p0:p1 + 1] = [n for n in seg if n in need] + [n for n in seg if n not in need]
        for i in range(p0, p1 + 1):
            pos[order[i]] = i
        return True

    ahead(0, N)
    behind(N - 1)
    cur = span(order)
    keep = (cur, list(order), list(way), [list(h) for h in banks], list(end), list(cost))
    wb = N
    for it in range(moves + 1):
        if it % STAY == 0 or it == moves:
            ahead(0, N)
            behind(N - 1)
            cur = span(order)
            if cur < keep[0]:
                keep = (cur, list(order), list(way), [list(h) for h in banks], list(end), list(cost))
            if it == moves:
                break
            wa = max(0, wb - WIN // 2) if wb < N else 0
            wb = min(N, wa + WIN)
            cur, crit = tight(order[wa:wb])
        if not crit[it & 1]:
            continue
        v = crit[it & 1][int(rs.randint(len(crit[it & 1])))]
        fin = (end, en2)[it & 1]
        beg, x, undo = fin[v] - (cost, cos2)[it & 1][v], rs.rand(), None
        p0 = p1 = pos[v]
        if len(ways[v]) > 1 and x < 0.35:
            e, c = ways[v][1 - way[v]]
            i = p0 - 1
            while i >= 0 and eng[order[i]] != e:
                i -= 1
            if i < 0:
                continue
            old = (mp[v], mn[v], eng[v], cost[v], cos2[v])
            unlink(v)
            insert(v, order[i], mn[order[i]])
            eng[v], cost[v], cos2[v], way[v] = e, c * lo[v], c * hi[v], 1 - way[v]
            undo = 0
        elif bp[v] and max(fin[d] + w for d, w in bp[v]) >= beg - 1.0 and x < 0.8:
            b = [b for b in range(3) if v in banks[b]][0]
            old = [list(h) for h in banks]
            seg = None
            i = banks[b].index(v)
            if x < 0.5:
                b2 = (b + 1 + int(rs.randint(2))) % 3
                j = len([m for m in banks[b2] if pos[m] < p0])
                banks[b][i:], banks[b2][j:] = banks[b2][j:], banks[b][i:]
                if (j and max(pos[m] for m in head[banks[b2][j - 1]]) > p0) or (i < len(banks[b]) and max(pos[m] for m in head[banks[b][i - 1]]) > pos[banks[b][i]]):
                    banks[:] = old
                    continue
                link()
            else:
                u = banks[b][i - 1]
                banks[b][i - 1], banks[b][i] = v, u
                link()
                p0, p1 = pos[u], max(pos[m] for m in head[v])
                seg = order[p0:p1 + 1]
                if not all(lift(u, m) for m in head[v] if pos[m] > pos[u]):
                    banks[:] = old
                    link()
                    order[p0:p1 + 1] = seg
                    for k, m in enumerate(seg):
                        pos[m] = p0 + k
                    continue
            undo = 1
        else:
            if x > 0.6 and mn[v] >= 0:
                u, v = v, mn[v]
                for k in range(int(FAR * rs.rand() ** 2)):
                    v = mn[v] if mn[v] >= 0 else v
                p0, p1 = pos[u], pos[v]
                seg, old, mv = order[p0:p1 + 1], (mp[u], mn[u]), u
                unlink(u)
                insert(u, v, mn[v])
            else:
                u = mp[v]
                if u < 0 or fin[u] < beg - 1.0:
                    continue
                for k in range(int(FAR * rs.rand() ** 2)):
                    u = mp[u] if mp[u] >= 0 else u
                p0, p1 = pos[u], pos[v]
                seg, old, mv = order[p0:p1 + 1], (mp[v], mn[v]), v
                unlink(v)
                insert(v, mp[u], u)
            if not lift(u, v):
                unlink(mv)
                insert(mv, old[0], old[1])
                continue
            undo = 2
        p2 = min(N, p1 + 60)
        was = [end[n] for n in order[p0:p2]], [en2[n] for n in order[p0:p2]], order[p0:p2]
        ahead(p0, p2)
        lim = cur + COOL * (1.0 - it / moves) * -np.log(1.0 - rs.rand())
        ok = span(order[p1 + (p1 + 1 < p2):p2]) <= lim
        p3 = max(p2, wb)
        if ok and p3 > p2:
            ahead(p2, p3)
            ok = span(order[p2:p3]) <= lim
            if not ok:
                was = None
        if ok:
            behind(p3 - 1 if undo == 1 else p1, min(p0, wa))
            cur, crit = tight(order[wa:wb])
            continue
        if undo == 0:
            unlink(v)
            insert(v, old[0], old[1])
            eng[v], cost[v], cos2[v], way[v] = old[2], old[3], old[4], 1 - way[v]
        else:
            if undo == 1:
                banks[:] = old
                link()
            else:
                unlink(mv)
                insert(mv, old[0], old[1])
            if seg:
                order[p0:p1 + 1] = seg
                for k, m in enumerate(seg):
                    pos[m] = p0 + k
        if was:
            for t, u, n in zip(*was):
                end[n], en2[n] = t, u
        else:
            ahead(p0, p3)
    cur, order, way, banks, end, cost = keep
    beg = [end[n] - cost[n] for n in range(N)]
    for i, n in enumerate(order):
        beg[n] += 1e-6 * i
    slots = {e: [(beg[n], end[n], n) for n in order if ways[n][way[n]][0] == e] for e in "VSPGY"}
    return cur, slots, beg, beg, end, way, [[(beg[n], 0.0, n) for n in h] for h in banks]


def plan():
    program()
    last_w, last_r = {}, {}
    bank = lambda q: SCR[q[0]][0] == "psum"
    for o in OPS:
        raw, oth = set(), set()
        for q in o["r"]:
            raw.update(d for (c0, c1, d) in last_w.get(q[0], []) if bank(q) or (c0 < q[2] and q[1] < c1))
            if bank(q):
                oth.update(d for (c0, c1, d) in last_r.get(q[0], []) if OPS[d]["eng"] != o["eng"] or o["alt"] or OPS[d]["alt"])
        for q in o["w"]:
            oth.update(d for (c0, c1, d) in last_w.get(q[0], []) + last_r.get(q[0], [])
                       if (bank(q) or (c0 < q[2] and q[1] < c1)) and not (o["acc"] and OPS[d]["acc"]))
        for q in o["w"]:
            keep = lambda t: o["acc"] or not (bank(q) or (q[1] <= t[0] and t[1] <= q[2]))
            last_w[q[0]] = [t for t in last_w.get(q[0], []) if keep(t)]
            last_r[q[0]] = [t for t in last_r.get(q[0], []) if keep(t)]
        for q in o["w"]:
            last_w[q[0]].append((q[1], q[2], o["n"]))
        if o["track"]:
            for q in o["r"]:
                last_r.setdefault(q[0], []).append((q[1], q[2], o["n"]))
        if o["eng"] is None:
            raw, oth = set(), set()
        o["deps"] = (raw | oth | set(x["n"] for x in o["after"])) - {o["n"]}
        o["know"] = {}
        o["early"] = set()
        o["wait"] = set(d for d in o["deps"] if not (OPS[d]["eng"] == o["eng"] and o["eng"] in "PG"))
    N = len(OPS)
    use = {}
    for o in OPS:
        for q in set(q[0] for q in o["r"] + o["w"] if q[0][:2] == "D#"):
            use.setdefault(q, []).append(o["n"])
    head, inside = {}, set()
    for q, l in use.items():
        head[l[0]] = l
        inside.update(l[1:])
        first = OPS[l[0]]
        for m in l[1:]:
            for d in OPS[m]["deps"] - set(l) - first["deps"]:
                first["deps"].add(d)
                first["early"].add(d)
    ways = [[(o["eng"], o["cost"])] + ([(o["alt"][0], o["alt"][2])] if o["alt"] else []) for o in OPS]
    lat = [o["lat"] for o in OPS]
    dl = [[(d, lat[d] + SL if d in o["wait"] else -o["cost"] if d in o["early"] else 0.0) for d in sorted(o["deps"])] for o in OPS]
    rl = [[] for o in OPS]
    for n in range(N):
        for d, w in dl[n]:
            rl[d].append((n, w))
    topo, left = [n for n in range(N) if not dl[n]], [len(x) for x in dl]
    for d in topo:
        for n, w in rl[d]:
            left[n] -= 1
            if not left[n]:
                topo.append(n)
    topo.reverse()
    pr = [o["cost"] + o["lat"] for o in OPS]
    for n in topo:
        pr[n] += OPS[n].get("prio", 0.0)
        for d, w in dl[n]:
            pr[d] = max(pr[d], pr[n] + w + OPS[d]["cost"] + 1.0)
    zero = [0.0] * N

    def place(pr, bias, dl=dl, base=zero, fix=None):
        slots = {e: [] for e in "VSPGY"}
        beg, end, rdy, way = [0.0] * N, [0.0] * N, [0.0] * N, [0] * N
        held = [[] for b in range(3)]

        def put(n, t0):
            for d, w in dl[n]:
                if end[d] + w > t0:
                    t0 = end[d] + w
            rdy[n] = t0
            best = None
            for j in (range(len(ways[n])) if fix is None else (fix[n],)):
                e, c = ways[n][j]
                t, i = t0, 0
                if e is not None:
                    sl = slots[e]
                    i = len(sl)
                    while i > 0 and sl[i - 1][1] > t:
                        i -= 1
                    while i < len(sl) and sl[i][0] < t + c:
                        t = max(t, sl[i][1])
                        i += 1
                f = t + c + (bias[n] if j else 0.0)
                if best is None or f < best[0]:
                    best = (f, j, e, c, t, i)
            f, j, e, c, t, i = best
            if e is not None:
                slots[e].insert(i, (t, t + c, n))
            beg[n], end[n], way[n] = t, t + c, j
        for n in sorted(range(N), key=lambda n: (-pr[n], n)):
            if fix is not None or n not in head:
                if fix is not None or n not in inside:
                    put(n, base[n])
                continue
            t0 = 0.0
            while True:
                for m in head[n]:
                    put(m, t0 if m == n else 0.0)
                t1, t2 = beg[n], max(end[m] for m in head[n]) + SL
                nxt = [max([y for x, y, m in h if x < t2 and t1 < y] + [0.0]) for h in held]
                if min(nxt) == 0.0:
                    free = [b for b in range(3) if nxt[b] == 0.0]
                    held[max(free, key=lambda b: max([y for x, y, m in held[b] if y <= t1] + [0.0]))].append((t1, t2, n))
                    break
                for m in head[n]:
                    slots[ways[m][way[m]][0]].remove((beg[m], end[m], m))
                t0 = min(nxt)
        return max(end[n] + lat[n] for n in range(N)), slots, beg, rdy, end, way, held

    def chain(sch):
        return [(m, h[i + 1][2]) for h in map(sorted, sch[6]) for i in range(len(h) - 1) for m in head[h[i][2]]]

    def mend(p, dl, order, step):
        for n in order:
            for d, w in dl[n]:
                if p[d] <= p[n]:
                    p[d] = p[n] + step
        return p

    def turn(sch, bias):
        r2 = [list(x) for x in rl]
        for m, n in chain(sch):
            r2[m].append((n, SL))
        back = place(mend([sch[4][n] + 1e-6 * n for n in range(N)], r2, sorted(range(N), key=lambda n: (sch[2][n], n)), 1e-3), bias, r2, lat, sch[5])
        p = mend([back[4][n] - 1e-6 * n for n in range(N)], dl, topo, 1e-3)
        return place(p, bias), p

    rs = np.random.RandomState(SEED)
    bias = [-LEAN0] * N
    kin = {}
    for o in OPS:
        kin.setdefault(o["kind"], []).append(o["n"])
    free = [n for n in range(N) if len(ways[n]) > 1]
    cur = best = place(pr, bias)
    for it in range(TRIES):
        fin, slots, beg, rdy, end, way, hd = cur
        after = {}
        for m, n in chain(cur):
            if n not in after or end[m] > end[after[n]]:
                after[n] = m
        prev = {sl[i][2]: sl[i - 1][2] for sl in slots.values() for i in range(1, len(sl))}
        n = max(range(N), key=lambda n: end[n] + lat[n])
        held = []
        while beg[n] > 0:
            if n in after and end[after[n]] + SL >= beg[n] - 1.0:
                held.append((n, 200.0))
                prev[n] = n = after[n]
            elif beg[n] > rdy[n] + 1.0:
                if pr[prev[n]] > pr[n]:
                    held.append((n, beg[n] - rdy[n]))
                n = prev[n]
            else:
                n = max(dl[n], key=lambda x: end[x[0]] + x[1])[0]
        p2, b2 = list(pr), bias
        for j in range(int(rs.randint(1, 4)) if held else 0):
            n, w = held[int(rs.randint(len(held)))]
            up = max(w * float(rs.rand()), pr[prev[n]] + 1.0 - p2[n])
            for m in (kin[OPS[n]["kind"]] if it % 4 else [n]):
                p2[m] += up
        if rs.rand() < RAND:
            x = 3000.0 * float(rs.randn())
            for m in kin[OPS[int(rs.randint(N))]["kind"]]:
                p2[m] += x
        if it % 3 == 0:
            b2 = list(bias)
            n = free[int(rs.randint(len(free)))]
            x = (1.0 if way[n] else -1.0) * LEAN * float(rs.rand())
            for m in kin[OPS[n]["kind"]]:
                b2[m] = x
        t2 = place(mend(p2, dl, topo, 1.0), b2)
        if it % TURN == 0:
            t2, p2 = turn(t2, b2)
        if t2[0] <= fin + HEAT * (1.0 - it / TRIES) * float(rs.rand()):
            cur, pr, bias = t2, p2, b2
            if t2[0] < best[0]:
                best = t2
    plain = [[x for x in dl[n] if x[0] not in OPS[n]["early"]] for n in range(N)]
    best = min((polish(best, plain, ways, lat, head, rs, FIRST) for it in range(STARTS)), key=lambda x: x[0])
    best = polish(best, plain, ways, lat, head, rs, MOVES)
    for o in OPS:
        o["t"] = best[2][o["n"]]
        o["deps"] -= o["early"]
        if best[5][o["n"]]:
            o["eng"], o["emit"], o["cost"] = o["alt"]
    for b, h in enumerate(best[6]):
        for x in h:
            BANK[[q for q in use if use[q][0] == x[2]][0]] = "D%d" % b
    for m, n in chain(best):
        OPS[n]["deps"].add(m)
        if OPS[m]["eng"] != "P":
            OPS[n]["wait"].add(m)
    order = {e: [x[2] for x in best[1][e]] for e in best[1]}
    pos = {n: i for e in order for i, n in enumerate(order[e])}
    need = set()
    seen = {e: {} for e in order}
    for o in sorted((o for o in OPS if o["eng"] is not None), key=lambda o: (o["t"], pos[o["n"]])):
        sn = seen[o["eng"]]
        o["toks"] = [d for d in o["wait"] if OPS[d]["tok"]]
        o["cw"] = []
        for d in sorted((d for d in o["wait"] if OPS[d]["tok"] is None), key=lambda d: -OPS[d]["t"]):
            de = OPS[d]["eng"]
            if pos[d] > sn.get(de, -1):
                o["cw"].append(d)
                sn[de] = pos[d]
                for x, y in OPS[d]["know"].items():
                    sn[x] = max(sn.get(x, -1), y)
        o["know"] = dict(sn)
        need.update(o["cw"])
    total = {}
    for e in order:
        total[e] = 0
        for i, n in enumerate(order[e]):
            real = [m for m in order[e][:i + 1] if OPS[m]["emit"]][-1] if "close" in OPS[n] else n
            if real != n:
                STOP.add(([m for m in order[e][:i] if any(q[0] == OPS[n]["close"] for q in OPS[m]["w"])][-1], OPS[n]["close"]))
            if n in need:
                total[e] += 1
                OPS[n]["inc"] = total[e]
                OPS[real]["add"] = OPS[real].get("add", 0) + 1
    return order, total, best[0]


ORDER, TOTAL, EST = plan()


def bits(es):
    return sum(1 << x for x in es)


def routes(topo, cores):
    n = len(cores)
    used, ways = set(cores), []

    def take(ok):
        x = [x for x in range(SIM) if x not in used and ok(x)][0]
        used.add(x)
        return x
    turn, spare = {}, {}
    for r in range(n):
        s, d = cores[r], cores[(r - SH) % n]
        if topo.chip(s) == topo.chip(d):
            ways.append({"X": [[s, d]] * NCH, "C": [[s, d]] * NCH})
            continue
        mate = lambda x: topo.mates(topo.chip(x), topo.chip(d)) and topo.may_write(x, d)
        probe = [x for x in range(SIM) if mate(x)][0]
        if topo.may_write(s, probe):
            w2 = [s, take(lambda x: mate(x) and topo.die(x) == topo.die(s)), d]
            ways.append({"X": [w2, w2, w2, [s, d]], "C": [w2] * NCH})
            continue
        here = lambda x: topo.chip(x) == topo.chip(s) and topo.die(x) != topo.die(s)
        o = take(lambda x: here(x) and topo.may_write(x, probe))
        w3 = [s, o, take(lambda x: mate(x) and topo.die(x) == topo.die(o)), d]
        w1 = [s, take(lambda x: here(x) and not topo.may_write(x, probe)), d]
        turn[topo.chip(s)] = 1 - turn.get(topo.chip(s), 0)
        t = turn[topo.chip(s)]
        ways.append({"X": [w3, w1, w1 if t else [s, d], [s, d]], "C": [w3, w1, w3, w1]})
        if not t:
            spare[topo.chip(s)] = (w3[1:-1], w1[1:-1])
    for w in ways:
        s, d = w["C"][0][0], w["C"][0][-1]
        if w["C"][0] == w["C"][1] and topo.chip(s) != topo.chip(d):
            w["C"] = w["C"][:2] + [[s] + x + [d] for x in spare[topo.chip(s)]]
            w["slot"] = {("C", 2): 1, ("C", 3): 0}
    return ways


def step(topo, w, j, far=None):
    es = topo.engines(w[j], w[j + 1])
    if (j + 2 < len(w) or far is not None) and topo.chip(w[j]) == topo.chip(w[j + 1]):
        es = [x for x in es if x not in topo.engines(w[j], w[-1] if far is None else far)]
    return es


def rank_program(g, core, T, topo):
    cores = list(T.cores)
    n = len(cores)
    rank = T.rank_of(core)
    ways = routes(topo, cores)
    far = lambda w: [x for x in cores if topo.chip(x) != topo.chip(w[0])][0] if len(w) == 2 else None

    def hand(what, r, i, j, ls):
        w, k, t = ways[r][what][i], ways[r].get("slot", {}).get((what, i), i), T.X if what == "X" else T.CU
        cs, ks = slice(CW * i, CW * i + CW), slice(CW * k, CW * k + CW)
        src, es, d = t[:, ks if j else cs], step(topo, w, j, far(w) if what == "C" else None), w[j + 1]
        if j + 2 < len(w):
            dst, sem = t[:, ks], T.sem[("hx%d" if what == "X" else "hc%d") % k]
        else:
            dst, sem = (T.X[:, VP + CW * i:VP + CW * i + CW], T.sem.xarr) if what == "X" else (T.CQ[:, cs], T.sem["ca%d" % i])
        g.remote_dma(dst, src, sem, ls, topo.addr(d)[1], topo.addr(d)[0], bits(es))
        return len(es)
    if rank is None:
        out = 0
        for what in "XC":
            for r in range(n):
                for i, w in enumerate(ways[r][what]):
                    if core in w:
                        j = w.index(core)
                        g.wait_ge(T.sem[("hx%d" if what == "X" else "hc%d") % ways[r].get("slot", {}).get((what, i), i)], len(step(topo, w, j - 1)))
                        out += hand(what, r, i, j, T.sem.ls0)
        if out:
            g.wait_ge(T.sem.ls0, out)
        return
    p, q = cores[(rank - SH) % n], cores[(rank + SH) % n]
    off = [x for x in cores if topo.chip(x) != topo.chip(core)][0]
    es = topo.engines(core, off)
    h = len(es) // 2
    sent, out = [0], [0]

    def big(what, i):
        ls, num = (T.sem.ls0, sent) if what == "X" else (T.sem.ls1, out)
        num[0] += hand(what, rank, i, 0, ls)

    def one(dst, src, sem):
        g.remote_dma(dst, src, T.sem[sem], T.sem.ls1, topo.addr(p)[1], topo.addr(p)[0], bits(es))
        out[0] += len(es)

    def two(d1, s1, m1, d2, s2, m2):
        g.remote_dma_fused([RemoteDMATransfer(dst_ids=[DstId(rid=topo.addr(to)[0], pnc=topo.addr(to)[1])], dma_engine_mask=bits(m), remote_sem=T.sem[sem], src=x, dst=y)
                            for to, m, sem, x, y in ((p, es[:h], m1, s1, d1), (q, es[h:], m2, s2, d2))], local_sem=T.sem.ls1)
        out[0] += len(es)
    c = {"big": big, "one": one, "two": two}
    vals = {"xarr": sum(len(step(topo, w, len(w) - 2)) for w in ways[(rank + SH) % n]["X"])}
    for i, w in enumerate(ways[(rank + SH) % n]["C"]):
        vals["ca%d" % i] = len(step(topo, w, len(w) - 2, far(w)))
    for r in range(RO):
        vals["am%d" % r], vals["aa%d" % r], vals["ak%d" % r] = len(es), h, len(es) - h
    qs = {"V": g.vector, "S": g.scalar, "P": g.tensor, "G": g, "Y": g.sync}
    for e in "GYSPV":
        got = set()
        vals["ls0"] = sent[0]
        for k in ORDER[e]:
            o = OPS[k]
            for d in o["toks"]:
                s, v = OPS[d]["tok"]
                if s not in got:
                    got.add(s)
                    qs[e].wait_ge(T.sem[s], vals[s] if v is None else v)
            for d in o["cw"]:
                qs[e].wait_ge(T.sem["s" + OPS[d]["eng"]], OPS[d]["inc"])
            r = o["emit"](g, T, c) if o["emit"] else None
            if "add" in o:
                r.then_inc(T.sem["s" + e], o["add"])
    for e in "VSPG":
        if TOTAL[e]:
            g.wait_ge(T.sem["s" + e], TOTAL[e])
    g.wait_ge(T.sem.ls1, out[0])
    for s in ("ox", "ow", "on"):
        g.wait_ge(T.sem[s], 16)
